import numpy as np, ml_dtypes
CORES = [23,119,17,113]
N = 4
BF = ml_dtypes.bfloat16
NL, W, B, RO, Q = 112, 3584, 224, 8, 2
def parts(rng):
    X = rng.integers(0, 256, (N, 8, 16, W)); L = rng.integers(0, W, (N, 8, 16, W))
    y = (rng.integers(0, 256, (N, 8, 16, B)) * rng.integers(1, 9, (N, 8, 1, B))) >> 3
    return X, L, y, rng.integers(0, NL, (N, 8, B)), rng.integers(0, 4096, (N, 8, B))
def pack(X, L, y, ln, T):
    return {"xw": np.ascontiguousarray(X.reshape(N, 128, W)).astype(np.float32).astype(BF), "il": np.ascontiguousarray(L.reshape(N, 128, W)).astype(np.int32),
            "y0": np.ascontiguousarray(y.reshape(N, 128, B)).astype(np.float32).astype(BF), "ln0": np.ascontiguousarray(ln).astype(np.int32), "tk0": np.ascontiguousarray(T).astype(np.int32)}
def setup_inputs(rng):
    return pack(*parts(rng))
def setup_inputs_spread(rng):
    X = rng.integers(0, 256, (N, 8, 16, W)) >> rng.integers(0, 9, (N, 8, 1, W)); y = rng.integers(0, 256, (N, 8, 16, B)) >> rng.integers(0, 9, (N, 8, 1, B))
    a = np.exp2(rng.integers(-2, 3, (N, 8, 16, 1))); b = np.exp2(rng.integers(-2, 3, (N, 8, 16, 1)))
    line = np.minimum((NL * rng.random((N, 8, 16, W)) ** a).astype(np.int64), NL - 1); wait = np.minimum((32 * rng.random((N, 8, 16, W)) ** b).astype(np.int64), 31)
    ln = np.minimum((NL * rng.random((N, 8, B)) ** 3).astype(np.int64), NL - 1); T = np.minimum(np.exp2(12 * rng.random((N, 8, B))).astype(np.int64) - 1, 4095)
    return pack(X, 32 * line + wait, y, ln, T)
def ends(rng, top, *shape):
    k = rng.integers(0, 4, shape[:-2] + (1, shape[-1]))
    return top * np.where(k < 2, k, rng.integers(0, 2, shape))
def setup_inputs_ends(rng):
    X = ends(rng, 255, N, 8, 16, W); y = ends(rng, 255, N, 8, 16, B)
    L = np.where(rng.random((N, 8, 16, W)) < 0.8, ends(rng, W - 1, N, 8, 16, W), rng.integers(0, W, (N, 8, 16, W)))
    ln = (NL - 1) * rng.integers(0, 2, (N, 8, B)); T = 4095 * rng.integers(0, 2, (N, 8, B))
    L[..., 0] = 0; L[:, :, 1, 0] = W - 1; L[..., 31] = (W - 1) * rng.integers(0, 2, (N, 8, 16))
    L[..., W - 32] = W - 1; L[:, :, 0, W - 32] = 0; L[..., W - 1] = W - 1; L[:, :, 0, W - 1] = 0
    X[..., 0] = 0; X[..., W - 1] = 0; X[..., W - 2] = 255
    for q in range(N):
        if q == 1:
            for c in (0, 31, W - 2, W - 1): X[q, :, :, c] = 255
            y[q] = np.where(np.argsort(rng.random((8, 16, B)), axis=1) < rng.integers(0, 9, (8, 1, B)), 0, 255)
        else:
            if q == N - 1: y[q] = 0
            for i, l, t, v in ((0, NL - 1, 4095, 0), (B - 1, NL - 1, 4095, 0), (B - 2, NL - 1, 4095, 255), (1, NL - 1, 0, 255), (B - 4, NL - 1, 0, 255), (3, 0, 0, 0), (B - 3, 0, 0, 0)):
                ln[q, :, i] = l; T[q, :, i] = t; y[q, :, :, i] = v
            if q == N - 1: y[q, :7, :, B - 2] = 0
            if q == 2: y[q] = np.where(np.argsort(rng.random((8, 16, B)), axis=1) < rng.integers(9, 17, (8, 1, B)), 0, 255)
    return pack(X, L, y, ln, T)
def setup_inputs_corners(rng):
    X, L, y, ln, T = parts(rng)
    T = np.where(rng.random(T.shape) < 0.7, rng.choice(np.array([0, 15, 16, 31, 32, 4064, 4080, 4095]), T.shape), T)
    ln = np.where(rng.random(ln.shape) < 0.4, rng.choice(np.array([0, NL - 1]), ln.shape), ln)
    for q in range(N):
        for g in range(8):
            e = (q + g) % 8
            if e == 0: ln[q, g] = ln[q, g, 0]; T[q, g] = T[q, g, B - 1]
            elif e == 1: L[q, g] = np.arange(W)
            elif e == 2: L[q, g] = 0
            elif e == 3: L[q, g] = W - 1
            elif e == 4: X[q, g] = np.maximum(X[q, g], 1); y[q, g] = np.where(np.argsort(rng.random((16, B)), axis=0) < rng.integers(8, 10, (1, B)), 0, 255)
            elif e == 5: X[q, g] = 0
            elif e == 6: X[q, g] = 255; y[q, g] = rng.integers(128, 256, (16, B))
            else:
                a = rng.permutation(W)[:B]; ln[q, g] = a >> 5; T[q, g] = (a & 31) + 32 * rng.integers(0, 128, B); h = B // 4
                pl = np.concatenate([np.array([0, W - 1]), 1 + rng.permutation(W - 2)])
                d = rng.permutation(np.concatenate([pl[:h], pl[:h], pl[h:B - h]]))
                L[q, g, 15, a] = (d & 4064) + ((d - T[q, g]) & 31)
    return pack(X, L, y, ln, T)
def setup_inputs_crowd(rng):
    X, L, y, ln, T = parts(rng)
    few = rng.integers(0, NL, (N, 8, 1, 4)); few[:, ::2, :, 0] = NL - 1; few[:, 1::2, :, 1] = 0
    L[:, :, 0:2] = (L[:, :, 0:2] & 31) + 32 * np.take_along_axis(few, rng.integers(0, 4, (N, 8, 1, 2 * W)), 3).reshape(N, 8, 2, W)
    L[:, :, 15:16] = (L[:, :, 15:16] & 31) + 32 * np.take_along_axis(few, rng.integers(0, 2, (N, 8, 1, W)), 3)
    ln = np.take_along_axis(few, rng.integers(0, 4, (N, 8, 1, B)), 3).reshape(N, 8, B)
    p = int(rng.integers(0, N)); q = (p + 1) % N
    X[p] = 0; y[p] = 255 - (rng.integers(0, 128, (8, 16, B)) >> (3 * rng.integers(0, 2, (8, 1, B))))
    X[q] = np.maximum(X[q], 1); y[q] = rng.integers(128, 256, (8, 16, B))
    y[q, int(rng.integers(0, 8)), :, rng.permutation(B)[:int(rng.integers(1, 32))]] = 0
    return pack(X, L, y, ln, T)
def check_inputs(d):
    bad = []
    for k, hi in (("xw", 255), ("il", W - 1), ("y0", 255), ("ln0", NL - 1), ("tk0", 4095)):
        v = np.asarray(d[k]).astype(np.float64)
        if not np.all((v >= 0) & (v <= hi)): bad.append("range of " + k)
        elif not np.all(v == np.floor(v)): bad.append("whole numbers of " + k)
    return bad
def reference(xw, il, y0, ln0, tk0):
    X = xw.astype(np.float32).astype(np.int64).reshape(N, 8, 16, W); L = il.astype(np.int64).reshape(N, 8, 16, W)
    y = y0.astype(np.float32).astype(np.int64).reshape(N, 8, 16, B); ln = ln0.astype(np.int64); T = tk0.astype(np.int64)
    A = np.zeros(N, np.int64)
    for step in range(RO):
        a = 32 * ln + (T & 31)
        c = np.take_along_axis(L, a[:, :, None, :], 3)
        s = (c & 4064) + ((c + T[:, :, None, :]) & 31)
        v = np.take_along_axis(X, np.ascontiguousarray(s.transpose(0, 1, 3, 2)).reshape(N, 8, 1, 16 * B), 3).reshape(N, 8, 16, B, 16 // Q, Q)
        m = np.max(np.min(v, axis=-1), axis=-1)
        z = np.abs(m - y)
        skip = np.add.reduce((z >= y).astype(np.int64), axis=2) >= 9
        ln = np.where(skip, c[:, :, 1], c[:, :, 0]) >> 5
        d = s[:, :, 15]
        T = (T + 1 + (np.add.reduce(z, axis=2) & 31) + (A & 31)[:, None, None]) & 4095
        A = np.add.reduce(skip.reshape(N, 8 * B).astype(np.int64), axis=1)
        y = np.roll(z, 1, axis=0); ln = np.roll(ln, 1, axis=0); T = np.roll(T, 1, axis=0); d = np.roll(d, 1, axis=0)
        for q in range(N):
            for g in range(8):
                p, first = np.unique(d[q, g], return_index=True)
                u = L[q, g]; o = u[:, p]
                u[:, p] = (o & 4064) + ((o + y[q, g][:, first]) & 31)
        if step < RO - 1:
            np.put_along_axis(X, (16 * np.arange(B) + (T & 15))[:, :, None, :], y, 3)
    return {"yw": (L & 31).reshape(N, 128, W).astype(np.float32).astype(BF), "yy": y.reshape(N, 128, B).astype(np.float32).astype(BF), "yl": ln.astype(np.float32), "yt": T.astype(np.float32)}

@@ -1,0 +1,536 @@
+from concourse.mybir import AluOpType as A, AxisListType, ActivationFunctionType as AF
+
+NP, NB, NR, ST = 3584, 224, 4, 8
+RB = 3
+LATE = 4
+CUT = 96
+CH = [(0, 12), (12, 28), (28, 48), (48, 72), (72, 92), (92, 112)]
+
+
+def _sb(dtype, **widths):
+    return {n: ("sbuf", [128, w], dtype) for n, w in widths.items()}
+
+
+SCRATCH = {
+    **_sb("int32", ilb=NP, TLi=2 * NB, TLj=2 * NB, iw=14, ip=14, ipq=14, SI=28, SJ=28, q=14, c2=28, b2=28, ao=28,
+          t1=14, t2=14, t3=14, Tn=14, B1=14),
+    **_sb("float16", f16t=NP, PM32=512, EF=8 * 240, EL=8 * 240, KQ=NB, fo=28),
+    **_sb("uint16", EO=8 * 240, DR=NB, DWu=16, OFF=16, AO=28),
+    **_sb("float32", h64=64, h32=32, rm=16, rq=16, wq1=1, th16=16, DG=NB, thA=NB, thB=NB, thr=NB, trm=NB, SC=NB, DW=14,
+          o2=14, sd=28, sa=28, lin=28, Ar=1, Au=1, A1=1, fr=2 * NB),
+    **_sb("bfloat16", XT=NP, LT=NP, WT=NP + NB, YW=NP, KF=NP, TLb=3 * NB, ONE=128, ZER=128, BO0=128, BO=128, BOE=256,
+          ID=128, NID=128, NID32=128, P4=512, P32=512, SEL=2048, BC=2048, SKA=1024, SKD=1024, WQ=128, BIG=128,
+          MASK=1792, ZS=9 * 448, ZO=8 * NB, YE=8 * 448, LF=NB, KA=1, DO=NB, KD=NB, DRED=NB, sel=14, bw=14,
+          BR=NB, WA=NB, LG=NB, VE=1792, U=1792, M=1792),
+    "EQ": ("sbuf", [128, 14, 240], "bfloat16"),
+    **{n: ("psum", [128, 512], "float32") for n in ("pXR", "pE", "pO", "pZ", "pW", "pS", "pD", "pC")},
+}
+SEMAPHORES = (["cv", "ct", "cs", "cp", "loc", "d_tk", "d_ln", "d_y", "d_x0", "d_x1", "d_t", "d_l"]
+              + ["d_il%d" % i for i in range(7)] + ["d_o%d" % i for i in range(8)]
+              + ["a%s%d" % (k, n) for k in "zbye" for n in range(ST)])
+
+
+def rank_program(g, core, T, topo):
+    rank = T.rank_of(core)
+    if rank is None:
+        return
+    queues = {"v": g.vector, "t": g.tensor, "s": g.scalar, "p": g, "y": g.sync}
+    semof = {"v": "cv", "t": "ct", "s": "cs", "p": "cp"}
+    count = {s: 0 for s in SEMAPHORES}
+    known = {e: {} for e in queues}
+    snaps = {}
+    hist = {}
+
+    def conflicts(e, name, lo, hi, write):
+        bank = name[0] == "p" and name[1:2].isupper()
+        out = []
+        for (a, b, e2, s2, v2, w2, asy) in hist.get(name, []):
+            if bank:
+                if e2 == e:
+                    if e == "t" or not (write or w2) or b <= lo or hi <= a:
+                        continue
+                out.append((s2, v2))
+                continue
+            if b <= lo or hi <= a or not (write or w2):
+                continue
+            if e2 == e and not asy and not w2:
+                continue
+            out.append((s2, v2))
+        return out
+
+    def waits(e, acc):
+        need = {}
+        for (name, lo, hi, w) in acc:
+            for s, v in conflicts(e, name, lo, hi, w):
+                need[s] = max(need.get(s, 0), v)
+        own = semof.get(e)
+        for s in sorted(need, key=lambda s: (s == own, s)):
+            v = need[s]
+            if known[e].get(s, 0) >= v:
+                continue
+            queues[e].wait_ge(T.sem[s], v)
+            for s2, v2 in snaps[(s, v)].items():
+                known[e][s2] = max(known[e].get(s2, 0), v2)
+
+    def note(e, acc, s, v, asy):
+        sn = dict(known[e]) if e in known else {}
+        sn[s] = v
+        snaps[(s, v)] = sn
+        for (name, lo, hi, w) in acc:
+            h = hist.setdefault(name, [])
+            if w:
+                h[:] = [x for x in h if not (lo <= x[0] and x[1] <= hi)]
+            else:
+                h[:] = [x for x in h if not (x[2] == e and not x[5] and not asy and lo <= x[0] and x[1] <= hi)]
+            h.append((lo, hi, e, s, v, w, asy))
+
+    def access(rd, wr):
+        return [(n, lo, hi, False) for (n, lo, hi) in rd] + [(n, lo, hi, True) for (n, lo, hi) in wr]
+
+    def op(e, rd, wr, fn):
+        acc = access(rd, wr)
+        waits(e, acc)
+        s = semof[e]
+        count[s] += 1
+        fn(queues[e]).then_inc(T.sem[s], 1)
+        note(e, acc, s, count[s], False)
+
+    def dma(e, rd, wr, out, in_, s):
+        acc = access(rd, wr)
+        waits(e, acc)
+        count[s] += 16
+        queues[e].dma_start(out, in_).then_inc(T.sem[s], 16)
+        note(e, acc, s, count[s], True)
+
+    def ap(o):
+        if o[0] == "EQ":
+            c, a = divmod(o[1], 240)
+            return T.EQ[:, c, a:a + o[2] - o[1]] if len(o) == 3 else T.EQ[:, c:o[2] // 240, 0:16]
+        if len(o) == 1:
+            return T[o[0]][:]
+        if len(o) == 4:
+            return T[o[0]][:, o[1]:o[2]:o[3]]
+        return T[o[0]][:, o[1]:o[2]]
+
+    def rg(o):
+        if o[0] == "sa":
+            return ("sa%d" % (o[1] % 2), 0, 28)
+        return (o[0], 0, SCRATCH[o[0]][1][1]) if len(o) == 1 else (o[0], o[1], o[2])
+
+    def vts(out, i, s1, o0, s2=None, o1=None):
+        rd = [rg(i)]
+        if isinstance(s1, tuple):
+            rd.append(rg(s1))
+            s1 = ap(s1)
+        if isinstance(s2, tuple):
+            rd.append(rg(s2))
+            s2 = ap(s2)
+        if o1 is None:
+            op("v", rd, [rg(out)], lambda q: q.tensor_scalar(ap(out), ap(i), s1, None, o0))
+        else:
+            op("v", rd, [rg(out)], lambda q: q.tensor_scalar(ap(out), ap(i), s1, s2, o0, o1))
+
+    def vtt(out, a, b, o):
+        op("v", [rg(a), rg(b)], [rg(out)], lambda q: q.tensor_tensor(ap(out), ap(a), ap(b), o))
+
+    def vcp(out, i):
+        op("v", [rg(i)], [rg(out)], lambda q: q.tensor_copy(ap(out), ap(i)))
+
+    def fill(out, c):
+        op("v", [], [rg(out)], lambda q: q.memset(ap(out), c))
+
+    def act(out, i, f, **kw):
+        op("s", [rg(i)] + ([("rm", 0, 16)] if "scale" in kw else []), [rg(out)], lambda q: q.activation(ap(out), ap(i), f, **kw))
+
+    def gat(out, win, off):
+        op("s", [rg(win), rg(off)], [rg(out)], lambda q: q.activation(ap(out), ap(win).indirect(ap(off)), AF.Copy))
+
+    def mm(out, l, r, start, stop):
+        op("t", [rg(l), rg(r)], [rg(out)], lambda q: q.matmul(ap(out), ap(l), ap(r), start, stop))
+
+    def mat(n, r):
+        return (n, 128 * r, 128 * r + 128)
+
+    nxt = T.cores[(rank + 1) % NR]
+    prv = T.cores[(rank - 1) % NR]
+    rid, pid = topo.addr(nxt)[:2]
+    emask = topo.mask(core, nxt)
+    n_out = len(topo.engines(core, nxt))
+    n_in = len(topo.engines(prv, core))
+
+    def send(dst, src, s):
+        waits("p", [rg(src) + (False,)])
+        g.remote_dma(out_ap=ap(dst), in_ap=ap(src), remote_sem=T.sem[s], local_sem=T.sem["loc"], pid=pid,
+                     routing_id=rid, dma_engine_mask=emask)
+        count["loc"] += n_out
+
+    def lands(dst, s):
+        count[s] = n_in
+        note("r", [rg(dst) + (True,)], s, n_in, True)
+
+    def zin(n):
+        return ("ZS", 448 * n, 448 * n + 224)
+
+    def ye(n):
+        return ("YE", 448 * n, 448 * n + 224)
+
+    def zparts(b, lo, hi):
+        return (b, lo, lo + 2 * CH[LATE][0]), (b, lo + 2 * CH[LATE][0], hi)
+
+    def row(n):
+        return ("ZS", 448 * n + 224, 448 * n + 448)
+
+    def lst(n, b, lo, hi):
+        return (b, 240 * n + lo, 240 * n + hi)
+
+    for n in range(ST):
+        lands(("YE", 448 * n, 448 * n + 448), "ay%d" % n)
+        lands(lst(n, "EL", 0, 238), "ae%d" % n)
+        for z, s in zip(zparts(*zin(n + 1)), "zb"):
+            lands(z, "a%s%d" % (s, n))
+
+    fill(("TLi",), 0)
+    fill(("ONE",), 1.0)
+    for i in range(7):
+        b = ("ilb", 512 * i, 512 * i + 512)
+        dma("y", [], [rg(b)], ap(b), T.il[:, 512 * i:512 * i + 512], "d_il%d" % i)
+    dma("s", [], [("TLi", 0, 224)], T.TLi[0:128:16, 0:224], T.tk0[:], "d_tk")
+    dma("s", [], [("TLi", 224, 448)], T.TLi[0:128:16, 224:448], T.ln0[:], "d_ln")
+    dma("s", [], [rg(zin(0))], ap(zin(0)), T.y0[:], "d_y")
+    for i in range(2):
+        b = ("XT", 1792 * i, 1792 * i + 1792)
+        dma("y", [], [rg(b)], ap(b), T.xw[:, 1792 * i:1792 * i + 1792], "d_x%d" % i)
+
+    def asel(out, i, pat, cmp, base, cm, other=0.0):
+        op("p", [rg(i)], [rg(out)], lambda q: q.affine_select(ap(out), ap(i), pat, cmp, other, base, cm))
+    asel(("BO0",), ("ONE",), [[-16, 8], [0, 16]], A.is_ge, 0, 1)
+    asel(("ID",), ("ONE",), [[-1, 128]], A.is_equal, 0, 1)
+    asel(("BO",), ("BO0",), [[16, 8], [0, 16]], A.is_ge, 15, -1)
+    fill(("SEL",), 0.0)
+    asel(("SKD",), ("SEL", 0, 1024), [[0, 1024]], A.is_ge, -1, 0)
+    asel(mat("BOE", 0), ("BO",), [[0, 8], [-1, 16]], A.is_ge, 7, 0)
+    asel(mat("BOE", 1), ("BO",), [[0, 8], [1, 16]], A.is_ge, -8, 0)
+    for k, (h, base) in enumerate(((0, 0), (1, 16), (0, -1), (1, 15))):
+        asel(mat("P4", k), mat("BOE", h), [[-16, 8], [-2, 16]], A.is_equal, base, 1)
+    op("p", [], [("iw", 0, 14)], lambda q: q.iota(T.iw[:], [[16, 14]], 0, 1))
+    op("p", [], [("ip", 0, 14)], lambda q: q.iota(T.ip[:], [[0, 14]], 0, 1))
+    for r in range(16):
+        fill(("th16", r, r + 1), 2.0 * 4.0 ** (15 - r))
+    vts(("NID32",), ("ID",), -32.0, A.mult)
+    asel(("SKA",), ("SKD",), [[0, 1024]], A.is_ge, -1, 0)
+    asel(("ZER",), ("ID",), [[0, 128]], A.is_ge, -1, 0)
+    for k in range(2):
+        asel(("MASK", 896 * k, 896 * k + 896), ("SKA", 0, 896), [[0, 112], [1, 8]], A.is_equal, 0, 0, 256.0)
+
+    def halves(i):
+        lo, hi = 512 * i, 512 * i + 512
+        vts(("f16t", lo, hi), ("ilb", lo, hi), -1792.0, A.add)
+
+    def table(i):
+        lo, hi = 512 * i, 512 * i + 512
+        vts(("LT", lo, hi), ("f16t", lo, hi), 1.0 / 32, A.mult, 184.515625, A.add)
+        pb = ("pXR", "pE", "pO", "pZ")[i % 4]
+        mm((pb,), ("ID",), ("f16t", lo, hi), True, False)
+        mm((pb,), ("NID32",), ("LT", lo, hi), False, True)
+        act(("WT", lo, hi), (pb,), AF.Copy, bias=5920.0)
+
+    def clocks():
+        vts(("TLj", 0, 224), ("TLi", 0, 224), 4064, A.bitwise_and)
+        vts(("TLj", 224, 448), ("TLi", 0, 224), 31, A.bitwise_and)
+        vcp(("TLb", 0, 448), ("TLj",))
+        vcp(("TLb", 448, 672), ("TLi", 224, 448))
+        for r in range(16):
+            mm(("pW", 0, 42), mat("SEL", r), ("TLb", r, 672, 16), r == 0, r == 15)
+
+    def places():
+        vcp(("c2", 0, 14), ("pW", 14, 28))
+        vcp(("bw",), ("pW", 14, 28))
+        vts(("b2", 0, 14), ("pW", 28, 42), 32.0, A.mult)
+        vcp(("t1",), ("pW", 0, 14))
+        vtt(("ao", 0, 14), ("c2", 0, 14), ("b2", 0, 14), A.add)
+        vcp(("AO", 0, 14), ("ao", 0, 14))
+        vtt(("Tn",), ("t1",), ("c2", 0, 14), A.add)
+
+    def broadcast(dst, src, lo):
+        for r in range(16):
+            mm((dst, r + lo, lo + 224, 16), mat("BC", r), src, True, True)
+
+    def pick(m, k):
+        for h in range(2):
+            for t in range(8):
+                act((m, 128 * t + 2 * t + h, 128 * t + 128, 16), ("ID", k + 8 * h, 128, 16), AF.Copy)
+
+    def weights():
+        op("p", [], [("trm", 0, 224)], lambda q: q.iota(T.trm[:], [[1, 224]], NP, 0, allow_small_or_imprecise_dtypes=True))
+        vtt(("rq",), ("rm",), ("th16",), A.mult)
+        vcp(("DG", 0, 16), ("rm",))
+        vts(("ipq",), ("ip",), 112, A.bitwise_and)
+        vts(("BIG",), ("BO",), 2.0 ** 32, A.mult)
+        op("v", [("rq", 0, 16)], [("wq1", 0, 1)], lambda q: q.tensor_reduce(T.wq1[:], T.rq[:], AxisListType.X, A.add))
+        vcp(("DG", 16, 32), ("DG", 0, 16))
+        vtt(("iw",), ("iw",), ("ipq",), A.subtract)
+        fill(("sd",), 0.0)
+        fill(("Ar",), 0.0)
+        vcp(("DG", 32, 64), ("DG", 0, 32))
+        vts(("WQ",), ("BO",), ("wq1", 0, 1), A.mult, 0.5, A.mult)
+        vts(("b2", 14, 28), ("iw",), 16.0, A.mult)
+        vcp(("DG", 64, 128), ("DG", 0, 64))
+        vts(("NID",), ("ID",), -1.0, A.mult)
+        vcp(("DG", 128, 224), ("DG", 0, 96))
+        vts(("thA",), ("DG",), ("wq1", 0, 1), A.mult)
+        vts(("thB",), ("DG",), 1.0, A.subtract)
+
+    for r in range(16):
+        act(("SEL", 128 * r + r, 128 * r + 128, 16), ("BO", r, 128, 16), AF.Copy)
+    halves(0)
+    vtt(("h64",), ("ID", 0, 64), ("ID", 64, 128), A.add)
+    halves(1)
+    vtt(("h32",), ("h64", 0, 32), ("h64", 32, 64), A.add)
+    table(0)
+    vtt(("rm",), ("h32", 0, 16), ("h32", 16, 32), A.add)
+    halves(2)
+    for r in range(16):
+        act(mat("BC", r), ("BO",), AF.Copy, scale=T.rm[:, r:r + 1])
+    table(1)
+    halves(3)
+    table(2)
+    halves(4)
+    table(3)
+    halves(5)
+    table(4)
+    clocks()
+    halves(6)
+    table(5)
+    pick("SKD", 7)
+    table(6)
+    places()
+    broadcast("pS", ("bw",), 256)
+    act(row(0), ("pS", 256, 480), AF.Copy)
+    vts(("PM32",), ("P4",), -32.0, A.mult)
+    vts(("P32",), ("P4",), 32.0, A.mult)
+    weights()
+
+    def reduced(i, k):
+        lo, hi = 512 * i, 512 * i + 512
+        if k == 0:
+            vts(("KF", lo, hi), ("WT", lo, hi), 1.0 / 32, A.mult, 191.515625, A.add)
+        elif k == 1:
+            pb = ("pE", "pO", "pZ")[i % 3]
+            mm((pb,), ("ID",), ("WT", lo, hi), True, False)
+            mm((pb,), ("NID32",), ("KF", lo, hi), False, True)
+            act(("YW", lo, hi), (pb,), AF.Copy, bias=6144.0)
+        elif k == 2:
+            vts(("f16t", lo, hi), ("KF", lo, hi), -32.0, A.mult, 6144.0, A.add)
+        else:
+            vtt(("YW", lo, hi), ("WT", lo, hi), ("f16t", lo, hi), A.add)
+        if k % 2:
+            dma("y", [("YW", lo, hi)], [], T.yw[:, lo:hi], T.YW[:, lo:hi], "d_o%d" % (1 + i))
+
+    def more(n, i):
+        if n == ST:
+            reduced(i, 0)
+            reduced(i, 1)
+
+    def arrive(n):
+        z = zin(n)
+        vtt(("ZS", 448 * n + 224, 448 * n + 448), z, ("pD", 256, 480), A.is_ge)
+        for r in range(16):
+            mm(("pW", 0, 28), mat("SEL", r), ("ZS", 448 * n + r, 448 * n + 448, 16), r == 0, r == 15)
+        vtt(("o2",), ("SC", 15, 224, 16), ("DW",), A.max)
+        vts(("SI",), ("pS", 0, 28), 1792.0, A.add)
+        vcp(("OFF", 0, 14), ("o2",))
+        vts(("SJ",), ("SI",), 4064, A.bitwise_and)
+        op("v", [rg(z), ("DRED", 0, 224), ("OFF", 0, 14)], [("WT", 0, NP + NB)],
+           lambda q: q.tensor_tensor(T.WT[:, 0:NP + NB].indirect(T.OFF[:, 0:14]), T.DRED[:], ap(z), A.add))
+        more(n, 0)
+        more(n, 1)
+        vtt(("sd", 1, 28, 2), ("SJ", 14, 28), ("SJ", 0, 14), A.subtract)
+        vcp(("sa", 1, 28, 2), ("SJ", 0, 14))
+        vts(("sa", 0, 28, 2), ("pW", 14, 28), 9.0, A.is_ge)
+        if n < ST:
+            vtt(("q",), ("pW", 0, 14), ("B1",), A.add)
+        vcp(("t1",), ("pW", 0, 14))
+        more(n, 2)
+        op("v", [("sd", 0, 28), ("sa0", 0, 28), ("sa1", 0, 28)], [("lin", 0, 28)],
+           lambda q: q.tensor_tensor_scan(T.lin[:], T.sd[:], T.sa[:], 0.0, A.mult, A.add))
+        if n < ST:
+            vts(("c2", 0, 14), ("q",), 31, A.bitwise_and)
+            vts(("c2", 14, 28), ("q",), 15, A.bitwise_and)
+        vts(("t2",), ("t1",), 31, A.bitwise_and)
+        if n < ST:
+            vtt(("ao", 0, 14), ("c2", 0, 14), ("lin", 1, 28, 2), A.add)
+            vtt(("ao", 14, 28), ("c2", 14, 28), ("b2", 14, 28), A.add)
+        more(n, 3)
+        vtt(("t3",), ("t2",), ("B1",), A.add)
+        if n < ST:
+            vcp(("AO", 0, 14), ("ao", 0, 14))
+            vcp(("AO", 14, 28), ("ao", 14, 28))
+            vcp(("bw",), ("c2", 0, 14))
+            vcp(("sel",), ("sa", 0, 28, 2))
+        more(n, 4)
+        vts(("Tn",), ("t3",), 4095, A.bitwise_and)
+        if n < ST:
+            op("v", [rg(z), ("AO", 14, 28)], [("XT", 0, NP)],
+               lambda q: q.tensor_copy(T.XT[:, 0:NP].indirect(T.AO[:, 14:28]), ap(z)))
+
+    def fetch(n):
+        parts = ((0, CUT, "pXR", ("pE", "pO")), (CUT, NB, "pC", ("pD", "pS")))
+        br = ("BR", 0) if n else row(0)[:2]
+
+        def x(o, lo, hi, h=None):
+            return (o[0], o[1] + lo, o[1] + hi) if h is None else (o[0], o[1] + lo + h, o[1] + hi, 2)
+
+        def lists(part, src, k):
+            lo, hi, _, banks = parts[part]
+            for h in range(2):
+                mm((banks[k // 2], lo // 2, hi // 2), mat({"WA": "P4", "LG": "P32", "KQ": "PM32"}[src], k + h),
+                   x((src, 0), lo, hi, h), False, src == "KQ" and h == 1)
+
+        def floors(part):
+            lo, hi, b, _ = parts[part]
+            mm((b, lo, hi), ("ID",), ("WA", lo, hi), False, True)
+            vts(("KQ", lo, hi), (b, lo, hi), 1.0 / 32, A.mult, 1535.515625, A.add)
+
+        for lo, hi, b, banks in parts:
+            gat(("WA", lo, hi), ("WT", 0, NP), ("AO", lo // 16, hi // 16))
+            gat(("LG", lo, hi), ("LT", 0, NP), ("AO", lo // 16, hi // 16))
+            mm((b, lo, hi), ("ID",), x(br, lo, hi), True, False)
+            if n:
+                mm((b, lo, hi), ("BO",), x(zin(n), lo, hi), False, False)
+        for lo, hi, b, banks in parts:
+            for k in (0, 2):
+                for h in range(2):
+                    mm((banks[k // 2], lo // 2, hi // 2), mat("P4", k + h), x(br, lo, hi, h), h == 0, False)
+                for h in range(2 if n else 0):
+                    mm((banks[k // 2], lo // 2, hi // 2), mat("BOE", h), x(zin(n), lo, hi, h), False, False)
+        floors(0)
+        vts(lst(n, "EF", 224, 238), ("Tn",), -2048.0, A.add)
+        lists(0, "WA", 0)
+        lists(0, "LG", 0)
+        lists(0, "WA", 2)
+        floors(1)
+        for src, k in (("KQ", 0), ("LG", 2), ("KQ", 2)):
+            lists(0, src, k)
+        for src, k in (("WA", 0), ("LG", 0), ("KQ", 0), ("WA", 2), ("LG", 2), ("KQ", 2)):
+            lists(1, src, k)
+        for lo, hi, _, banks in parts:
+            for b, o in ((banks[0], 0), (banks[1], 112)):
+                vts(lst(n, "EO", o + lo // 2, o + hi // 2), (b, lo // 2, hi // 2), 45024.0, A.add)
+                vts(lst(n, "EF", o + lo // 2, o + hi // 2), (b, lo // 2, hi // 2), 43232.0, A.add)
+
+    def big(n):
+        for (a, b) in CH:
+            gat(("VE", 16 * a, 16 * b), ("XT", 0, NP), lst(n, "EO", a, b))
+            if n and b == CH[RB][1]:
+                broadcast("pS", ("bw",), 256)
+                act(row(n), ("pS", 256, 480), AF.Copy)
+        last = 2 * CH[LATE][0]
+        early, late = zparts(*zin(n))
+        mm(("pZ", 0, last), ("NID",), early, True, False)
+        mm(("pC", 256 + last, 480), ("NID",), late, True, False)
+
+        def least(a, b):
+            off = lst(n, "EO", 112 + a, 112 + b)
+            op("v", [("XT", 0, NP), rg(off), ("VE", 16 * a, 16 * b)], [("U", 16 * a, 16 * b)],
+               lambda q: q.tensor_tensor(T.U[:, 16 * a:16 * b], T.XT[:, 0:NP].indirect(ap(off)), T.VE[:, 16 * a:16 * b], A.min))
+
+        def greatest(a, b):
+            r = slice(16 * a, 16 * b)
+            op("v", [("MASK", 16 * a, 16 * b), ("U", 16 * a, 16 * b)], [("M", 16 * a, 16 * b)],
+               lambda q: q.tensor_tensor_scan(T.M[:, r], T.MASK[:, r], T.U[:, r], 0.0, A.min, A.max))
+            o = ("pZ", 2 * a, 2 * b) if 2 * b <= last else ("pC", 256 + 2 * a, 256 + 2 * b)
+            mm(o, ("ID",), ("M", 16 * a + 7, 16 * b, 8), False, 2 * b in (last, 224))
+        for i, c in enumerate(CH):
+            least(*c)
+            if i:
+                greatest(*CH[i - 1])
+        if n:
+            op("v", [("pW", 32, 46)], [("Ar", 0, 1)], lambda q: q.tensor_reduce(T.Ar[:], T.pW[:, 32:46], AxisListType.X, A.add))
+        greatest(*CH[-1])
+        out = zparts("ZO", 224 * n, 224 * n + 224)
+        act(out[0], ("pZ", 0, last), AF.Abs)
+        act(out[1], ("pC", 256 + last, 480), AF.Abs)
+        send(("YE", 448 * n, 448 * n + 448), ("ZS", 448 * n, 448 * n + 448), "ay%d" % n)
+        for d, o, s in zip(zparts(*zin(n + 1)), out, "zb"):
+            send(d, o, "a%s%d" % (s, n))
+
+    def ready(n):
+        el = 240 * n
+        for k in (7, 15):
+            mm(("pD", k // 8, 224, 2), mat("BC", k), ("EL", el + 112, el + 224), True, True)
+        for t in range(8):
+            mm(("pS", 32, 46), mat("SKD", t), ("EL", el + 112 + t, el + 224, 8), t == 0, t == 7)
+        if n == 0:
+            pick("SKA", 0)
+            vtt(("trm",), ("trm",), ("DG",), A.mult)
+            vtt(("thr",), ("thA",), ("thB",), A.add)
+        vts(("KA",), ("Ar",), 1.0 / 32, A.mult, 191.515625, A.add)
+        vts(("Au",), ("KA",), -32.0, A.mult, 6145.0, A.add)
+        vts(("DR",), ("pD", 0, 224), 1792.0, A.add)
+        vts(("DW",), ("pS", 32, 46), 1792.0, A.add)
+        vts(("A1",), ("Au",), ("Ar", 0, 1), A.add)
+        vcp(("DWu", 0, 14), ("DW",))
+        gat(("DO",), ("WT", 0, NP), ("DWu", 0, 14))
+        half = (("pC", 0, 112), ("pE", 112, 224))
+        for b, lo, hi in half:
+            mm((b, lo, hi), ("ZER",), ("MASK", lo, hi), True, False)
+
+        def strips(h):
+            mm(half[h], ("WQ",), ("EQ", 7 * 240 * h, 7 * 240 * (h + 1), 1), False, True)
+
+        def losers(h):
+            b, lo, hi = half[h]
+            vtt(("LF", lo, hi), (b, lo, hi), ("thr", lo, hi), A.is_gt)
+            op("v", [("trm", lo, hi), ("LF", lo, hi)], [("SC", lo, hi)],
+               lambda q: q.tensor_tensor_scan(T.SC[:, lo:hi], T.trm[:, lo:hi], T.LF[:, lo:hi], 0.0, A.max, A.mult))
+
+        for c in range(14):
+            e = ("EQ", 240 * c, 240 * c + 224 - 16 * c)
+            vts(e, ("DR", 16 * c, 224), ("DW", c, c + 1), A.is_equal)
+            for b, lo, hi in half:
+                lo = max(lo, 16 * c + 16)
+                if lo < hi:
+                    mm((b, lo, hi), ("BIG",), (e[0], e[1] + lo - 16 * c, e[1] + hi - 16 * c), False, False)
+            if c % 7 == 6:
+                strips(c // 7)
+            if c == 2:
+                vts(("B1",), lst(n, "EL", 224, 238), ("A1", 0, 1), A.add, 2048.0, A.add)
+            if c == 9:
+                vts(("KD",), ("DO",), 1.0 / 32, A.mult, 191.515625, A.add)
+        losers(0)
+        losers(1)
+        mm(("pZ", 0, 224), ("ID",), ("DO",), True, False)
+        mm(("pZ", 0, 224), ("NID32",), ("KD",), False, True)
+        act(("DRED",), ("pZ", 0, 224), AF.Copy, bias=5984.0)
+        mm(("pD", 256, 480), ("ID",), ye(n), True, True)
+        for t in range(8):
+            mm(("pS", 0, 28), mat("SKA", t), ("EL", el + t, el + 224, 8), t == 0, t == 7)
+        if n < ST - 1:
+            op("s", [(ye(n)[0], ye(n)[2], ye(n)[2] + 224), ("A1", 0, 1)], [("BR", 0, 224)],
+               lambda q: q.activation(T.BR[:], T.YE[:, 448 * n + 224:448 * n + 448], AF.Identity, bias=T.A1[:]))
+
+    for n in range(ST):
+        if n:
+            arrive(n)
+        fetch(n)
+        if n:
+            mm(("pW", 32, 46), ("ONE",), ("sel",), True, True)
+        send(lst(n, "EL", 0, 238), lst(n, "EF", 0, 238), "ae%d" % n)
+        big(n)
+        ready(n)
+
+    dma("y", [rg(zin(ST))], [], T.yy[:], ap(zin(ST)), "d_o0")
+    arrive(ST)
+    vts(("fo", 0, 14), ("Tn",), -2048.0, A.add)
+    vcp(("fo", 14, 28), ("lin", 1, 28, 2))
+    for r in range(16):
+        mm(("pS", r, 448, 16), mat("BC", r), ("fo",), True, True)
+    for i, k in ((5, 0), (6, 0), (5, 2), (6, 2), (5, 3), (6, 3)):
+        reduced(i, k)
+    vts(("fr", 0, 224), ("pS", 0, 224), 2048.0, A.add)
+    vts(("fr", 224, 448), ("pS", 224, 448), 1.0 / 32, A.mult)
+    dma("s", [("fr", 0, 224)], [], T.yt[:], T.fr[0:128:16, 0:224], "d_t")
+    dma("s", [("fr", 224, 448)], [], T.yl[:], T.fr[0:128:16, 224:448], "d_l")
+    for s in SEMAPHORES:
+        if count[s] and known["p"].get(s, 0) < count[s]:
+            g.wait_ge(T.sem[s], count[s])

@@ -1,10 +1,14 @@
 from concourse.mybir import AluOpType as A, AxisListType, ActivationFunctionType as AF
 
 NP, NB, NR, ST = 3584, 224, 4, 8
-RB = 3
-LATE = 4
-CUT = 96
-CH = [(0, 12), (12, 28), (28, 48), (48, 72), (72, 92), (92, 112)]
+EARLY = 160
+CUT = 64
+CH = [(0, 8), (8, 20), (20, 32), (32, 56), (56, 80), (80, 98), (98, 112)]
+ARR = ((0, EARLY), (EARLY, NB))
+MSG = ((-28, EARLY), (EARLY, NB))
+FET = ((0, CUT, "pA"), (CUT, NB, "pB"))
+HALF = (("pY", 0, 112), ("pB", 112, 224))
+NEWS = ((0, 64), (64, 160), (160, 224))
 
 
 def _sb(dtype, **widths):
@@ -12,22 +16,23 @@ def _sb(dtype, **widths):
 
 
 SCRATCH = {
-    **_sb("int32", ilb=NP, TLi=2 * NB, TLj=2 * NB, iw=14, ip=14, ipq=14, SI=28, SJ=28, q=14, c2=28, b2=28, ao=28,
-          t1=14, t2=14, t3=14, Tn=14, B1=14),
-    **_sb("float16", f16t=NP, PM32=512, EF=8 * 240, EL=8 * 240, KQ=NB, fo=28),
-    **_sb("uint16", EO=8 * 240, DR=NB, DWu=16, OFF=16, AO=28),
-    **_sb("float32", h64=64, h32=32, rm=16, rq=16, wq1=1, th16=16, DG=NB, thA=NB, thB=NB, thr=NB, trm=NB, SC=NB, DW=14,
-          o2=14, sd=28, sa=28, lin=28, Ar=1, Au=1, A1=1, fr=2 * NB),
-    **_sb("bfloat16", XT=NP, LT=NP, WT=NP + NB, YW=NP, KF=NP, TLb=3 * NB, ONE=128, ZER=128, BO0=128, BO=128, BOE=256,
-          ID=128, NID=128, NID32=128, P4=512, P32=512, SEL=2048, BC=2048, SKA=1024, SKD=1024, WQ=128, BIG=128,
-          MASK=1792, ZS=9 * 448, ZO=8 * NB, YE=8 * 448, LF=NB, KA=1, DO=NB, KD=NB, DRED=NB, sel=14, bw=14,
-          BR=NB, WA=NB, LG=NB, VE=1792, U=1792, M=1792),
+    **_sb("int32", ilb=NP, TLi=2 * NB, MODi=128, iw=14, ip=14, ipq=14, q=14, c2=28, ao=28, hi0=14, t1=14, t2=14, t3=14),
+    **_sb("float16", f16t=NP, TLh=2 * NB, EF=8 * NB, EL=8 * NB, fo=28),
+    **_sb("uint16", DR=NB, DWu=16, OFF=16, AO=28),
+    **_sb("float32", h64=64, h32=32, rm=16, rq=16, qt=16, zr=16, wq1=1, wq2=1, th16=16, DG=NB, trf=NB, PK=2 * NB,
+          trm=NB, SC=NB, DW=14, o2=14, LB=56, Ar=1, Au=1, A1=1, Aj=14, fr=2 * NB),
+    **_sb("bfloat16", XT=NP, WT=NP + NB, YW=NP, KF=NP, ONE=128, BO0=128, BO=128, BO8=128, G8=128, MOD=512,
+          ID=128, NID=128, NID32=128, P4=512, P32=512, BC=256, SKA=1024, SKD=1024, WQ=128, BIG=128, NEG=NB, NE2=NB,
+          NTH=NB, RST=2 * NB, ZS=9 * 256, ZO=9 * 256, YE=8 * NB, SG=NB, LF=NB, KA=1, DO=NB,
+          KD=NB, NW=NB, NK=NB, B=14, LL=28, sd=28, sa=56, WA=NB, LG=NB, VE=1792, MASK=1792, U=1792, M=1792),
     "EQ": ("sbuf", [128, 14, 240], "bfloat16"),
-    **{n: ("psum", [128, 512], "float32") for n in ("pXR", "pE", "pO", "pZ", "pW", "pS", "pD", "pC")},
+    "EO": ("sbuf", [128, 2, 112], "uint16"),
+    **{n: ("psum", [128, 512], "float32") for n in ("pA", "pB", "pZ", "pY", "pD", "pW", "pE", "pL")},
 }
 SEMAPHORES = (["cv", "ct", "cs", "cp", "loc", "d_tk", "d_ln", "d_y", "d_x0", "d_x1", "d_t", "d_l"]
               + ["d_il%d" % i for i in range(7)] + ["d_o%d" % i for i in range(8)]
               + ["a%s%d" % (k, n) for k in "zbye" for n in range(ST)])
+TOP = ("TLi", "TLh", "G8", "fr")
 
 
 def rank_program(g, core, T, topo):
@@ -85,7 +90,7 @@ def rank_program(g, core, T, topo):
             h.append((lo, hi, e, s, v, w, asy))
 
     def access(rd, wr):
-        return [(n, lo, hi, False) for (n, lo, hi) in rd] + [(n, lo, hi, True) for (n, lo, hi) in wr]
+        return [rg(o) + (False,) for o in rd] + [rg(o) + (True,) for o in wr]
 
     def op(e, rd, wr, fn):
         acc = access(rd, wr)
@@ -106,47 +111,50 @@ def rank_program(g, core, T, topo):
         if o[0] == "EQ":
             c, a = divmod(o[1], 240)
             return T.EQ[:, c, a:a + o[2] - o[1]] if len(o) == 3 else T.EQ[:, c:o[2] // 240, 0:16]
+        if o[0] == "EO":
+            return T.EO[:, o[3], o[1]:o[2]] if len(o) == 4 else T.EO[:, :, o[1]:o[2]]
+        rows = slice(0, 8) if o[0] in TOP or o[-1] == "top" else slice(None)
+        o = o[:-1] if o[-1] == "top" else o
         if len(o) == 1:
-            return T[o[0]][:]
+            return T[o[0]][rows]
         if len(o) == 4:
-            return T[o[0]][:, o[1]:o[2]:o[3]]
-        return T[o[0]][:, o[1]:o[2]]
+            return T[o[0]][rows, o[1]:o[2]:o[3]]
+        return T[o[0]][rows, o[1]:o[2]]
 
     def rg(o):
         if o[0] == "sa":
-            return ("sa%d" % (o[1] % 2), 0, 28)
+            return ("sa%d" % (o[1] % 2), 0, 56)
         return (o[0], 0, SCRATCH[o[0]][1][1]) if len(o) == 1 else (o[0], o[1], o[2])
 
     def vts(out, i, s1, o0, s2=None, o1=None):
-        rd = [rg(i)]
-        if isinstance(s1, tuple):
-            rd.append(rg(s1))
-            s1 = ap(s1)
-        if isinstance(s2, tuple):
-            rd.append(rg(s2))
-            s2 = ap(s2)
+        rd = [i] + [s for s in (s1, s2) if isinstance(s, tuple)]
+        s1, s2 = [ap(s) if isinstance(s, tuple) else s for s in (s1, s2)]
         if o1 is None:
-            op("v", rd, [rg(out)], lambda q: q.tensor_scalar(ap(out), ap(i), s1, None, o0))
+            op("v", rd, [out], lambda q: q.tensor_scalar(ap(out), ap(i), s1, None, o0))
         else:
-            op("v", rd, [rg(out)], lambda q: q.tensor_scalar(ap(out), ap(i), s1, s2, o0, o1))
+            op("v", rd, [out], lambda q: q.tensor_scalar(ap(out), ap(i), s1, s2, o0, o1))
 
     def vtt(out, a, b, o):
-        op("v", [rg(a), rg(b)], [rg(out)], lambda q: q.tensor_tensor(ap(out), ap(a), ap(b), o))
+        op("v", [a, b], [out], lambda q: q.tensor_tensor(ap(out), ap(a), ap(b), o))
 
     def vcp(out, i):
-        op("v", [rg(i)], [rg(out)], lambda q: q.tensor_copy(ap(out), ap(i)))
+        op("v", [i], [out], lambda q: q.tensor_copy(ap(out), ap(i)))
+
+    def scan(out, a, b, o0, o1, init=0.0, also=()):
+        op("v", [a, b] + list(also), [out], lambda q: q.tensor_tensor_scan(ap(out), ap(a), ap(b), init, o0, o1))
 
     def fill(out, c):
-        op("v", [], [rg(out)], lambda q: q.memset(ap(out), c))
+        op("v", [], [out], lambda q: q.memset(ap(out), c))
 
-    def act(out, i, f, **kw):
-        op("s", [rg(i)] + ([("rm", 0, 16)] if "scale" in kw else []), [rg(out)], lambda q: q.activation(ap(out), ap(i), f, **kw))
-
-    def gat(out, win, off):
-        op("s", [rg(win), rg(off)], [rg(out)], lambda q: q.activation(ap(out), ap(win).indirect(ap(off)), AF.Copy))
+    def act(out, i, f, off=None, **kw):
+        cols = {k: v for k, v in kw.items() if isinstance(v, tuple)}
+        kw.update({k: ap(v) for k, v in cols.items()})
+        src = ap(i).indirect(ap(off)) if off else ap(i)
+        op("s", [i] + ([off] if off else []) + [v for k, v in cols.items() if k != "accum_out"],
+           [out] + [v for k, v in cols.items() if k == "accum_out"], lambda q: q.activation(ap(out), src, f, **kw))
 
     def mm(out, l, r, start, stop):
-        op("t", [rg(l), rg(r)], [rg(out)], lambda q: q.matmul(ap(out), ap(l), ap(r), start, stop))
+        op("t", [l, r], [out], lambda q: q.matmul(ap(out), ap(l), ap(r), start, stop))
 
     def mat(n, r):
         return (n, 128 * r, 128 * r + 128)
@@ -159,378 +167,381 @@ def rank_program(g, core, T, topo):
     n_in = len(topo.engines(prv, core))
 
     def send(dst, src, s):
-        waits("p", [rg(src) + (False,)])
+        waits("p", access([src], []))
         g.remote_dma(out_ap=ap(dst), in_ap=ap(src), remote_sem=T.sem[s], local_sem=T.sem["loc"], pid=pid,
                      routing_id=rid, dma_engine_mask=emask)
         count["loc"] += n_out
 
     def lands(dst, s):
         count[s] = n_in
-        note("r", [rg(dst) + (True,)], s, n_in, True)
+        note("r", access([], [dst]), s, n_in, True)
 
-    def zin(n):
-        return ("ZS", 448 * n, 448 * n + 224)
-
-    def ye(n):
-        return ("YE", 448 * n, 448 * n + 224)
-
-    def zparts(b, lo, hi):
-        return (b, lo, lo + 2 * CH[LATE][0]), (b, lo + 2 * CH[LATE][0], hi)
-
-    def row(n):
-        return ("ZS", 448 * n + 224, 448 * n + 448)
-
-    def lst(n, b, lo, hi):
-        return (b, 240 * n + lo, 240 * n + hi)
+    def slot(b, n, lo=0, hi=NB):
+        o = 256 * n + 32 if b in ("ZS", "ZO") else NB * n
+        return (b, o + lo, o + hi)
 
     for n in range(ST):
-        lands(("YE", 448 * n, 448 * n + 448), "ay%d" % n)
-        lands(lst(n, "EL", 0, 238), "ae%d" % n)
-        for z, s in zip(zparts(*zin(n + 1)), "zb"):
-            lands(z, "a%s%d" % (s, n))
+        lands(slot("YE", n), "ay%d" % n)
+        lands(slot("EL", n), "ae%d" % n)
+        for (lo, hi), s in zip(MSG, "zb"):
+            lands(slot("ZS", n + 1, lo, hi), "a%s%d" % (s, n))
 
-    fill(("TLi",), 0)
-    fill(("ONE",), 1.0)
+    dma("s", [], [("TLi", 0, 224)], ap(("TLi", 0, 224)), T.tk0[:], "d_tk")
+    dma("s", [], [("TLi", 224, 448)], ap(("TLi", 224, 448)), T.ln0[:], "d_ln")
+    dma("s", [], [slot("ZS", 0)], ap(slot("ZS", 0)), T.y0[:], "d_y")
     for i in range(7):
         b = ("ilb", 512 * i, 512 * i + 512)
-        dma("y", [], [rg(b)], ap(b), T.il[:, 512 * i:512 * i + 512], "d_il%d" % i)
-    dma("s", [], [("TLi", 0, 224)], T.TLi[0:128:16, 0:224], T.tk0[:], "d_tk")
-    dma("s", [], [("TLi", 224, 448)], T.TLi[0:128:16, 224:448], T.ln0[:], "d_ln")
-    dma("s", [], [rg(zin(0))], ap(zin(0)), T.y0[:], "d_y")
+        dma("y", [], [b], ap(b), T.il[:, 512 * i:512 * i + 512], "d_il%d" % i)
     for i in range(2):
         b = ("XT", 1792 * i, 1792 * i + 1792)
-        dma("y", [], [rg(b)], ap(b), T.xw[:, 1792 * i:1792 * i + 1792], "d_x%d" % i)
+        dma("y", [], [b], ap(b), T.xw[:, 1792 * i:1792 * i + 1792], "d_x%d" % i)
 
-    def asel(out, i, pat, cmp, base, cm, other=0.0):
-        op("p", [rg(i)], [rg(out)], lambda q: q.affine_select(ap(out), ap(i), pat, cmp, other, base, cm))
-    asel(("BO0",), ("ONE",), [[-16, 8], [0, 16]], A.is_ge, 0, 1)
+    def asel(out, i, pat, cmp, base, cm):
+        op("p", [i], [out], lambda q: q.affine_select(ap(out), ap(i), pat, cmp, 0.0, base, cm))
+
+    def iota(out, pat, base, cm, **kw):
+        op("p", [], [out], lambda q: q.iota(ap(out), pat, base, cm, **kw))
+    fill(("ONE",), 1.0)
+    iota(("MODi",), [[0, 4], [1, 32]], -1792, 0)
     asel(("ID",), ("ONE",), [[-1, 128]], A.is_equal, 0, 1)
+    asel(("G8",), ("ONE", 0, 128, "top"), [[1, 8], [0, 16]], A.is_equal, 0, -1)
+    asel(("BO0",), ("ONE",), [[-16, 8], [0, 16]], A.is_ge, 0, 1)
     asel(("BO",), ("BO0",), [[16, 8], [0, 16]], A.is_ge, 15, -1)
-    fill(("SEL",), 0.0)
-    asel(("SKD",), ("SEL", 0, 1024), [[0, 1024]], A.is_ge, -1, 0)
-    asel(mat("BOE", 0), ("BO",), [[0, 8], [-1, 16]], A.is_ge, 7, 0)
-    asel(mat("BOE", 1), ("BO",), [[0, 8], [1, 16]], A.is_ge, -8, 0)
-    for k, (h, base) in enumerate(((0, 0), (1, 16), (0, -1), (1, 15))):
-        asel(mat("P4", k), mat("BOE", h), [[-16, 8], [-2, 16]], A.is_equal, base, 1)
-    op("p", [], [("iw", 0, 14)], lambda q: q.iota(T.iw[:], [[16, 14]], 0, 1))
-    op("p", [], [("ip", 0, 14)], lambda q: q.iota(T.ip[:], [[0, 14]], 0, 1))
-    for r in range(16):
-        fill(("th16", r, r + 1), 2.0 * 4.0 ** (15 - r))
-    vts(("NID32",), ("ID",), -32.0, A.mult)
-    asel(("SKA",), ("SKD",), [[0, 1024]], A.is_ge, -1, 0)
-    asel(("ZER",), ("ID",), [[0, 128]], A.is_ge, -1, 0)
+    for k, base in enumerate((0, 16, -1, 15)):
+        asel(mat("P4", k), ("BO",), [[-16, 8], [-2, 16]], A.is_equal, base, 1)
+    send(slot("YE", 0), slot("ZS", 0), "ay0")
+    iota(("iw",), [[16, 14]], 0, 1)
+    iota(("ip",), [[0, 14]], 0, 1)
+    iota(("trf",), [[1, NB]], NP, 0, allow_small_or_imprecise_dtypes=True)
     for k in range(2):
-        asel(("MASK", 896 * k, 896 * k + 896), ("SKA", 0, 896), [[0, 112], [1, 8]], A.is_equal, 0, 0, 256.0)
+        asel(mat("BC", k), ("ONE",), [[-16, 8], [0, 16]], A.is_equal, -7 - 8 * k, 1)
+    for m, k in (("SKD", 7), ("SKA", 0)):
+        for t in range(8):
+            asel(mat(m, t), ("BO",), [[-16, 8], [-8, 16]], A.is_equal, 16 * t - k, 1)
+    fill(("RST",), 1.0)
+    fill(("qt",), 0.25)
+    fill(("zr",), 0.0)
+    fill(("RST", 0, 448, 16), 0.0)
+    for k in range(4):
+        vcp(("pW", 128 * k, 128 * k + 128), ("MODi",))
+    vts(("NID32",), ("ID",), -32.0, A.mult)
+    vtt(("h64",), ("ID", 0, 64), ("ID", 64, 128), A.add)
+    fill(("MASK",), 256.0)
+    vtt(("h32",), ("h64", 0, 32), ("h64", 32, 64), A.add)
+    fill(("MASK", 0, 1792, 8), 0.0)
 
-    def halves(i):
-        lo, hi = 512 * i, 512 * i + 512
-        vts(("f16t", lo, hi), ("ilb", lo, hi), -1792.0, A.add)
+    def shift(i):
+        vtt(("f16t", 512 * i, 512 * i + 512), ("ilb", 512 * i, 512 * i + 512), ("pW",), A.add)
 
     def table(i):
         lo, hi = 512 * i, 512 * i + 512
-        vts(("LT", lo, hi), ("f16t", lo, hi), 1.0 / 32, A.mult, 184.515625, A.add)
-        pb = ("pXR", "pE", "pO", "pZ")[i % 4]
+        vts(("KF", lo, hi), ("f16t", lo, hi), 1.0 / 32, A.mult, 184.515625, A.add)
+        pb = ("pA", "pB", "pZ")[i % 3]
         mm((pb,), ("ID",), ("f16t", lo, hi), True, False)
-        mm((pb,), ("NID32",), ("LT", lo, hi), False, True)
+        mm((pb,), ("NID32",), ("KF", lo, hi), False, True)
         act(("WT", lo, hi), (pb,), AF.Copy, bias=5920.0)
 
-    def clocks():
-        vts(("TLj", 0, 224), ("TLi", 0, 224), 4064, A.bitwise_and)
-        vts(("TLj", 224, 448), ("TLi", 0, 224), 31, A.bitwise_and)
-        vcp(("TLb", 0, 448), ("TLj",))
-        vcp(("TLb", 448, 672), ("TLi", 224, 448))
-        for r in range(16):
-            mm(("pW", 0, 42), mat("SEL", r), ("TLb", r, 672, 16), r == 0, r == 15)
+    def diagonal():
+        for lo, hi in ((0, 16), (16, 32)):
+            act(("DG", lo, hi), ("rm",), AF.Copy)
+        act(("BO8",), ("BO",), AF.Copy, scale=8192.0)
+        act(("DG", 32, 64), ("DG", 0, 32), AF.Copy)
+        act(("BIG",), ("BO",), AF.Copy, scale=2.0 ** 32)
+        act(("DG", 64, 128), ("DG", 0, 64), AF.Copy)
+        act(("NID",), ("ID",), AF.Copy, scale=-1.0)
+        act(("DG", 128, 224), ("DG", 0, 96), AF.Copy)
+        act(("P32", 0, 256), ("P4", 0, 256), AF.Copy, scale=32.0)
+        act(("NE2",), ("DG",), AF.Copy, scale=65536.0 + 2.0 ** 20, bias=-2.0 ** 20)
 
-    def places():
-        vcp(("c2", 0, 14), ("pW", 14, 28))
-        vcp(("bw",), ("pW", 14, 28))
-        vts(("b2", 0, 14), ("pW", 28, 42), 32.0, A.mult)
-        vcp(("t1",), ("pW", 0, 14))
-        vtt(("ao", 0, 14), ("c2", 0, 14), ("b2", 0, 14), A.add)
-        vcp(("AO", 0, 14), ("ao", 0, 14))
-        vtt(("Tn",), ("t1",), ("c2", 0, 14), A.add)
-
-    def broadcast(dst, src, lo):
-        for r in range(16):
-            mm((dst, r + lo, lo + 224, 16), mat("BC", r), src, True, True)
-
-    def pick(m, k):
+    def spread():
         for h in range(2):
-            for t in range(8):
-                act((m, 128 * t + 2 * t + h, 128 * t + 128, 16), ("ID", k + 8 * h, 128, 16), AF.Copy)
+            mm(("pE", 224 * h, 224 * h + 224), ("ID",), ("NE2",), h == 0, False)
+        mm(("pE", 0, 448), ("G8",), ("TLh",), False, True)
+    lin = ("LB", 1, 28, 2)
+    between = [
+        [lambda: vtt(("rm",), ("h32", 0, 16), ("h32", 16, 32), A.add), lambda: vts(("TLh",), ("TLi",), -2048.0, A.add),
+         diagonal],
+        [lambda: scan(("th16",), ("qt",), ("zr",), A.mult, A.add, 2.0 ** 33),
+         lambda: fill(("sd",), 0.0), lambda: fill(("A1",), 1.0), lambda: fill(slot("ZO", 0, -14, 0), 129.0)],
+        [spread, lambda: vtt(("rq",), ("rm",), ("th16",), A.mult),
+         lambda: act(("P32", 256, 512), ("P4", 256, 512), AF.Copy, scale=32.0)],
+        [lambda: scan(("PK",), ("RST",), ("pE", 0, 448), A.mult, A.max), lambda: vts(("ipq",), ("ip",), 112, A.bitwise_and),
+         lambda: op("v", [("rq",)], [("wq1",)], lambda q: q.tensor_reduce(T.wq1[:], T.rq[:], AxisListType.X, A.add))],
+        [lambda: vts(("q",), ("PK", 15, 224, 16), -63488.0, A.add),
+         lambda: vts(lin, ("PK", 239, 448, 16), -63488.0, A.add, 32.0, A.mult),
+         lambda: vtt(("iw",), ("iw",), ("ipq",), A.subtract)],
+        [lambda: vts(("c2", 0, 14), ("q",), 31, A.bitwise_and), lambda: vts(("hi0",), ("q",), 4064, A.bitwise_and),
+         lambda: vts(("wq2",), ("wq1",), -1.0, A.mult, -1.0, A.add)],
+        [lambda: vtt(("ao", 0, 14), ("c2", 0, 14), lin, A.add), lambda: vcp(slot("ZO", 0, -28, -14), ("c2", 0, 14)),
+         lambda: vts(("LB", 29, 56, 2), ("iw",), 16.0, A.mult)],
+    ]
+    for i in range(7):
+        shift(i)
+        if i:
+            table(i - 1)
+        for f in between[i]:
+            f()
+    table(6)
+    vcp(("AO", 0, 14), ("ao", 0, 14))
 
     def weights():
-        op("p", [], [("trm", 0, 224)], lambda q: q.iota(T.trm[:], [[1, 224]], NP, 0, allow_small_or_imprecise_dtypes=True))
-        vtt(("rq",), ("rm",), ("th16",), A.mult)
-        vcp(("DG", 0, 16), ("rm",))
-        vts(("ipq",), ("ip",), 112, A.bitwise_and)
-        vts(("BIG",), ("BO",), 2.0 ** 32, A.mult)
-        op("v", [("rq", 0, 16)], [("wq1", 0, 1)], lambda q: q.tensor_reduce(T.wq1[:], T.rq[:], AxisListType.X, A.add))
-        vcp(("DG", 16, 32), ("DG", 0, 16))
-        vtt(("iw",), ("iw",), ("ipq",), A.subtract)
-        fill(("sd",), 0.0)
-        fill(("Ar",), 0.0)
-        vcp(("DG", 32, 64), ("DG", 0, 32))
-        vts(("WQ",), ("BO",), ("wq1", 0, 1), A.mult, 0.5, A.mult)
-        vts(("b2", 14, 28), ("iw",), 16.0, A.mult)
-        vcp(("DG", 64, 128), ("DG", 0, 64))
-        vts(("NID",), ("ID",), -1.0, A.mult)
-        vcp(("DG", 128, 224), ("DG", 0, 96))
-        vts(("thA",), ("DG",), ("wq1", 0, 1), A.mult)
-        vts(("thB",), ("DG",), 1.0, A.subtract)
+        act(("WQ",), ("BO",), AF.Copy, scale=("wq1",))
+        act(("NTH",), ("DG",), AF.Copy, scale=("wq2",), bias=1.0)
+        act(("NEG",), ("DG",), AF.Copy, scale=2.0 ** 20, bias=-2.0 ** 20)
+        act(("MOD",), ("pW",), AF.Copy, bias=1792.0)
 
-    for r in range(16):
-        act(("SEL", 128 * r + r, 128 * r + 128, 16), ("BO", r, 128, 16), AF.Copy)
-    halves(0)
-    vtt(("h64",), ("ID", 0, 64), ("ID", 64, 128), A.add)
-    halves(1)
-    vtt(("h32",), ("h64", 0, 32), ("h64", 32, 64), A.add)
-    table(0)
-    vtt(("rm",), ("h32", 0, 16), ("h32", 16, 32), A.add)
-    halves(2)
-    for r in range(16):
-        act(mat("BC", r), ("BO",), AF.Copy, scale=T.rm[:, r:r + 1])
-    table(1)
-    halves(3)
-    table(2)
-    halves(4)
-    table(3)
-    halves(5)
-    table(4)
-    clocks()
-    halves(6)
-    table(5)
-    pick("SKD", 7)
-    table(6)
-    places()
-    broadcast("pS", ("bw",), 256)
-    act(row(0), ("pS", 256, 480), AF.Copy)
-    vts(("PM32",), ("P4",), -32.0, A.mult)
-    vts(("P32",), ("P4",), 32.0, A.mult)
-    weights()
+    SUM, NEW = ("pE", "pL"), ("pD", "pA")
 
-    def reduced(i, k):
-        lo, hi = 512 * i, 512 * i + 512
-        if k == 0:
-            vts(("KF", lo, hi), ("WT", lo, hi), 1.0 / 32, A.mult, 191.515625, A.add)
-        elif k == 1:
-            pb = ("pE", "pO", "pZ")[i % 3]
-            mm((pb,), ("ID",), ("WT", lo, hi), True, False)
-            mm((pb,), ("NID32",), ("KF", lo, hi), False, True)
-            act(("YW", lo, hi), (pb,), AF.Copy, bias=6144.0)
-        elif k == 2:
-            vts(("f16t", lo, hi), ("KF", lo, hi), -32.0, A.mult, 6144.0, A.add)
-        else:
-            vtt(("YW", lo, hi), ("WT", lo, hi), ("f16t", lo, hi), A.add)
-        if k % 2:
-            dma("y", [("YW", lo, hi)], [], T.yw[:, lo:hi], T.YW[:, lo:hi], "d_o%d" % (1 + i))
+    def reach(n, p):
+        lo, hi = ARR[p]
+        vtt(("SG", lo, hi), slot("ZS", n, lo, hi), ("pZ", lo, hi), A.is_ge)
 
-    def more(n, i):
-        if n == ST:
-            reduced(i, 0)
-            reduced(i, 1)
+    def sums(n, p):
+        lo, hi = ARR[p]
+        mm((SUM[p], lo, hi), ("BO",), slot("ZS", n, lo, hi), False, False)
+        mm((SUM[p], lo, hi), ("BO8",), ("SG", lo, hi), False, True)
 
-    def arrive(n):
-        z = zin(n)
-        vtt(("ZS", 448 * n + 224, 448 * n + 448), z, ("pD", 256, 480), A.is_ge)
-        for r in range(16):
-            mm(("pW", 0, 28), mat("SEL", r), ("ZS", 448 * n + r, 448 * n + 448, 16), r == 0, r == 15)
-        vtt(("o2",), ("SC", 15, 224, 16), ("DW",), A.max)
-        vts(("SI",), ("pS", 0, 28), 1792.0, A.add)
+    def renew(n, p):
+        lo, hi = ARR[p]
+        b = (NEW[p], lo, hi)
+        mm(b, ("ID",), ("DO", lo, hi), True, False)
+        mm(b, ("ID",), slot("ZS", n, lo, hi), False, True)
+        act(("KD", lo, hi), b, AF.Copy, scale=1.0 / 32, bias=191.515625)
+        act(("NW", lo, hi), b, AF.Copy, bias=-64.0)
+        act(("NK", lo, hi), ("KD", lo, hi), AF.Copy, scale=-32.0, bias=6208.0)
+
+    def rewrite(k):
+        lo, hi = NEWS[k]
+        off = ("OFF", lo // 16, hi // 16)
+        op("v", [("NW", lo, hi), ("NK", lo, hi), off], [("WT",)],
+           lambda q: q.tensor_tensor(T.WT[:].indirect(ap(off)), T.NW[:, lo:hi], T.NK[:, lo:hi], A.add))
+
+    def pick(p):
+        lo, hi = ARR[p]
+        scan(("PK", lo, hi), ("RST", lo, hi), (SUM[p], lo, hi), A.mult, A.max)
+
+    def losers(h):
+        lo, hi = HALF[h][1:]
+        scan(("SC", lo, hi), ("trm", lo, hi), ("LF", lo, hi), A.max, A.mult)
+
+    def late(n):
+        reach(n, 1)
+        renew(n, 1)
+        sums(n, 1)
+        losers(0)
+        losers(1)
+        pick(0)
+        vtt(("o2",), ("SC", 15, NB, 16), ("DW",), A.max)
+        pick(1)
         vcp(("OFF", 0, 14), ("o2",))
-        vts(("SJ",), ("SI",), 4064, A.bitwise_and)
-        op("v", [rg(z), ("DRED", 0, 224), ("OFF", 0, 14)], [("WT", 0, NP + NB)],
-           lambda q: q.tensor_tensor(T.WT[:, 0:NP + NB].indirect(T.OFF[:, 0:14]), T.DRED[:], ap(z), A.add))
-        more(n, 0)
-        more(n, 1)
-        vtt(("sd", 1, 28, 2), ("SJ", 14, 28), ("SJ", 0, 14), A.subtract)
-        vcp(("sa", 1, 28, 2), ("SJ", 0, 14))
-        vts(("sa", 0, 28, 2), ("pW", 14, 28), 9.0, A.is_ge)
+        pk = ("PK", 15, NB, 16)
+        vts(("sa", 0, 28, 2), pk, 9.0 * 8192, A.is_ge)
+        vtt(("q",), pk, ("B",), A.add)
+        rewrite(0)
+        scan(("LB", 0, 28), ("sd", 0, 28), ("sa", 0, 28), A.mult, A.add, also=[("sa", 1, 28)])
+        vts(("c2", 0, 14), ("q",), 31, A.bitwise_and)
         if n < ST:
-            vtt(("q",), ("pW", 0, 14), ("B1",), A.add)
-        vcp(("t1",), ("pW", 0, 14))
-        more(n, 2)
-        op("v", [("sd", 0, 28), ("sa0", 0, 28), ("sa1", 0, 28)], [("lin", 0, 28)],
-           lambda q: q.tensor_tensor_scan(T.lin[:], T.sd[:], T.sa[:], 0.0, A.mult, A.add))
-        if n < ST:
-            vts(("c2", 0, 14), ("q",), 31, A.bitwise_and)
             vts(("c2", 14, 28), ("q",), 15, A.bitwise_and)
-        vts(("t2",), ("t1",), 31, A.bitwise_and)
+        rewrite(1)
         if n < ST:
-            vtt(("ao", 0, 14), ("c2", 0, 14), ("lin", 1, 28, 2), A.add)
-            vtt(("ao", 14, 28), ("c2", 14, 28), ("b2", 14, 28), A.add)
-        more(n, 3)
-        vtt(("t3",), ("t2",), ("B1",), A.add)
+            vtt(("ao",), ("c2",), ("LB", 1, 56, 2), A.add)
+        rewrite(2)
         if n < ST:
-            vcp(("AO", 0, 14), ("ao", 0, 14))
-            vcp(("AO", 14, 28), ("ao", 14, 28))
-            vcp(("bw",), ("c2", 0, 14))
-            vcp(("sel",), ("sa", 0, 28, 2))
-        more(n, 4)
-        vts(("Tn",), ("t3",), 4095, A.bitwise_and)
-        if n < ST:
-            op("v", [rg(z), ("AO", 14, 28)], [("XT", 0, NP)],
-               lambda q: q.tensor_copy(T.XT[:, 0:NP].indirect(T.AO[:, 14:28]), ap(z)))
+            vcp(("AO",), ("ao",))
 
-    def fetch(n):
-        parts = ((0, CUT, "pXR", ("pE", "pO")), (CUT, NB, "pC", ("pD", "pS")))
-        br = ("BR", 0) if n else row(0)[:2]
+    def carry(n, k):
+        if k == 0:
+            vcp(slot("ZO", n, -28, -14), ("c2", 0, 14))
+            mm(("pW", 64, 78), ("NID32",), slot("ZS", n, -14, 0), True, False)
+            mm(("pW", 64, 78), ("NID",), ("B",), False, False)
+            mm(("pW", 64, 78), ("ID",), slot("ZO", n, -28, -14), False, True)
+            if n < ST:
+                mm(("pW", 80, 94), ("ONE",), ("sa", 0, 28, 2), True, True)
+        else:
+            act(slot("ZO", n, -14, 0), ("pW", 64, 78), AF.Copy, scale=-1.0 / 32, bias=0.484375)
+            if n < ST:
+                act(("Aj",), ("pW", 80, 94), AF.Copy, accum_out=("Ar",))
 
-        def x(o, lo, hi, h=None):
-            return (o[0], o[1] + lo, o[1] + hi) if h is None else (o[0], o[1] + lo + h, o[1] + hi, 2)
+    def lines(f):
+        lo, hi, b = FET[f]
+        off = ("AO", lo // 16, hi // 16)
+        op("v", [("ilb",), off], [("LG", lo, hi)],
+           lambda q: q.tensor_scalar(T.LG[:, lo:hi], T.ilb[:].indirect(ap(off)), 1.0 / 32, 128.515625, A.mult, A.add))
 
-        def lists(part, src, k):
-            lo, hi, _, banks = parts[part]
-            for h in range(2):
-                mm((banks[k // 2], lo // 2, hi // 2), mat({"WA": "P4", "LG": "P32", "KQ": "PM32"}[src], k + h),
-                   x((src, 0), lo, hi, h), False, src == "KQ" and h == 1)
+    def lows(f):
+        lo, hi, b = FET[f]
+        act(("WA", lo, hi), ("WT", 0, NP), AF.Copy, ("AO", lo // 16, hi // 16))
 
-        def floors(part):
-            lo, hi, b, _ = parts[part]
-            mm((b, lo, hi), ("ID",), ("WA", lo, hi), False, True)
-            vts(("KQ", lo, hi), (b, lo, hi), 1.0 / 32, A.mult, 1535.515625, A.add)
+    def lists(f):
+        lo, hi, b = FET[f]
+        w = (hi - lo) // 2
+        for src, m in (("LG", "P32"), ("WA", "P4")):
+            for k in range(4):
+                mm((b, w * (k // 2), w * (k // 2 + 1)), mat(m, k), (src, lo + k % 2, hi, 2),
+                   src == "LG" and k == 0, src == "WA" and k == 3)
 
-        for lo, hi, b, banks in parts:
-            gat(("WA", lo, hi), ("WT", 0, NP), ("AO", lo // 16, hi // 16))
-            gat(("LG", lo, hi), ("LT", 0, NP), ("AO", lo // 16, hi // 16))
-            mm((b, lo, hi), ("ID",), x(br, lo, hi), True, False)
-            if n:
-                mm((b, lo, hi), ("BO",), x(zin(n), lo, hi), False, False)
-        for lo, hi, b, banks in parts:
-            for k in (0, 2):
-                for h in range(2):
-                    mm((banks[k // 2], lo // 2, hi // 2), mat("P4", k + h), x(br, lo, hi, h), h == 0, False)
-                for h in range(2 if n else 0):
-                    mm((banks[k // 2], lo // 2, hi // 2), mat("BOE", h), x(zin(n), lo, hi, h), False, False)
-        floors(0)
-        vts(lst(n, "EF", 224, 238), ("Tn",), -2048.0, A.add)
-        lists(0, "WA", 0)
-        lists(0, "LG", 0)
-        lists(0, "WA", 2)
-        floors(1)
-        for src, k in (("KQ", 0), ("LG", 2), ("KQ", 2)):
-            lists(0, src, k)
-        for src, k in (("WA", 0), ("LG", 0), ("KQ", 0), ("WA", 2), ("LG", 2), ("KQ", 2)):
-            lists(1, src, k)
-        for lo, hi, _, banks in parts:
-            for b, o in ((banks[0], 0), (banks[1], 112)):
-                vts(lst(n, "EO", o + lo // 2, o + hi // 2), (b, lo // 2, hi // 2), 45024.0, A.add)
-                vts(lst(n, "EF", o + lo // 2, o + hi // 2), (b, lo // 2, hi // 2), 43232.0, A.add)
+    def offsets(f):
+        lo, hi, b = FET[f]
+        vts(("EO", lo // 2, hi // 2), (b, 0, hi - lo), -4128.0, A.add)
 
-    def big(n):
-        for (a, b) in CH:
-            gat(("VE", 16 * a, 16 * b), ("XT", 0, NP), lst(n, "EO", a, b))
-            if n and b == CH[RB][1]:
-                broadcast("pS", ("bw",), 256)
-                act(row(n), ("pS", 256, 480), AF.Copy)
-        last = 2 * CH[LATE][0]
-        early, late = zparts(*zin(n))
-        mm(("pZ", 0, last), ("NID",), early, True, False)
-        mm(("pC", 256 + last, 480), ("NID",), late, True, False)
+    ZB = ("pZ", "pY")
 
-        def least(a, b):
-            off = lst(n, "EO", 112 + a, 112 + b)
-            op("v", [("XT", 0, NP), rg(off), ("VE", 16 * a, 16 * b)], [("U", 16 * a, 16 * b)],
-               lambda q: q.tensor_tensor(T.U[:, 16 * a:16 * b], T.XT[:, 0:NP].indirect(ap(off)), T.VE[:, 16 * a:16 * b], A.min))
+    def even(i):
+        a, b = CH[i]
+        act(("VE", 16 * a, 16 * b), ("XT",), AF.Copy, ("EO", a, b, 0))
 
-        def greatest(a, b):
-            r = slice(16 * a, 16 * b)
-            op("v", [("MASK", 16 * a, 16 * b), ("U", 16 * a, 16 * b)], [("M", 16 * a, 16 * b)],
-               lambda q: q.tensor_tensor_scan(T.M[:, r], T.MASK[:, r], T.U[:, r], 0.0, A.min, A.max))
-            o = ("pZ", 2 * a, 2 * b) if 2 * b <= last else ("pC", 256 + 2 * a, 256 + 2 * b)
-            mm(o, ("ID",), ("M", 16 * a + 7, 16 * b, 8), False, 2 * b in (last, 224))
-        for i, c in enumerate(CH):
-            least(*c)
-            if i:
-                greatest(*CH[i - 1])
+    def least(i):
+        a, b = CH[i]
+        off = ("EO", a, b, 1)
+        op("v", [("XT",), off, ("VE", 16 * a, 16 * b)], [("U", 16 * a, 16 * b)],
+           lambda q: q.tensor_tensor(T.U[:, 16 * a:16 * b], T.XT[:].indirect(ap(off)), T.VE[:, 16 * a:16 * b], A.min))
+
+    def greatest(i):
+        a, b = CH[i]
+        scan(("M", 16 * a, 16 * b), ("MASK", 16 * a, 16 * b), ("U", 16 * a, 16 * b), A.min, A.max)
+        mm((ZB[2 * b > EARLY], 2 * a, 2 * b), ("ID",), ("M", 16 * a + 7, 16 * b, 8), False, 2 * b in (EARLY, NB))
+
+    def out_z(n, p):
+        act(slot("ZO", n, *ARR[p]), (ZB[p],) + ARR[p], AF.Abs)
+        send(slot("ZS", n + 1, *MSG[p]), slot("ZO", n, *MSG[p]), "a%s%d" % ("zb"[p], n))
+
+    def step(n):
+        z = slot("ZS", n)
         if n:
-            op("v", [("pW", 32, 46)], [("Ar", 0, 1)], lambda q: q.tensor_reduce(T.Ar[:], T.pW[:, 32:46], AxisListType.X, A.add))
-        greatest(*CH[-1])
-        out = zparts("ZO", 224 * n, 224 * n + 224)
-        act(out[0], ("pZ", 0, last), AF.Abs)
-        act(out[1], ("pC", 256 + last, 480), AF.Abs)
-        send(("YE", 448 * n, 448 * n + 448), ("ZS", 448 * n, 448 * n + 448), "ay%d" % n)
-        for d, o, s in zip(zparts(*zin(n + 1)), out, "zb"):
-            send(d, o, "a%s%d" % (s, n))
+            late(n)
+            send(slot("YE", n), z, "ay%d" % n)
+        for f in range(2):
+            lines(f)
+            lows(f)
+            lists(f)
+        if n:
+            op("v", [z, ("AO", 14, 28)], [("XT",)], lambda q: q.tensor_copy(T.XT[:].indirect(T.AO[:, 14:28]), ap(z)))
+        else:
+            vtt(("trm", 0, NB), ("trf",), ("DG",), A.mult)
+        offsets(0)
+        if n:
+            carry(n, 0)
+        offsets(1)
+        for p in range(2):
+            mm((ZB[p],) + ARR[p], ("NID",), slot("ZS", n, *ARR[p]), True, False)
+        even(0)
+        even(1)
+        least(0)
+        vts(slot("EF", n), ("EO", 0, 112), -1792.0, A.add)
+        send(slot("EL", n), slot("EF", n), "ae%d" % n)
+        least(1)
+        greatest(0)
+        for i in range(2, len(CH)):
+            even(i)
+        if n == 0:
+            weights()
+        mm((SUM[0],) + ARR[0], ("ID",), ("NEG",) + ARR[0], True, False)
+        mm(HALF[1], ("ID",), ("NTH",) + HALF[1][1:], True, False)
+        if n:
+            carry(n, 1)
+            act(("KA",), ("Ar",), AF.Copy, scale=1.0 / 32, bias=191.515625)
+        for i in range(2, len(CH)):
+            least(i)
+            if 2 * CH[i - 1][1] == EARLY:
+                ahead(n)
+            greatest(i - 1)
+            if 2 * CH[i - 1][1] == EARLY:
+                out_z(n, 0)
+                if n:
+                    act(("Au",), ("KA",), AF.Copy, scale=-32.0, bias=6145.0)
+                act(("sa", 1, 56, 2), ("LL",), AF.Copy, scale=32.0, bias=-4128.0)
+        vts(("DR",), ("pD", 0, 224), 1792.0, A.add)
+        greatest(len(CH) - 1)
+        out_z(n, 1)
+        mm(("pZ", 0, NB), ("ID",), slot("YE", n), True, True)
+        mm(HALF[0], ("ID",), ("NTH",) + HALF[0][1:], True, False)
+
+    def ahead(n):
+        el = NB * n
+        for k in range(2):
+            mm(("pD", k, 224, 2), mat("BC", k), ("EL", el + 112, el + 224), True, True)
+        for t in range(8):
+            mm(("pW", 32, 46), mat("SKD", t), ("EL", el + 112 + t, el + 224, 8), t == 0, t == 7)
+        for t in range(8):
+            mm(("pL", 0, 28), mat("SKA", t), ("EL", el + t, el + 224, 8), t == 0, t == 7)
+        act(("DW",), ("pW", 32, 46), AF.Copy, bias=1792.0)
+        act(("LL",), ("pL", 0, 28), AF.Copy, scale=1.0 / 32, bias=184.515625)
 
     def ready(n):
-        el = 240 * n
-        for k in (7, 15):
-            mm(("pD", k // 8, 224, 2), mat("BC", k), ("EL", el + 112, el + 224), True, True)
-        for t in range(8):
-            mm(("pS", 32, 46), mat("SKD", t), ("EL", el + 112 + t, el + 224, 8), t == 0, t == 7)
-        if n == 0:
-            pick("SKA", 0)
-            vtt(("trm",), ("trm",), ("DG",), A.mult)
-            vtt(("thr",), ("thA",), ("thB",), A.add)
-        vts(("KA",), ("Ar",), 1.0 / 32, A.mult, 191.515625, A.add)
-        vts(("Au",), ("KA",), -32.0, A.mult, 6145.0, A.add)
-        vts(("DR",), ("pD", 0, 224), 1792.0, A.add)
-        vts(("DW",), ("pS", 32, 46), 1792.0, A.add)
-        vts(("A1",), ("Au",), ("Ar", 0, 1), A.add)
         vcp(("DWu", 0, 14), ("DW",))
-        gat(("DO",), ("WT", 0, NP), ("DWu", 0, 14))
-        half = (("pC", 0, 112), ("pE", 112, 224))
-        for b, lo, hi in half:
-            mm((b, lo, hi), ("ZER",), ("MASK", lo, hi), True, False)
-
-        def strips(h):
-            mm(half[h], ("WQ",), ("EQ", 7 * 240 * h, 7 * 240 * (h + 1), 1), False, True)
-
-        def losers(h):
-            b, lo, hi = half[h]
-            vtt(("LF", lo, hi), (b, lo, hi), ("thr", lo, hi), A.is_gt)
-            op("v", [("trm", lo, hi), ("LF", lo, hi)], [("SC", lo, hi)],
-               lambda q: q.tensor_tensor_scan(T.SC[:, lo:hi], T.trm[:, lo:hi], T.LF[:, lo:hi], 0.0, A.max, A.mult))
+        if n:
+            act(("A1",), ("Au",), AF.Identity, bias=("Ar",))
+        act(("DO",), ("WT", 0, NP), AF.Copy, ("DWu", 0, 14))
 
         for c in range(14):
             e = ("EQ", 240 * c, 240 * c + 224 - 16 * c)
-            vts(e, ("DR", 16 * c, 224), ("DW", c, c + 1), A.is_equal)
-            for b, lo, hi in half:
+            vts(e, ("DR", 16 * c, 224), ("DW", c, c + 1), A.is_equal, 0.5, A.mult)
+            for b, lo, hi in HALF:
                 lo = max(lo, 16 * c + 16)
                 if lo < hi:
                     mm((b, lo, hi), ("BIG",), (e[0], e[1] + lo - 16 * c, e[1] + hi - 16 * c), False, False)
             if c % 7 == 6:
-                strips(c // 7)
-            if c == 2:
-                vts(("B1",), lst(n, "EL", 224, 238), ("A1", 0, 1), A.add, 2048.0, A.add)
-            if c == 9:
-                vts(("KD",), ("DO",), 1.0 / 32, A.mult, 191.515625, A.add)
-        losers(0)
-        losers(1)
-        mm(("pZ", 0, 224), ("ID",), ("DO",), True, False)
-        mm(("pZ", 0, 224), ("NID32",), ("KD",), False, True)
-        act(("DRED",), ("pZ", 0, 224), AF.Copy, bias=5984.0)
-        mm(("pD", 256, 480), ("ID",), ye(n), True, True)
-        for t in range(8):
-            mm(("pS", 0, 28), mat("SKA", t), ("EL", el + t, el + 224, 8), t == 0, t == 7)
-        if n < ST - 1:
-            op("s", [(ye(n)[0], ye(n)[2], ye(n)[2] + 224), ("A1", 0, 1)], [("BR", 0, 224)],
-               lambda q: q.activation(T.BR[:], T.YE[:, 448 * n + 224:448 * n + 448], AF.Identity, bias=T.A1[:]))
+                h = c // 7
+                mm(HALF[h], ("WQ",), ("EQ", 7 * 240 * h, 7 * 240 * (h + 1), 1), False, True)
+                act(("LF",) + HALF[h][1:], HALF[h], AF.Sign)
+        mm((SUM[1],) + ARR[1], ("ID",), ("NEG",) + ARR[1], True, False)
+        act(("B",), slot("ZS", n + 1, -28, -14), AF.Identity, bias=("A1",))
+        vtt(("sd", 1, 28, 2), ("sa", 29, 56, 2), ("sa", 1, 28, 2), A.subtract)
+        reach(n + 1, 0)
+        renew(n + 1, 0)
+        sums(n + 1, 0)
 
     for n in range(ST):
-        if n:
-            arrive(n)
-        fetch(n)
-        if n:
-            mm(("pW", 32, 46), ("ONE",), ("sel",), True, True)
-        send(lst(n, "EL", 0, 238), lst(n, "EF", 0, 238), "ae%d" % n)
-        big(n)
+        step(n)
         ready(n)
 
-    dma("y", [rg(zin(ST))], [], T.yy[:], ap(zin(ST)), "d_o0")
-    arrive(ST)
-    vts(("fo", 0, 14), ("Tn",), -2048.0, A.add)
-    vcp(("fo", 14, 28), ("lin", 1, 28, 2))
-    for r in range(16):
-        mm(("pS", r, 448, 16), mat("BC", r), ("fo",), True, True)
-    for i, k in ((5, 0), (6, 0), (5, 2), (6, 2), (5, 3), (6, 3)):
-        reduced(i, k)
-    vts(("fr", 0, 224), ("pS", 0, 224), 2048.0, A.add)
-    vts(("fr", 224, 448), ("pS", 224, 448), 1.0 / 32, A.mult)
-    dma("s", [("fr", 0, 224)], [], T.yt[:], T.fr[0:128:16, 0:224], "d_t")
-    dma("s", [("fr", 224, 448)], [], T.yl[:], T.fr[0:128:16, 224:448], "d_l")
+    FIN = ("pB", "pY", "pA", "pZ", "pL", "pD", "pB")
+
+    def reduced(i, k):
+        if not 0 <= i < 7:
+            return
+        lo, hi = 512 * i, 512 * i + 512
+        b = (FIN[i],)
+        if k == 0:
+            mm(b, ("NID",), ("MOD",), True, False)
+        elif k == 1:
+            mm(b, ("ID",), ("WT", lo, hi), False, False)
+        elif k == 2:
+            vtt(("KF", lo, hi), ("WT", lo, hi), ("pE",), A.is_ge)
+        else:
+            mm(b, ("NID32",), ("KF", lo, hi), False, True)
+            act(("YW", lo, hi), b, AF.Copy, bias=32.0)
+            dma("y", [("YW", lo, hi)], [], T.yw[:, lo:hi], T.YW[:, lo:hi], "d_o%d" % (1 + i))
+
+    def rows():
+        for r in range(16):
+            mm(("pW", r, 448, 16, "top"), ("ID", r, 128, 16), ("fo",), True, True)
+    clock = [lambda: vtt(("t1",), ("hi0",), ("c2", 0, 14), A.add),
+             lambda: vts(("t2",), slot("ZO", ST, -14, 0), 32.0, A.mult, -4128.0, A.add),
+             lambda: vtt(("t3",), ("t1",), ("t2",), A.add),
+             lambda: vts(("q",), ("t3",), 4095, A.bitwise_and),
+             lambda: vts(("fo", 0, 14), ("q",), -2048.0, A.add),
+             rows,
+             lambda: vts(("fr", 0, 224), ("pW", 0, 224, "top"), 2048.0, A.add)]
+
+    dma("y", [slot("ZS", ST)], [], T.yy[:], ap(slot("ZS", ST)), "d_o0")
+    late(ST)
+    mm(("pE",), ("ID",), ("MOD",), True, True)
+    for i in range(3):
+        reduced(i, 0)
+    carry(ST, 0)
+    vcp(("fo", 14, 28), ("LB", 1, 28, 2))
+    carry(ST, 1)
+    reduced(0, 1)
+    for i in range(7):
+        reduced(i, 2)
+        reduced(i, 3)
+        reduced(i + 3, 0)
+        reduced(i + 1, 1)
+        clock[i]()
+    vts(("fr", 224, 448), ("pW", 224, 448, "top"), 1.0 / 32, A.mult)
+    dma("s", [("fr", 0, 224)], [], T.yt[:], ap(("fr", 0, 224)), "d_t")
+    dma("s", [("fr", 224, 448)], [], T.yl[:], ap(("fr", 224, 448)), "d_l")
     for s in SEMAPHORES:
         if count[s] and known["p"].get(s, 0) < count[s]:
             g.wait_ge(T.sem[s], count[s])

@@ -3,12 +3,14 @@ from concourse.mybir import AluOpType as A, AxisListType, ActivationFunctionType
 NP, NB, NR, ST = 3584, 224, 4, 8
 EARLY = 160
 CUT = 64
-CH = [(0, 8), (8, 20), (20, 32), (32, 56), (56, 80), (80, 98), (98, 112)]
+CH = [(0, 10), (10, 32), (32, 54), (54, 80), (80, 98), (98, 112)]
 ARR = ((0, EARLY), (EARLY, NB))
 MSG = ((-28, EARLY), (EARLY, NB))
 FET = ((0, CUT, "pA"), (CUT, NB, "pB"))
-HALF = (("pY", 0, 112), ("pB", 112, 224))
-NEWS = ((0, 64), (64, 160), (160, 224))
+HALF = (("pA", 0, 112), ("pB", 112, 224))
+NEWS = ((0, 128), (128, 224))
+LOAD = [512 * i for i in range(7)] + [3392, NP]
+M32 = 1.5 * 2.0 ** 28
 
 
 def _sb(dtype, **widths):
@@ -16,23 +18,23 @@ def _sb(dtype, **widths):
 
 
 SCRATCH = {
-    **_sb("int32", ilb=NP, TLi=2 * NB, MODi=128, iw=14, ip=14, ipq=14, q=14, c2=28, ao=28, hi0=14, t1=14, t2=14, t3=14),
-    **_sb("float16", f16t=NP, TLh=2 * NB, EF=8 * NB, EL=8 * NB, fo=28),
+    **_sb("int32", ilb=NP, TLi=NB, MODi=128, iw=14, ip=14, ipq=14, q=14, c2=14, ao=14, hi0=14, t1=14, t2=14, t3=14),
+    **_sb("float16", f16t=NP, TLh=NB, EF=8 * NB, EL=8 * NB, fo=28),
     **_sb("uint16", DR=NB, DWu=16, OFF=16, AO=28),
-    **_sb("float32", h64=64, h32=32, rm=16, rq=16, qt=16, zr=16, wq1=1, wq2=1, th16=16, DG=NB, trf=NB, PK=2 * NB,
-          trm=NB, SC=NB, DW=14, o2=14, LB=56, Ar=1, Au=1, A1=1, Aj=14, fr=2 * NB),
-    **_sb("bfloat16", XT=NP, WT=NP + NB, YW=NP, KF=NP, ONE=128, BO0=128, BO=128, BO8=128, G8=128, MOD=512,
-          ID=128, NID=128, NID32=128, P4=512, P32=512, BC=256, SKA=1024, SKD=1024, WQ=128, BIG=128, NEG=NB, NE2=NB,
-          NTH=NB, RST=2 * NB, ZS=9 * 256, ZO=9 * 256, YE=8 * NB, SG=NB, LF=NB, KA=1, DO=NB,
-          KD=NB, NW=NB, NK=NB, B=14, LL=28, sd=28, sa=56, WA=NB, LG=NB, VE=1792, MASK=1792, U=1792, M=1792),
+    **_sb("float32", h64=64, h32=32, rm=16, rq=16, qt=16, zr=16, wq1=1, wq2=1, th16=16, DG=NB, trf=NB, PK=NB, tc=1,
+          trm=NB, SC=NB, DW=14, o2=14, LB=140, sd=140, sa=210, THR=14, ONF=128, Ar=1, Au=1, A1=1, Aj=14, fr=2 * NB),
+    **_sb("bfloat16", XT=NP, WT=NP + NB, YW=NP, KF=NP, ONE=128, BO0=128, BO=128, BO8=128, G8=384, MOD=512, BLK=NB,
+          ID=128, NID=128, NID32=128, P4=512, P32=512, BC=256, SKA=144, SKD=144, WQ=128, BIG=128, NEG=NB,
+          NTH=NB, RST=NB, ZS=9 * 256, ZO=9 * 256, YE=8 * NB, SG=NB, LF=NB, KA=1, DO=NB,
+          KD=NB, NW=NB, NK=NB, B=NB, LL=28, WA=NB, LG=NB, VE=1792, MASK=1792, U=1792, M=1792),
     "EQ": ("sbuf", [128, 14, 240], "bfloat16"),
     "EO": ("sbuf", [128, 2, 112], "uint16"),
     **{n: ("psum", [128, 512], "float32") for n in ("pA", "pB", "pZ", "pY", "pD", "pW", "pE", "pL")},
 }
 SEMAPHORES = (["cv", "ct", "cs", "cp", "loc", "d_tk", "d_ln", "d_y", "d_x0", "d_x1", "d_t", "d_l"]
-              + ["d_il%d" % i for i in range(7)] + ["d_o%d" % i for i in range(8)]
+              + ["d_il%d" % i for i in range(8)] + ["d_o%d" % i for i in range(8)]
               + ["a%s%d" % (k, n) for k in "zbye" for n in range(ST)])
-TOP = ("TLi", "TLh", "G8", "fr")
+TOP = {"TLi": 16, "TLh": 16, "G8": 16, "tc": 16, "fr": 8}
 
 
 def rank_program(g, core, T, topo):
@@ -113,7 +115,7 @@ def rank_program(g, core, T, topo):
             return T.EQ[:, c, a:a + o[2] - o[1]] if len(o) == 3 else T.EQ[:, c:o[2] // 240, 0:16]
         if o[0] == "EO":
             return T.EO[:, o[3], o[1]:o[2]] if len(o) == 4 else T.EO[:, :, o[1]:o[2]]
-        rows = slice(0, 8) if o[0] in TOP or o[-1] == "top" else slice(None)
+        rows = slice(0, 8) if o[-1] == "top" else slice(0, TOP[o[0]]) if o[0] in TOP else slice(None)
         o = o[:-1] if o[-1] == "top" else o
         if len(o) == 1:
             return T[o[0]][rows]
@@ -122,8 +124,10 @@ def rank_program(g, core, T, topo):
         return T[o[0]][rows, o[1]:o[2]]
 
     def rg(o):
-        if o[0] == "sa":
-            return ("sa%d" % (o[1] % 2), 0, 56)
+        if o[0] in ("sa", "sd"):
+            return ("%s%d" % (o[0], o[1] % 5), o[1], o[2])
+        if o[0] == "trm" and len(o) == 4:
+            return ("trm", o[1], o[1] + 1)
         return (o[0], 0, SCRATCH[o[0]][1][1]) if len(o) == 1 else (o[0], o[1], o[2])
 
     def vts(out, i, s1, o0, s2=None, o1=None):
@@ -186,111 +190,138 @@ def rank_program(g, core, T, topo):
         for (lo, hi), s in zip(MSG, "zb"):
             lands(slot("ZS", n + 1, lo, hi), "a%s%d" % (s, n))
 
-    dma("s", [], [("TLi", 0, 224)], ap(("TLi", 0, 224)), T.tk0[:], "d_tk")
-    dma("s", [], [("TLi", 224, 448)], ap(("TLi", 224, 448)), T.ln0[:], "d_ln")
+    dma("s", [], [("TLi", 0, 1)], T.TLi[0:8], T.tk0[:], "d_tk")
+    dma("s", [], [("TLi", 1, 2)], T.TLi[8:16], T.ln0[:], "d_ln")
     dma("s", [], [slot("ZS", 0)], ap(slot("ZS", 0)), T.y0[:], "d_y")
-    for i in range(7):
-        b = ("ilb", 512 * i, 512 * i + 512)
-        dma("y", [], [b], ap(b), T.il[:, 512 * i:512 * i + 512], "d_il%d" % i)
+    for i, (lo, hi) in enumerate(zip(LOAD, LOAD[1:])):
+        dma("y", [], [("ilb", lo, hi)], T.ilb[:, lo:hi], T.il[:, lo:hi], "d_il%d" % i)
     for i in range(2):
         b = ("XT", 1792 * i, 1792 * i + 1792)
         dma("y", [], [b], ap(b), T.xw[:, 1792 * i:1792 * i + 1792], "d_x%d" % i)
 
     def asel(out, i, pat, cmp, base, cm):
-        op("p", [i], [out], lambda q: q.affine_select(ap(out), ap(i), pat, cmp, 0.0, base, cm))
+        op("p", [i], [out], lambda q: q.affine_select(ap(out), i if i is None else ap(i), pat, cmp, 0.0, base, cm))
 
     def iota(out, pat, base, cm, **kw):
         op("p", [], [out], lambda q: q.iota(ap(out), pat, base, cm, **kw))
     fill(("ONE",), 1.0)
+    fill(mat("G8", 2), 1.0)
     iota(("MODi",), [[0, 4], [1, 32]], -1792, 0)
     asel(("ID",), ("ONE",), [[-1, 128]], A.is_equal, 0, 1)
-    asel(("G8",), ("ONE", 0, 128, "top"), [[1, 8], [0, 16]], A.is_equal, 0, -1)
+    for k in range(2):
+        asel(mat("G8", k), mat("G8", 2), [[1, 8], [0, 16]], A.is_equal, 8 * k, -1)
     asel(("BO0",), ("ONE",), [[-16, 8], [0, 16]], A.is_ge, 0, 1)
     asel(("BO",), ("BO0",), [[16, 8], [0, 16]], A.is_ge, 15, -1)
     for k, base in enumerate((0, 16, -1, 15)):
         asel(mat("P4", k), ("BO",), [[-16, 8], [-2, 16]], A.is_equal, base, 1)
     send(slot("YE", 0), slot("ZS", 0), "ay0")
+    iota(("trf",), [[1, NB]], NP, 0, allow_small_or_imprecise_dtypes=True)
     iota(("iw",), [[16, 14]], 0, 1)
     iota(("ip",), [[0, 14]], 0, 1)
-    iota(("trf",), [[1, NB]], NP, 0, allow_small_or_imprecise_dtypes=True)
+    iota(("BLK",), [[2048, 14], [0, 16]], 0, 0, allow_small_or_imprecise_dtypes=True)
+    iota(("THR",), [[32, 14]], 9, 0, allow_small_or_imprecise_dtypes=True)
     for k in range(2):
         asel(mat("BC", k), ("ONE",), [[-16, 8], [0, 16]], A.is_equal, -7 - 8 * k, 1)
     for m, k in (("SKD", 7), ("SKA", 0)):
-        for t in range(8):
-            asel(mat(m, t), ("BO",), [[-16, 8], [-8, 16]], A.is_equal, 16 * t - k, 1)
+        fill((m, 0, 16), 0.0)
+        asel((m, 16, 144), ("BO",), [[-16, 8], [-8, 16]], A.is_equal, -k, 1)
     fill(("RST",), 1.0)
+    fill(("tc",), -1.0)
     fill(("qt",), 0.25)
     fill(("zr",), 0.0)
-    fill(("RST", 0, 448, 16), 0.0)
+    fill(("RST", 0, NB, 16), 0.0)
+    fill(("tc", 0, 1, "top"), 2048.0)
     for k in range(4):
         vcp(("pW", 128 * k, 128 * k + 128), ("MODi",))
-    vts(("NID32",), ("ID",), -32.0, A.mult)
+    act(("MOD",), ("pW",), AF.Copy, bias=1792.0)
     vtt(("h64",), ("ID", 0, 64), ("ID", 64, 128), A.add)
-    fill(("MASK",), 256.0)
+    vts(("NID32",), ("ID",), -32.0, A.mult)
+    fill(("MASK", 0, 896), 256.0)
     vtt(("h32",), ("h64", 0, 32), ("h64", 32, 64), A.add)
-    fill(("MASK", 0, 1792, 8), 0.0)
+    fill(("MASK", 896, 1792), 256.0)
+    vtt(("rm",), ("h32", 0, 16), ("h32", 16, 32), A.add)
 
     def shift(i):
-        vtt(("f16t", 512 * i, 512 * i + 512), ("ilb", 512 * i, 512 * i + 512), ("pW",), A.add)
+        lo, hi = LOAD[i:i + 2]
+        vtt(("f16t", lo, hi), ("ilb", lo, hi), ("pW", 0, hi - lo), A.add)
 
     def table(i):
-        lo, hi = 512 * i, 512 * i + 512
+        lo, hi = LOAD[i:i + 2]
         vts(("KF", lo, hi), ("f16t", lo, hi), 1.0 / 32, A.mult, 184.515625, A.add)
-        pb = ("pA", "pB", "pZ")[i % 3]
-        mm((pb,), ("ID",), ("f16t", lo, hi), True, False)
-        mm((pb,), ("NID32",), ("KF", lo, hi), False, True)
-        act(("WT", lo, hi), (pb,), AF.Copy, bias=5920.0)
+        pb = (("pA", "pB", "pZ")[i % 3], 0, hi - lo)
+        mm(pb, ("ID",), ("f16t", lo, hi), True, False)
+        mm(pb, ("NID32",), ("KF", lo, hi), False, True)
+        act(("WT", lo, hi), pb, AF.Copy, bias=5920.0)
 
     def diagonal():
         for lo, hi in ((0, 16), (16, 32)):
             act(("DG", lo, hi), ("rm",), AF.Copy)
-        act(("BO8",), ("BO",), AF.Copy, scale=8192.0)
+        act(mat("G8", 1), mat("G8", 1), AF.Copy, scale=4096.0)
         act(("DG", 32, 64), ("DG", 0, 32), AF.Copy)
-        act(("BIG",), ("BO",), AF.Copy, scale=2.0 ** 32)
-        act(("DG", 64, 128), ("DG", 0, 64), AF.Copy)
         act(("NID",), ("ID",), AF.Copy, scale=-1.0)
+        act(("DG", 64, 128), ("DG", 0, 64), AF.Copy)
+        act(("BO8",), ("BO",), AF.Copy, scale=8192.0)
         act(("DG", 128, 224), ("DG", 0, 96), AF.Copy)
-        act(("P32", 0, 256), ("P4", 0, 256), AF.Copy, scale=32.0)
-        act(("NE2",), ("DG",), AF.Copy, scale=65536.0 + 2.0 ** 20, bias=-2.0 ** 20)
+        act(("BIG",), ("BO",), AF.Copy, scale=2.0 ** 32)
+        act(("NEG",), ("DG",), AF.Copy, scale=2.0 ** 23, bias=-2.0 ** 23)
 
     def spread():
-        for h in range(2):
-            mm(("pE", 224 * h, 224 * h + 224), ("ID",), ("NE2",), h == 0, False)
-        mm(("pE", 0, 448), ("G8",), ("TLh",), False, True)
-    lin = ("LB", 1, 28, 2)
+        mm(("pE", 0, NB), ("ID",), ("NEG",), True, False)
+        for k in range(2):
+            mm(("pE", 0, NB), mat("G8", k), ("TLh",), False, k == 1)
     between = [
-        [lambda: vtt(("rm",), ("h32", 0, 16), ("h32", 16, 32), A.add), lambda: vts(("TLh",), ("TLi",), -2048.0, A.add),
-         diagonal],
-        [lambda: scan(("th16",), ("qt",), ("zr",), A.mult, A.add, 2.0 ** 33),
-         lambda: fill(("sd",), 0.0), lambda: fill(("A1",), 1.0), lambda: fill(slot("ZO", 0, -14, 0), 129.0)],
-        [spread, lambda: vtt(("rq",), ("rm",), ("th16",), A.mult),
+        [diagonal, lambda: vts(("TLh",), ("TLi",), ("tc",), A.subtract)],
+        [lambda: act(("P32", 0, 256), ("P4", 0, 256), AF.Copy, scale=32.0)],
+        [spread],
+        [lambda: scan(("PK",), ("RST",), ("pE", 0, NB), A.mult, A.max)],
+        [lambda: vts(("q",), ("PK", 15, NB, 16), -2048.0, A.add),
          lambda: act(("P32", 256, 512), ("P4", 256, 512), AF.Copy, scale=32.0)],
-        [lambda: scan(("PK",), ("RST",), ("pE", 0, 448), A.mult, A.max), lambda: vts(("ipq",), ("ip",), 112, A.bitwise_and),
-         lambda: op("v", [("rq",)], [("wq1",)], lambda q: q.tensor_reduce(T.wq1[:], T.rq[:], AxisListType.X, A.add))],
-        [lambda: vts(("q",), ("PK", 15, 224, 16), -63488.0, A.add),
-         lambda: vts(lin, ("PK", 239, 448, 16), -63488.0, A.add, 32.0, A.mult),
-         lambda: vtt(("iw",), ("iw",), ("ipq",), A.subtract)],
-        [lambda: vts(("c2", 0, 14), ("q",), 31, A.bitwise_and), lambda: vts(("hi0",), ("q",), 4064, A.bitwise_and),
-         lambda: vts(("wq2",), ("wq1",), -1.0, A.mult, -1.0, A.add)],
-        [lambda: vtt(("ao", 0, 14), ("c2", 0, 14), lin, A.add), lambda: vcp(slot("ZO", 0, -28, -14), ("c2", 0, 14)),
-         lambda: vts(("LB", 29, 56, 2), ("iw",), 16.0, A.mult)],
+        [lambda: vts(("c2",), ("q",), 31, A.bitwise_and),
+         lambda: vts(("t1",), ("q",), 7, A.arith_shift_right, 4064, A.bitwise_and)],
+        [lambda: vtt(("ao",), ("c2",), ("t1",), A.add)],
+        [lambda: vcp(("AO", 14, 28), ("ao",))],
     ]
-    for i in range(7):
+    for i in range(8):
         shift(i)
         if i:
             table(i - 1)
         for f in between[i]:
             f()
-    table(6)
-    vcp(("AO", 0, 14), ("ao", 0, 14))
+    table(7)
 
-    def weights():
-        act(("WQ",), ("BO",), AF.Copy, scale=("wq1",))
-        act(("NTH",), ("DG",), AF.Copy, scale=("wq2",), bias=1.0)
-        act(("NEG",), ("DG",), AF.Copy, scale=2.0 ** 20, bias=-2.0 ** 20)
-        act(("MOD",), ("pW",), AF.Copy, bias=1792.0)
+    def weights(k):
+        if k == 0:
+            scan(("th16",), ("qt",), ("zr",), A.mult, A.add, 2.0 ** 33)
+            fill(("MASK", 0, 1792, 8), 0.0)
+            vts(("ipq",), ("ip",), 112, A.bitwise_and)
+            vcp(slot("ZO", 0, -28, -14), ("c2",))
+            vtt(("rq",), ("rm",), ("th16",), A.mult)
+            vts(("hi0",), ("q",), 4064, A.bitwise_and)
+            fill(slot("ZO", 0, -14, 0), 129.0)
+            vtt(("iw",), ("iw",), ("ipq",), A.subtract)
+            op("v", [("rq",)], [("wq1",)], lambda q: q.tensor_reduce(T.wq1[:], T.rq[:], AxisListType.X, A.add))
+            fill(("A1",), 1.0)
+            fill(("B",), 0.0)
+            vts(("sa", 1, 70, 5), ("iw",), -16.0, A.mult)
+            vts(("wq2",), ("wq1",), -1.0, A.mult, -1.0, A.add)
+        elif k == 1:
+            for o, c in ((("sd", 0, 140, 5), 0.0), (("sd", 1, 70, 5), 0.0), (("sd", 2, 140, 5), 1.0),
+                         (("sd", 3, 140, 5), -1.0), (("sd", 4, 140, 5), 1.0), (("sa", 0, 70, 5), 0.0),
+                         (("sa", 3, 70, 5), M32 / 2), (("sa", 73, 140, 5), M32)):
+                fill(o, c)
+        else:
+            act(("WQ",), ("BO",), AF.Copy, scale=("wq1",))
+            act(("NTH",), ("DG",), AF.Copy, scale=("wq2",), bias=1.0)
+            act(("THR",), ("THR",), AF.Copy, scale=8192.0)
+            act(("ONF",), ("ONE",), AF.Copy)
+            for r in range(16):
+                act(("trm", r, NB, 16), ("trf", r, NB, 16), AF.Copy, scale=("rm", r, r + 1))
 
     SUM, NEW = ("pE", "pL"), ("pD", "pA")
+
+    def opened(p):
+        mm((SUM[p],) + ARR[p], ("ID",), ("NEG",) + ARR[p], True, False)
+        mm((SUM[p],) + ARR[p], ("ONE",), ("BLK",) + ARR[p], False, False)
 
     def reach(n, p):
         lo, hi = ARR[p]
@@ -310,15 +341,14 @@ def rank_program(g, core, T, topo):
         act(("NW", lo, hi), b, AF.Copy, bias=-64.0)
         act(("NK", lo, hi), ("KD", lo, hi), AF.Copy, scale=-32.0, bias=6208.0)
 
-    def rewrite(k):
-        lo, hi = NEWS[k]
+    def rewrite(lo, hi):
         off = ("OFF", lo // 16, hi // 16)
         op("v", [("NW", lo, hi), ("NK", lo, hi), off], [("WT",)],
            lambda q: q.tensor_tensor(T.WT[:].indirect(ap(off)), T.NW[:, lo:hi], T.NK[:, lo:hi], A.add))
 
     def pick(p):
         lo, hi = ARR[p]
-        scan(("PK", lo, hi), ("RST", lo, hi), (SUM[p], lo, hi), A.mult, A.max)
+        scan(("PK", lo, hi), (SUM[p], lo, hi), ("B", lo, hi), A.max, A.add)
 
     def losers(h):
         lo, hi = HALF[h][1:]
@@ -328,53 +358,49 @@ def rank_program(g, core, T, topo):
         reach(n, 1)
         renew(n, 1)
         sums(n, 1)
-        losers(0)
         losers(1)
-        pick(0)
         vtt(("o2",), ("SC", 15, NB, 16), ("DW",), A.max)
+        pick(0)
         pick(1)
         vcp(("OFF", 0, 14), ("o2",))
         pk = ("PK", 15, NB, 16)
-        vts(("sa", 0, 28, 2), pk, 9.0 * 8192, A.is_ge)
-        vtt(("q",), pk, ("B",), A.add)
-        rewrite(0)
-        scan(("LB", 0, 28), ("sd", 0, 28), ("sa", 0, 28), A.mult, A.add, also=[("sa", 1, 28)])
-        vts(("c2", 0, 14), ("q",), 31, A.bitwise_and)
+        vtt(("sa", 70, 140, 5), pk, ("THR",), A.is_ge)
+        vts(("sa", 72, 140, 5), pk, -15.5, A.add, M32, A.add)
+        act(("sa", 74, 140, 5), pk, AF.Copy)
         if n < ST:
-            vts(("c2", 14, 28), ("q",), 15, A.bitwise_and)
-        rewrite(1)
+            vts(("sa", 2, 70, 5), pk, -7.5, A.add, M32 / 2, A.add)
+            act(("sa", 4, 70, 5), pk, AF.Copy)
+            rewrite(*NEWS[0])
+        else:
+            rewrite(0, NB)
+        lo = 0 if n < ST else 70
+        scan(("LB", lo, 140), ("sd", lo, 140), ("sa", lo, 140), A.mult, A.add,
+             also=[(b, k + lo, 140) for b in ("sa", "sd") for k in range(1, 5)])
         if n < ST:
-            vtt(("ao",), ("c2",), ("LB", 1, 56, 2), A.add)
-        rewrite(2)
-        if n < ST:
-            vcp(("AO",), ("ao",))
+            rewrite(*NEWS[1])
+            vcp(("AO",), ("LB", 4, 140, 5))
 
     def carry(n, k):
         if k == 0:
-            vcp(slot("ZO", n, -28, -14), ("c2", 0, 14))
+            vtt(slot("ZO", n, -28, -14), ("LB", 74, 140, 5), ("LB", 71, 140, 5), A.add)
+        elif k == 1:
             mm(("pW", 64, 78), ("NID32",), slot("ZS", n, -14, 0), True, False)
-            mm(("pW", 64, 78), ("NID",), ("B",), False, False)
+            mm(("pW", 64, 78), ("NID",), ("B", 15, NB, 16), False, False)
             mm(("pW", 64, 78), ("ID",), slot("ZO", n, -28, -14), False, True)
             if n < ST:
-                mm(("pW", 80, 94), ("ONE",), ("sa", 0, 28, 2), True, True)
+                mm(("pW", 80, 94), ("ONF",), ("sa", 70, 140, 5), True, True)
         else:
             act(slot("ZO", n, -14, 0), ("pW", 64, 78), AF.Copy, scale=-1.0 / 32, bias=0.484375)
             if n < ST:
                 act(("Aj",), ("pW", 80, 94), AF.Copy, accum_out=("Ar",))
 
-    def lines(f):
-        lo, hi, b = FET[f]
-        off = ("AO", lo // 16, hi // 16)
-        op("v", [("ilb",), off], [("LG", lo, hi)],
-           lambda q: q.tensor_scalar(T.LG[:, lo:hi], T.ilb[:].indirect(ap(off)), 1.0 / 32, 128.515625, A.mult, A.add))
-
-    def lows(f):
-        lo, hi, b = FET[f]
-        act(("WA", lo, hi), ("WT", 0, NP), AF.Copy, ("AO", lo // 16, hi // 16))
-
-    def lists(f):
+    def fetch(f):
         lo, hi, b = FET[f]
         w = (hi - lo) // 2
+        off = ("AO", 14 + lo // 16, 14 + hi // 16)
+        op("v", [("ilb",), off], [("LG", lo, hi)],
+           lambda q: q.tensor_scalar(T.LG[:, lo:hi], T.ilb[:].indirect(ap(off)), 1.0 / 32, 128.515625, A.mult, A.add))
+        act(("WA", lo, hi), ("WT", 0, NP), AF.Copy, off)
         for src, m in (("LG", "P32"), ("WA", "P4")):
             for k in range(4):
                 mm((b, w * (k // 2), w * (k // 2 + 1)), mat(m, k), (src, lo + k % 2, hi, 2),
@@ -388,7 +414,12 @@ def rank_program(g, core, T, topo):
 
     def even(i):
         a, b = CH[i]
-        act(("VE", 16 * a, 16 * b), ("XT",), AF.Copy, ("EO", a, b, 0))
+        off = ("EO", a, b, 0)
+        if i:
+            act(("VE", 16 * a, 16 * b), ("XT",), AF.Copy, off)
+        else:
+            op("v", [("XT",), off], [("VE", 16 * a, 16 * b)],
+               lambda q: q.tensor_copy(T.VE[:, 16 * a:16 * b], T.XT[:].indirect(ap(off))))
 
     def least(i):
         a, b = CH[i]
@@ -410,22 +441,22 @@ def rank_program(g, core, T, topo):
         if n:
             late(n)
             send(slot("YE", n), z, "ay%d" % n)
-        for f in range(2):
-            lines(f)
-            lows(f)
-            lists(f)
+        fetch(0)
+        fetch(1)
         if n:
-            op("v", [z, ("AO", 14, 28)], [("XT",)], lambda q: q.tensor_copy(T.XT[:].indirect(T.AO[:, 14:28]), ap(z)))
+            op("v", [z, ("AO", 0, 14)], [("XT",)], lambda q: q.tensor_copy(T.XT[:].indirect(T.AO[:, 0:14]), ap(z)))
         else:
-            vtt(("trm", 0, NB), ("trf",), ("DG",), A.mult)
+            weights(0)
         offsets(0)
         if n:
             carry(n, 0)
-        offsets(1)
-        for p in range(2):
-            mm((ZB[p],) + ARR[p], ("NID",), slot("ZS", n, *ARR[p]), True, False)
         even(0)
         even(1)
+        offsets(1)
+        if n:
+            carry(n, 1)
+        for p in range(2):
+            mm((ZB[p],) + ARR[p], ("NID",), slot("ZS", n, *ARR[p]), True, False)
         least(0)
         vts(slot("EF", n), ("EO", 0, 112), -1792.0, A.add)
         send(slot("EL", n), slot("EF", n), "ae%d" % n)
@@ -434,36 +465,38 @@ def rank_program(g, core, T, topo):
         for i in range(2, len(CH)):
             even(i)
         if n == 0:
-            weights()
-        mm((SUM[0],) + ARR[0], ("ID",), ("NEG",) + ARR[0], True, False)
-        mm(HALF[1], ("ID",), ("NTH",) + HALF[1][1:], True, False)
+            weights(2)
+        opened(0)
+        for h in HALF:
+            mm(h, ("ID",), ("NTH",) + h[1:], True, False)
         if n:
-            carry(n, 1)
+            carry(n, 2)
             act(("KA",), ("Ar",), AF.Copy, scale=1.0 / 32, bias=191.515625)
         for i in range(2, len(CH)):
             least(i)
-            if 2 * CH[i - 1][1] == EARLY:
-                ahead(n)
-            greatest(i - 1)
-            if 2 * CH[i - 1][1] == EARLY:
+            if 2 * CH[i - 1][1] != EARLY:
+                greatest(i - 1)
+            if 2 * CH[i][1] == EARLY:
+                greatest(i)
                 out_z(n, 0)
+                ahead(n)
                 if n:
                     act(("Au",), ("KA",), AF.Copy, scale=-32.0, bias=6145.0)
-                act(("sa", 1, 56, 2), ("LL",), AF.Copy, scale=32.0, bias=-4128.0)
+                act(("sa", 71, 210, 5), ("LL",), AF.Copy, scale=-32.0, bias=4128.0)
         vts(("DR",), ("pD", 0, 224), 1792.0, A.add)
         greatest(len(CH) - 1)
         out_z(n, 1)
         mm(("pZ", 0, NB), ("ID",), slot("YE", n), True, True)
-        mm(HALF[0], ("ID",), ("NTH",) + HALF[0][1:], True, False)
+        opened(1)
 
     def ahead(n):
         el = NB * n
         for k in range(2):
             mm(("pD", k, 224, 2), mat("BC", k), ("EL", el + 112, el + 224), True, True)
         for t in range(8):
-            mm(("pW", 32, 46), mat("SKD", t), ("EL", el + 112 + t, el + 224, 8), t == 0, t == 7)
+            mm(("pW", 32, 46), ("SKD", 16 - 2 * t, 144 - 2 * t), ("EL", el + 112 + t, el + 224, 8), t == 0, t == 7)
         for t in range(8):
-            mm(("pL", 0, 28), mat("SKA", t), ("EL", el + t, el + 224, 8), t == 0, t == 7)
+            mm(("pL", 0, 28), ("SKA", 16 - 2 * t, 144 - 2 * t), ("EL", el + t, el + 224, 8), t == 0, t == 7)
         act(("DW",), ("pW", 32, 46), AF.Copy, bias=1792.0)
         act(("LL",), ("pL", 0, 28), AF.Copy, scale=1.0 / 32, bias=184.515625)
 
@@ -484,9 +517,11 @@ def rank_program(g, core, T, topo):
                 h = c // 7
                 mm(HALF[h], ("WQ",), ("EQ", 7 * 240 * h, 7 * 240 * (h + 1), 1), False, True)
                 act(("LF",) + HALF[h][1:], HALF[h], AF.Sign)
-        mm((SUM[1],) + ARR[1], ("ID",), ("NEG",) + ARR[1], True, False)
-        act(("B",), slot("ZS", n + 1, -28, -14), AF.Identity, bias=("A1",))
-        vtt(("sd", 1, 28, 2), ("sa", 29, 56, 2), ("sa", 1, 28, 2), A.subtract)
+        act(("B", 15, NB, 16), slot("ZS", n + 1, -28, -14), AF.Identity, bias=("A1",))
+        if n == 0:
+            weights(1)
+        vtt(("sd", 71, 140, 5), ("sa", 141, 210, 5), ("sa", 71, 140, 5), A.subtract)
+        losers(0)
         reach(n + 1, 0)
         renew(n + 1, 0)
         sums(n + 1, 0)
@@ -495,7 +530,7 @@ def rank_program(g, core, T, topo):
         step(n)
         ready(n)
 
-    FIN = ("pB", "pY", "pA", "pZ", "pL", "pD", "pB")
+    FIN = ("pY", "pB", "pZ", "pD", "pL", "pA", "pY")
 
     def reduced(i, k):
         if not 0 <= i < 7:
@@ -510,38 +545,48 @@ def rank_program(g, core, T, topo):
             vtt(("KF", lo, hi), ("WT", lo, hi), ("pE",), A.is_ge)
         else:
             mm(b, ("NID32",), ("KF", lo, hi), False, True)
-            act(("YW", lo, hi), b, AF.Copy, bias=32.0)
+            if i < 6:
+                act(("YW", lo, hi), b, AF.Copy, bias=32.0)
+            else:
+                vts(("YW", lo, hi), b, 32.0, A.add)
             dma("y", [("YW", lo, hi)], [], T.yw[:, lo:hi], T.YW[:, lo:hi], "d_o%d" % (1 + i))
 
     def rows():
         for r in range(16):
             mm(("pW", r, 448, 16, "top"), ("ID", r, 128, 16), ("fo",), True, True)
-    clock = [lambda: vtt(("t1",), ("hi0",), ("c2", 0, 14), A.add),
-             lambda: vts(("t2",), slot("ZO", ST, -14, 0), 32.0, A.mult, -4128.0, A.add),
-             lambda: vtt(("t3",), ("t1",), ("t2",), A.add),
-             lambda: vts(("q",), ("t3",), 4095, A.bitwise_and),
-             lambda: vts(("fo", 0, 14), ("q",), -2048.0, A.add),
-             rows,
-             lambda: vts(("fr", 0, 224), ("pW", 0, 224, "top"), 2048.0, A.add)]
+
+    def last():
+        act(("fr", 0, 224), ("pW", 0, 224, "top"), AF.Copy, bias=2048.0)
+        act(("fr", 224, 448), ("pW", 224, 448, "top"), AF.Copy, scale=1.0 / 32)
+        dma("s", [("fr", 0, 224)], [], T.yt[:], ap(("fr", 0, 224)), "d_t")
+        dma("s", [("fr", 224, 448)], [], T.yl[:], ap(("fr", 224, 448)), "d_l")
+    clock = [[lambda: vtt(("t1",), ("hi0",), slot("ZO", ST, -28, -14), A.add)],
+             [lambda: vts(("t2",), slot("ZO", ST, -14, 0), 32.0, A.mult, -4128.0, A.add)],
+             [lambda: vtt(("t3",), ("t1",), ("t2",), A.add)],
+             [lambda: vts(("q",), ("t3",), 4095, A.bitwise_and)],
+             [lambda: vts(("fo", 0, 14), ("q",), -2048.0, A.add), rows],
+             [last], []]
 
     dma("y", [slot("ZS", ST)], [], T.yy[:], ap(slot("ZS", ST)), "d_o0")
     late(ST)
     mm(("pE",), ("ID",), ("MOD",), True, True)
-    for i in range(3):
+    for i in range(6):
         reduced(i, 0)
+    reduced(0, 2)
     carry(ST, 0)
-    vcp(("fo", 14, 28), ("LB", 1, 28, 2))
-    carry(ST, 1)
+    vts(("fo", 14, 28), ("LB", 71, 140, 5), -1.0, A.mult)
     reduced(0, 1)
     for i in range(7):
-        reduced(i, 2)
+        reduced(i + 1, 2)
         reduced(i, 3)
-        reduced(i + 3, 0)
+        if i == 0:
+            carry(ST, 1)
+            carry(ST, 2)
+        if i == 3:
+            reduced(6, 0)
         reduced(i + 1, 1)
-        clock[i]()
-    vts(("fr", 224, 448), ("pW", 224, 448, "top"), 1.0 / 32, A.mult)
-    dma("s", [("fr", 0, 224)], [], T.yt[:], ap(("fr", 0, 224)), "d_t")
-    dma("s", [("fr", 224, 448)], [], T.yl[:], ap(("fr", 224, 448)), "d_l")
+        for f in clock[i]:
+            f()
     for s in SEMAPHORES:
         if count[s] and known["p"].get(s, 0) < count[s]:
             g.wait_ge(T.sem[s], count[s])

@@ -1,16 +1,51 @@
+from concourse.bass import DstId, RemoteDMATransfer
 from concourse.mybir import AluOpType as A, AxisListType, ActivationFunctionType as AF
 
 NP, NB, NR, ST = 3584, 224, 4, 8
-EARLY = 160
-CUT = 64
-CH = [(0, 10), (10, 32), (32, 54), (54, 80), (80, 98), (98, 112)]
-ARR = ((0, EARLY), (EARLY, NB))
-MSG = ((-28, EARLY), (EARLY, NB))
-FET = ((0, CUT, "pA"), (CUT, NB, "pB"))
-HALF = (("pA", 0, 112), ("pB", 112, 224))
-NEWS = ((0, 128), (128, 224))
+LATE = 96
+EDGE = (112, 102, 80, 64, 48, 20, 0)
+CH = [(b, a) for a, b in zip(EDGE, EDGE[1:])]
+ARR = ((LATE, NB), (0, LATE))
+MSG = ((LATE, NB + 28), (0, LATE))
+NL = LATE // 16
+SLOT = ((2 * NL, 28), (0, 2 * NL))
+WORD = ((14 + NL, 28), (0, NL))
+HALF = (("pB",) + ARR[0], ("pW",) + ARR[1])
 LOAD = [512 * i for i in range(7)] + [3392, NP]
-M32 = 1.5 * 2.0 ** 28
+ONV = ()
+BYV = (6,)
+M32, M16 = 2.0 ** 28, 2.0 ** 27
+
+STEP = {
+    "v": """sum1+ skip0+ target1+ rewrite0+ pick1+ place0+ target1b+ skip1+ place0b+ rewrite1+ place1+ first0 words0+
+         place1b+ first1 carry words1+ lists0 even0 lists1 least0 send least3 most0 least2 least1 most2 most3 most1
+         least4 least5 most4 most5 rows spares d alike3 alike3b alike4 alike4b alike5 alike5b alike6 alike6b alike0
+         alike2 alike0b alike1 alike2b alike1b sum0 next lost0 target0 pick0 lost1 target0b""",
+    "s": """lost1+ whole0+ off0+ floor0+ sums0+ sumw0+ half0+ renew1+ whole1+ off1+ half1+ sums1+ sumw1+ floor1+ lines0
+         fetch0 skips lines1 fetch1 A even3 Ab even2 Ac even1 carry even4 even5 table tableb most3 tablec wrapped
+         tabled most5 old both lost0 B renew0 next""",
+    "t": """alike2+ lost1+ sum0+ sum0b+ open1+ renew1b+ sum1+ sum1b+ less skips fetch0 fetch0b fetch1 fetch1b carry
+         table most0 most1 most2 most3 rows wrapped most4 y most5 open0 alone both alike3 alike4 alike5 alike6 lost0
+         renew1 renew0 renew0b alike0 alike1""",
+    "p": "send most3 most5",
+}
+LAST = {
+    "v": """sum1+ skip0+ target1+ rewrite0+ pick1+ place0+ target1b+ skip1+ place0b+ rewrite1+ place1+ words0+ place1b+
+         words1+ lists0 carry even0 lists1 least0 send least3 most0 least2 least1 most3 most2 most1 least4 least5 rows
+         most4 most5 alike3b alike4 alike4b alike3 alike5 alike6 alike5b alike6b alike1b alike2b d alike0b alike0
+         alike1 alike2 lost0 sum0 target0 lost1 target0b target1 rewrite0 target1b pick0 sum1 rewrite1 skip0 next
+         turn0 pick1 turn1 skip1 turn2 place0 place1 turn3 final turn4 clockb turn5 clockc turn6 clockd clocke clock
+         clockf turn6b""",
+    "s": """lost1+ whole0+ off0+ sumw0+ floor0+ sums0+ renew1+ half0+ whole1+ off1+ sumw1+ sums1+ half1+ floor1+ lines0
+         fetch0 skips lines1 fetch1 even3 even2 even1 even4 even5 A carry most3 Ab wrapped Ac most5 both lost0 lost1
+         old mod B sums1 floor0 floor1 sums0 next turn0b turn1b turn2b final turn3b turn4b turn5b clock clockb clockc
+         clockd""",
+    "t": """alike2+ lost1+ sum0+ sum0b+ renew1b+ open1+ sum1+ open0 sum1b+ skips fetch0 fetch0b fetch1 fetch1b less most0
+         most1 most2 alone most3 carry rows wrapped most4 y most5 both alike3 alike4 alike5 alike6 lost0 alike0 alike1
+         alike2 lost1 less2 sum0 sum0b open1 less0 less3 less4 sum1 sum1b turn0 less1 turn0b turn1 turn2 turn1b turn3
+         turn2b less5 turn4 final turn3b turn4b less6 turn5 turn6 turn5b turn6b clock""",
+    "p": "send most3 most5",
+}
 
 
 def _sb(dtype, **widths):
@@ -19,28 +54,510 @@ def _sb(dtype, **widths):
 
 SCRATCH = {
     **_sb("int32", ilb=NP, TLi=NB, MODi=128, iw=14, ip=14, ipq=14, q=14, c2=14, ao=14, hi0=14, t1=14, t2=14, t3=14),
-    **_sb("float16", f16t=NP, TLh=NB, EF=8 * NB, EL=8 * NB, fo=28),
+    **_sb("float16", f16t=NP, TLh=NB, fo=28, EF=8 * NB, EL=8 * NB),
     **_sb("uint16", DR=NB, DWu=16, OFF=16, AO=28),
-    **_sb("float32", h64=64, h32=32, rm=16, rq=16, qt=16, zr=16, wq1=1, wq2=1, th16=16, DG=NB, trf=NB, PK=NB, tc=1,
-          trm=NB, SC=NB, DW=14, o2=14, LB=140, sd=140, sa=210, THR=14, ONF=128, Ar=1, Au=1, A1=1, Aj=14, fr=2 * NB),
-    **_sb("bfloat16", XT=NP, WT=NP + NB, YW=NP, KF=NP, ONE=128, BO0=128, BO=128, BO8=128, G8=384, MOD=512, BLK=NB,
-          ID=128, NID=128, NID32=128, P4=512, P32=512, BC=256, SKA=144, SKD=144, WQ=128, BIG=128, NEG=NB,
-          NTH=NB, RST=NB, ZS=9 * 256, ZO=9 * 256, YE=8 * NB, SG=NB, LF=NB, KA=1, DO=NB,
-          KD=NB, NW=NB, NK=NB, B=NB, LL=28, WA=NB, LG=NB, VE=1792, MASK=1792, U=1792, M=1792),
+    **_sb("float32", h64=64, h32=32, rm=16, DG=NB, PK=NB, tc=1, o2=14, DW=14, rq=16, qt=16, zr=16, wq1=1, wq2=1,
+          th16=16, trf=NB, trm=NB, SC=NB, LB=140, sd=140, sa=140, THR=14, ONF=128, Ar=1, Au=1, A1=1, Aj=14, fr=2 * NB),
+    **_sb("bfloat16", XT=NP, LT=NP, WT=NP + NB, YW=NP, KF=NP, ONE=128, BO0=128, BO=128, BO8=128, G8=384, MOD=512,
+          BLK=NB,
+          ID=128, NID=128, NID32=128, P4=512, BC=256, SKA=144, SKD=144, WQ=128, BIG=128, NTH=NB, LF=NB, LL=28,
+          NEG=NB, RST=NB, ZS=9 * 256, ZO=9 * 256, YE=8 * 256, SG=NB, KA=1, DO=NB, KD=NB, NW=NB, NK=NB, B=NB,
+          LW=2 * NB, VE=1792, MASK=1792, U=1792, M=1792),
     "EQ": ("sbuf", [128, 14, 240], "bfloat16"),
     "EO": ("sbuf", [128, 2, 112], "uint16"),
     **{n: ("psum", [128, 512], "float32") for n in ("pA", "pB", "pZ", "pY", "pD", "pW", "pE", "pL")},
 }
 SEMAPHORES = (["cv", "ct", "cs", "cp", "loc", "d_tk", "d_ln", "d_y", "d_x0", "d_x1", "d_t", "d_l"]
               + ["d_il%d" % i for i in range(8)] + ["d_o%d" % i for i in range(8)]
-              + ["a%s%d" % (k, n) for k in "zbye" for n in range(ST)])
+              + ["a%s%d" % (k, n) for k in "zbeyx" for n in range(ST)])
 TOP = {"TLi": 16, "TLh": 16, "G8": 16, "tc": 16, "fr": 8}
+
+
+def bank(name):
+    return name[0] == "p" and name[1:2].isupper()
 
 
 def rank_program(g, core, T, topo):
     rank = T.rank_of(core)
     if rank is None:
         return
+    calls, now = [], [-1, ""]
+
+    def tag(*name):
+        now[1] = "".join(str(x) for x in name)
+
+    def ap(o):
+        if o[0] == "EQ":
+            c, a = divmod(o[1], 240)
+            return T.EQ[:, c, a:a + o[2] - o[1]] if len(o) == 3 else T.EQ[:, c:o[2] // 240, 0:16]
+        if o[0] == "EO":
+            return T.EO[:, o[3], o[1]:o[2]] if len(o) == 4 else T.EO[:, :, o[1]:o[2]]
+        rows = slice(0, 8) if o[-1] == "top" else slice(0, TOP[o[0]]) if o[0] in TOP else slice(None)
+        o = o[:-1] if o[-1] == "top" else o
+        if len(o) == 1:
+            return T[o[0]][rows]
+        if len(o) == 4:
+            return T[o[0]][rows, o[1]:o[2]:o[3]]
+        return T[o[0]][rows, o[1]:o[2]]
+
+    def rg(o):
+        if o[0] in ("sa", "sd"):
+            return ("%s%d" % (o[0], o[1] % 5), o[1], o[2])
+        return (o[0], 0, SCRATCH[o[0]][1][1]) if len(o) == 1 else (o[0], o[1], o[2])
+
+    def op(e, rd, wr, fn, sem=None, **more):
+        acc = [rg(o) + (False,) for o in rd if o] + [rg(o) + (True,) for o in wr]
+        calls.append(dict(e=e, acc=acc, fn=fn, sem=sem, step=now[0], name=now[1], **more))
+
+    def dma(e, rd, wr, out, in_, s):
+        op(e, rd, wr, lambda q: q.dma_start(out, in_), s)
+
+    def by(o, off):
+        return ap(o).indirect(ap(off)) if off else ap(o)
+
+    def vts(out, i, s1, o0, s2=None, o1=None, off=None):
+        rd = [i, off] + [s for s in (s1, s2) if isinstance(s, tuple)]
+        s1, s2 = [ap(s) if isinstance(s, tuple) else s for s in (s1, s2)]
+        more = () if o1 is None else (o1,)
+        op("v", rd, [out], lambda q: q.tensor_scalar(ap(out), by(i, off), s1, s2, o0, *more))
+
+    def vtt(out, a, b, o, off=None, into=None):
+        op("v", [a, b, off, into], [out], lambda q: q.tensor_tensor(by(out, into), by(a, off), ap(b), o))
+
+    def vcp(out, i, off=None, into=None):
+        op("v", [i, off, into], [out], lambda q: q.tensor_copy(by(out, into), by(i, off)))
+
+    def scan(out, a, b, o0, o1, also=(), init=0.0):
+        op("v", [a, b] + list(also), [out], lambda q: q.tensor_tensor_scan(ap(out), ap(a), ap(b), init, o0, o1))
+
+    def fill(out, c):
+        op("v", [], [out], lambda q: q.memset(ap(out), c))
+
+    def act(out, i, f, off=None, **kw):
+        cols = {k: v for k, v in kw.items() if isinstance(v, tuple)}
+        kw.update({k: ap(v) for k, v in cols.items()})
+        op("s", [i, off] + [v for k, v in cols.items() if k != "accum_out"],
+           [out] + [v for k, v in cols.items() if k == "accum_out"],
+           lambda q: q.activation(ap(out), by(i, off), f, **kw))
+
+    def lin(out, i, scale=1.0, bias=0.0):
+        if now[1] in ONV:
+            vts(out, i, scale, A.mult, bias, A.add)
+        else:
+            act(out, i, AF.Copy, scale=scale, bias=bias)
+
+    def mm(out, l, r, start, stop):
+        op("t", [l, r], [out], lambda q: q.matmul(ap(out), ap(l), ap(r), start, stop))
+
+    def mat(n, r):
+        return (n, 128 * r, 128 * r + 128)
+
+    def ahead(a, k):
+        return T.cores[(T.rank_of(a) + k) % NR]
+
+    def engines(a, k):
+        return [e for e in topo.engines(a, ahead(a, k)) if k == 1 or e not in topo.engines(a, ahead(a, 1))]
+
+    def send(src, *ways):
+        def transfer(k, dst, s):
+            rid, pid = topo.addr(ahead(core, k))[:2]
+            return RemoteDMATransfer(dst_ids=[DstId(rid=rid, pnc=pid)], remote_sem=T.sem[s], src=ap(src), dst=ap(dst),
+                                     dma_engine_mask=sum(1 << e for e in engines(core, k)))
+        op("p", [src], [], lambda q: q.remote_dma_fused([transfer(k + 1, *w) for k, w in enumerate(ways)],
+                                                        local_sem=T.sem["loc"]),
+           ways[0][1], out=sum(len(engines(core, k + 1)) for k in range(len(ways))))
+        for k, (dst, s) in enumerate(ways):
+            op("ro"[k], [], [dst], None, s, n=len(engines(ahead(core, -k - 1), k + 1)), by=ways[0][1])
+
+    def slot(b, n, lo=0, hi=NB):
+        o = {"EF": NB, "EL": NB}.get(b, 256) * n
+        return (b, o + lo, o + hi)
+
+    def five(b, lo, hi, k):
+        return (b, 5 * lo + k, 5 * hi, 5)
+
+    T32, CAR = (NB, NB + 14), (NB + 14, NB + 28)
+
+    dma("s", [], [("TLi", 0, 1)], T.TLi[0:8], T.tk0[:], "d_tk")
+    dma("s", [], [("TLi", 1, 2)], T.TLi[8:16], T.ln0[:], "d_ln")
+    dma("s", [], [slot("ZS", 0)], ap(slot("ZS", 0)), T.y0[:], "d_y")
+    for i, (lo, hi) in enumerate(zip(LOAD, LOAD[1:])):
+        dma("y", [], [("ilb", lo, hi)], T.ilb[:, lo:hi], T.il[:, lo:hi], "d_il%d" % i)
+    for i in range(2):
+        b = ("XT", 1792 * i, 1792 * i + 1792)
+        dma("y", [], [b], ap(b), T.xw[:, 1792 * i:1792 * i + 1792], "d_x%d" % i)
+
+    def asel(out, i, pat, cmp, base, cm):
+        op("p", [i], [out], lambda q: q.affine_select(ap(out), ap(i), pat, cmp, 0.0, base, cm))
+
+    def iota(out, pat, base, cm):
+        kw = {} if SCRATCH[out[0]][2] == "int32" else {"allow_small_or_imprecise_dtypes": True}
+        op("p", [], [out], lambda q: q.iota(ap(out), pat, base, cm, **kw))
+    for o, c in ((("ONE",), 1.0), (mat("G8", 2), 1.0), (("RST",), 1.0), (("tc",), -1.0), (("B",), 0.0),
+                 (("RST", 0, NB, 16), 0.0), (("tc", 0, 1, "top"), 2048.0)):
+        fill(o, c)
+    iota(("MODi",), [[0, 4], [1, 32]], -1792, 0)
+    asel(("ID",), ("ONE",), [[-1, 128]], A.is_equal, 0, 1)
+    for k in range(2):
+        asel(mat("G8", k), mat("G8", 2), [[1, 8], [0, 16]], A.is_equal, 8 * k, -1)
+    asel(("BO0",), ("ONE",), [[-16, 8], [0, 16]], A.is_ge, 0, 1)
+    asel(("BO",), ("BO0",), [[16, 8], [0, 16]], A.is_ge, 15, -1)
+    for k, base in enumerate((0, 16, -1, 15)):
+        asel(mat("P4", k), ("BO",), [[-16, 8], [-2, 16]], A.is_equal, base, 1)
+    send(slot("ZS", 0), (slot("YE", 0), "ay0"))
+    iota(("iw",), [[16, 14]], 0, 1)
+    iota(("ip",), [[0, 14]], 0, 1)
+    iota(("trf",), [[1, NB]], NP, 0)
+    for k in range(2):
+        asel(mat("BC", k), ("ONE",), [[-16, 8], [0, 16]], A.is_equal, -7 - 8 * k, 1)
+    for m, k in (("SKD", 7), ("SKA", 0)):
+        asel((m, 16, 144), ("BO",), [[-16, 8], [-8, 16]], A.is_equal, -k, 1)
+    iota(("BLK",), [[2048, 14], [0, 16]], 0, 0)
+    iota(("THR",), [[32, 14]], 9, 0)
+    for k in range(4):
+        vcp(("pW", 128 * k, 128 * k + 128), ("MODi",))
+    act(("NID32",), ("ID",), AF.Copy, scale=-32.0)
+    act(("MOD",), ("pW",), AF.Copy, bias=1792.0)
+    act(("NID",), ("ID",), AF.Copy, scale=-1.0)
+    vtt(("h64",), ("ID", 0, 64), ("ID", 64, 128), A.add)
+    fill(("MASK", 0, 896), 256.0)
+    vtt(("h32",), ("h64", 0, 32), ("h64", 32, 64), A.add)
+    fill(("MASK", 896, 1792), 256.0)
+    vtt(("rm",), ("h32", 0, 16), ("h32", 16, 32), A.add)
+    fill(("MASK", 0, 1792, 8), 0.0)
+    vts(("TLh",), ("TLi",), ("tc",), A.subtract)
+    more = [(("ONF",), ("ONE",), 1.0), (mat("G8", 1), mat("G8", 1), 4096.0), None,
+            (("BO8",), ("BO",), 8192.0), (("BIG",), ("BO",), 2.0 ** 32)]
+    for (lo, hi), x in zip(((0, 16), (16, 32), (32, 64), (64, 128), (128, 224)), more):
+        act(("DG", lo, hi), ("rm",) if hi <= 32 else ("DG", 0, hi - lo), AF.Copy)
+        if x:
+            act(x[0], x[1], AF.Copy, scale=x[2])
+    act(("NEG",), ("DG",), AF.Copy, scale=2.0 ** 23, bias=-2.0 ** 23)
+    mm(("pE", 0, NB), ("ID",), ("NEG",), True, False)
+    for k in range(2):
+        mm(("pE", 0, NB), mat("G8", k), ("TLh",), False, k == 1)
+
+    def table(i, b):
+        lo, hi = LOAD[i:i + 2]
+        mm((b, 0, hi - lo), ("ID",), ("f16t", lo, hi), True, False)
+        mm((b, 0, hi - lo), ("NID",), ("MOD", 0, hi - lo), False, True)
+        act(("LT", lo, hi), (b, 0, hi - lo), AF.Copy, bias=5904.5)
+    between = [
+        [lambda: fill(("qt",), 0.25), lambda: fill(slot("ZO", 0, *CAR), 129.0), lambda: fill(("zr",), 0.0)],
+        [lambda: fill(("SKD", 0, 16), 0.0), lambda: scan(("PK",), ("RST",), ("pE", 0, NB), A.mult, A.max)],
+        [lambda: vts(("q",), ("PK", 15, NB, 16), -2048.0, A.add), lambda: vts(("c2",), ("q",), 31, A.bitwise_and),
+         lambda: vts(("t1",), ("q",), 7, A.arith_shift_right, 4064, A.bitwise_and),
+         lambda: vts(("hi0",), ("q",), 4064, A.bitwise_and)],
+        [lambda: vtt(("ao",), ("c2",), ("t1",), A.add), lambda: vcp(("AO", NL, NL + 14), ("ao",)),
+         lambda: vcp(slot("ZO", 0, *T32), ("c2",))],
+        [lambda: vts(("ipq",), ("ip",), 112, A.bitwise_and), lambda: vtt(("iw",), ("iw",), ("ipq",), A.subtract)],
+        [lambda: fill(("SKA", 0, 16), 0.0), lambda: act(("WQ",), ("BO",), AF.Copy, scale=("wq1",)),
+         lambda: act(("NTH",), ("DG",), AF.Copy, scale=("wq2",), bias=1.0)],
+        [lambda: vts(five("sa", 0, NL, 1), ("iw", 0, NL), -16.0, A.mult)],
+        [lambda: vts(five("sa", 14 + NL, 28, 1), ("iw", NL, 14), -16.0, A.mult),
+         lambda: act(("THR",), ("THR",), AF.Copy, scale=8192.0)],
+    ]
+    weights = [lambda: None,
+               lambda: scan(("th16",), ("qt",), ("zr",), A.mult, A.add, init=2.0 ** 33),
+               lambda: vtt(("rq",), ("rm",), ("th16",), A.mult),
+               lambda: op("v", [("rq",)], [("wq1",)],
+                          lambda q: q.tensor_reduce(T.wq1[:], T.rq[:], AxisListType.X, A.add)),
+               lambda: vts(("wq2",), ("wq1",), -1.0, A.mult, -1.0, A.add)]
+    fills = [(five("sa", 0, 28, 3), M16), (five("sa", 0, 28, 0), 0.0), (five("sd", 0, 28, 0), 0.0),
+             (five("sd", 0, 28, 1), 0.0), (five("sd", 0, 28, 2), 1.0), (five("sd", 0, 28, 3), -1.0),
+             (five("sd", 0, 28, 4), 1.0), (five("sa", NL, NL + 14, 3), M32), (("A1",), 65.5),
+             (("WT", NP, NP + NB), 0.0)]
+    for i, (lo, hi) in enumerate(zip(LOAD, LOAD[1:])):
+        vtt(("f16t", lo, hi), ("ilb", lo, hi), ("pW", 0, hi - lo), A.add)
+        between[i][0]()
+        if weights:
+            weights.pop(0)()
+        for o, c in fills[i::8]:
+            fill(o, c)
+        vts(("KF", lo, hi), ("f16t", lo, hi), 1.0 / 32, A.mult, 184.515625, A.add)
+        pb = (("pA", "pB", "pZ")[i % 3], 0, hi - lo)
+        mm(pb, ("ID",), ("f16t", lo, hi), True, False)
+        mm(pb, ("NID32",), ("KF", lo, hi), False, True)
+        act(("WT", lo, hi), pb, AF.Copy, bias=5920.0)
+        for f in between[i][1:]:
+            f()
+    now[0] = 0
+    tag("spares")
+    vtt(("trm",), ("trf",), ("DG",), A.mult)
+
+    SUM, NEW, ZB, LIST = ("pE", "pL"), ("pD", "pY"), ("pZ", "pY"), ("pA", "pB")
+
+    def summed(n, p):
+        lo, hi = ARR[p]
+        z, b = slot("ZS", n, lo, hi), (SUM[p], lo, hi)
+        tag("open", p)
+        mm(b, ("ID",), ("NEG", lo, hi), True, False)
+        mm(b, ("ONE",), ("BLK", lo, hi), False, False)
+        tag("sum", p)
+        vtt(("SG", lo, hi), z, ("pZ", lo, hi), A.is_ge)
+        mm(b, ("BO",), z, False, False)
+        tag("sum", p, "b")
+        mm(b, ("BO8",), ("SG", lo, hi), False, True)
+        tag("pick", p)
+        scan(("PK", lo, hi), b, ("B", lo, hi), A.max, A.add)
+
+    def places(n, p):
+        lo, hi = ARR[p]
+        pk, a = ("PK", lo + 15, hi, 16), (NL + lo // 16, NL + hi // 16)
+        tag("skip", p)
+        vtt(five("sa", *a, 0), pk, ("THR", lo // 16, hi // 16), A.is_ge)
+        tag("floor", p)
+        lin(five("sa", *a, 2), pk, bias=M32 - 16)
+        tag("sums", p)
+        lin(five("sa", *a, 4), pk, bias=-0.5)
+        if n < ST:
+            tag("half", p)
+            lin(five("sa", *WORD[p], 2), pk, bias=M16 - 8)
+            tag("sumw", p)
+            lin(five("sa", *WORD[p], 4), pk, bias=-0.5)
+            a = SLOT[p]
+        tag("place", p)
+        scan(("LB", 5 * a[0], 5 * a[1]), ("sd", 5 * a[0], 5 * a[1]), ("sa", 5 * a[0], 5 * a[1]), A.mult, A.add,
+             also=[five(x, *a, k) for x in ("sa", "sd") for k in range(1, 5)])
+        if n < ST:
+            vcp(("AO",) + a, five("LB", *a, 4))
+            tag("words", p)
+            vcp(("XT",), slot("ZS", n, lo, hi), into=("AO",) + WORD[p])
+
+    def renew(n, p):
+        lo, hi = ARR[p]
+        b, off = (NEW[p], lo, hi), ("OFF", lo // 16, hi // 16)
+        if n == ST:
+            tag("rewrite", p)
+            return vtt(("WT",), ("DO", lo, hi), slot("ZS", n, lo, hi), A.add, into=off)
+        tag("renew", p)
+        mm(b, ("ID",), ("DO", lo, hi), True, False)
+        tag("renew", p, "b")
+        mm(b, ("ID",), slot("ZS", n, lo, hi), False, True)
+        tag("renew", p)
+        lin(("KD", lo, hi), b, 1.0 / 32, 191.515625)
+        tag("whole", p)
+        lin(("NW", lo, hi), b, bias=-64.0)
+        tag("off", p)
+        lin(("NK", lo, hi), ("KD", lo, hi), -32.0, 6208.0)
+        tag("rewrite", p)
+        vtt(("WT",), ("NW", lo, hi), ("NK", lo, hi), A.add, into=off)
+
+    def carry(n):
+        tag("carry" if n < ST else "final")
+        vtt(slot("ZO", n, *T32), five("LB", NL, NL + 14, 4), five("LB", NL, NL + 14, 1), A.add)
+        b = ("pA" if n < ST else "pW", 464, 478)
+        mm(b, ("NID32",), slot("ZS", n, *CAR), True, False)
+        mm(b, ("NID",), ("B", 15, NB, 16), False, False)
+        mm(b, ("ID",), slot("ZO", n, *T32), False, True)
+        lin(slot("ZO", n, *CAR), b, -1.0 / 32, -1.53125)
+
+    def skips():
+        tag("skips")
+        mm(("pL", 480, 494), ("ONF",), five("sa", NL, NL + 14, 0), True, True)
+        act(("Aj",), ("pL", 480, 494), AF.Copy, accum_out=("Ar",))
+        tag("A")
+        lin(("KA",), ("Ar",), 1.0 / 32, 191.515625)
+        lin(("Au",), ("KA",), -32.0, 6209.5)
+        act(("A1",), ("Au",), AF.Identity, bias=("Ar",))
+
+    def fetch(p):
+        (lo, hi), b = ARR[p], LIST[p]
+        off = ("AO", NL + lo // 16, NL + hi // 16)
+        tag("lines", p)
+        if now[0] > 1:
+            act(("LW", lo, hi), ("LT",), AF.Copy, off)
+        else:
+            tag("first", p)
+            vts(("LW", lo, hi), ("ilb",), 4112.5, A.add, off=off)
+        tag("fetch", p)
+        act(("LW", NB + lo, NB + hi), ("WT", 0, NP), AF.Copy, off)
+        w = (hi - lo) // 2
+        for src in range(2):
+            tag("fetch", p, "b" * src)
+            for k in range(4):
+                mm((b, w * (k // 2), w * (k // 2 + 1)), mat("P4", k), ("LW", NB * src + lo + k % 2, NB * src + hi, 2),
+                   src == 0 and k == 0, src == 1 and k == 3)
+        tag("lists", p)
+        vts(("EO", lo // 2, hi // 2), (b, 0, hi - lo), -4128.0, A.add)
+
+    def lowest(n):
+        el = NB * n
+        tag("rows")
+        for k in range(2):
+            mm(("pD", k, 224, 2), mat("BC", k), ("EL", el + 112, el + 224), True, True)
+        vts(("DR",), ("pD", 0, 224), 1792.0, A.add)
+        tag("wrapped")
+        for t in range(8):
+            mm(("pL", 32, 46), ("SKD", 16 - 2 * t, 144 - 2 * t), ("EL", el + 112 + t, el + 224, 8), t == 0, t == 7)
+        act(("DW",), ("pL", 32, 46), AF.Copy, bias=1792.0)
+        tag("both")
+        for t in range(8):
+            mm(("pL", 0, 28), ("SKA", 16 - 2 * t, 144 - 2 * t), ("EL", el + t, el + 224, 8), t == 0, t == 7)
+        act(("LL",), ("pL", 0, 28), AF.Copy, bias=5904.5)
+        tag("next")
+        lin(five("sa", NL, NL + 14, 1), ("LL", 0, 14), -1.0, 4128.0)
+        vtt(five("sd", NL, NL + 14, 1), ("LL", 0, 14), ("LL", 14, 28), A.subtract)
+        tag("d")
+        vcp(("DWu", 0, 14), ("DW",))
+        tag("old")
+        act(("DO",), ("WT", 0, NP), AF.Copy, ("DWu", 0, 14), bias=0.0 if n + 1 < ST else -128.0)
+        tag("alone")
+        for h in HALF:
+            mm(h, ("ID",), ("NTH",) + h[1:], True, False)
+        for p, (b, lo, hi) in enumerate(HALF):
+            for c in range(lo // 16, hi // 16):
+                tag("alike", c // 2)
+                e = ("EQ", 240 * c, 240 * c + hi - 16 * c)
+                vts(e, ("DR", 16 * c, hi), ("DW", c, c + 1), A.is_equal, 0.5, A.mult)
+                if 16 * c + 16 < hi:
+                    mm((b, 16 * c + 16, hi), ("BIG",), (e[0], e[1] + 16, e[2]), False, False)
+            tag("lost", p)
+            mm(HALF[p], ("WQ",), ("EQ", 15 * lo, 15 * hi, 1), False, True)
+            act(("LF", lo, hi), HALF[p], AF.Sign)
+            scan(("SC", lo, hi), ("trm", lo, hi), ("LF", lo, hi), A.max, A.mult)
+            tag("target", p)
+            vtt(("o2", lo // 16, hi // 16), ("SC", lo + 15, hi, 16), ("DW", lo // 16, hi // 16), A.max)
+            vcp(("OFF", lo // 16, hi // 16), ("o2", lo // 16, hi // 16))
+
+    def results(n):
+        for p in range(2):
+            fetch(p)
+        if n:
+            carry(n)
+            skips()
+        if n < 2:
+            tag("table")
+            for k, b in enumerate(("pD", "pL", "pW", "pE")):
+                table(4 * n + k, b)
+        tag("less")
+        for p in range(2):
+            mm((ZB[p],) + ARR[p], ("NID",), slot("ZS", n, *ARR[p]), True, False)
+        tag("send")
+        vts(slot("EF", n), ("EO", 0, 112), -1792.0, A.add)
+        send(slot("EF", n), (slot("EL", n), "ae%d" % n))
+        for i, (a, b) in enumerate(CH):
+            u, p = (16 * a, 16 * b), int(2 * a < LATE)
+            tag("even", i)
+            if i:
+                act(("VE",) + u, ("XT",), AF.Copy, ("EO", a, b, 0))
+            else:
+                vcp(("VE",) + u, ("XT",), off=("EO", a, b, 0))
+            tag("least", i)
+            vtt(("U",) + u, ("XT",), ("VE",) + u, A.min, off=("EO", a, b, 1))
+            tag("most", i)
+            scan(("M",) + u, ("MASK",) + u, ("U",) + u, A.min, A.max)
+            mm((ZB[p], 2 * a, 2 * b), ("ID",), ("M", 16 * a + 7, 16 * b, 8), False, 2 * a == ARR[p][0])
+            if 2 * a == ARR[p][0]:
+                lo, hi = MSG[p]
+                act(slot("ZO", n, *ARR[p]), (ZB[p],) + ARR[p], AF.Abs)
+                ways = [(slot(x, n + 1, lo, hi), "a%s%d" % (s[p], m)) for x, s, m in (("ZS", "zb", n), ("YE", "yx", n + 1))]
+                send(slot("ZO", n, lo, hi), *ways[:1 + (n + 1 < ST)])
+
+    def arrival(n):
+        tag("y")
+        mm(("pZ", 0, NB), ("ID",), slot("YE", n - 1), True, True)
+        lowest(n - 1)
+        tag("B")
+        act(("B", 15, NB, 16), slot("ZS", n, *T32), AF.Identity, bias=("A1",))
+        for p in range(2):
+            summed(n, p)
+            renew(n, p)
+            places(n, p)
+
+    for n in range(ST):
+        now[0] = n
+        results(n)
+        arrival(n + 1)
+
+    dma("y", [slot("ZS", ST)], [], T.yy[:], ap(slot("ZS", ST)), "d_o0")
+    carry(ST)
+    tag("mod")
+    act(("pA",), ("MOD",), AF.Copy, bias=-6128.5)
+    for i, b in enumerate(("pY", "pZ", "pD", "pB", "pE", "pL", "pY")):
+        lo, hi, b = 512 * i, 512 * i + 512, (b,)
+        tag("less", i)
+        mm(b, ("NID",), ("MOD",), True, False)
+        tag("turn", i)
+        mm(b, ("ID",), ("WT", lo, hi), False, False)
+        vtt(("KF", lo, hi), ("WT", lo, hi), ("pA",), A.subtract)
+        tag("turn", i, "b")
+        mm(b, ("NID",), ("KF", lo, hi), False, True)
+        if i in BYV:
+            vts(("YW", lo, hi), b, 6144.0, A.add)
+        else:
+            act(("YW", lo, hi), b, AF.Copy, bias=6144.0)
+        dma("y", [("YW", lo, hi)], [], T.yw[:, lo:hi], T.YW[:, lo:hi], "d_o%d" % (1 + i))
+    tag("clock")
+    vts(("fo", 14, 28), five("LB", NL, NL + 14, 1), -1.0, A.mult)
+    vtt(("t1",), ("hi0",), slot("ZO", ST, *T32), A.add)
+    vts(("t2",), slot("ZO", ST, *CAR), 32.0, A.mult, -4128.0, A.add)
+    vtt(("t3",), ("t1",), ("t2",), A.add)
+    vts(("q",), ("t3",), 4095, A.bitwise_and)
+    vts(("fo", 0, 14), ("q",), -2048.0, A.add)
+    for r in range(16):
+        mm(("pW", r, 448, 16, "top"), ("ID", r, 128, 16), ("fo",), True, True)
+    act(("fr", 0, 224), ("pW", 0, 224, "top"), AF.Copy, bias=2048.0)
+    act(("fr", 224, 448), ("pW", 224, 448, "top"), AF.Copy, scale=1.0 / 32)
+    dma("s", [("fr", 0, 224)], [], T.yt[:], ap(("fr", 0, 224)), "d_t")
+    dma("s", [("fr", 224, 448)], [], T.yl[:], ap(("fr", 224, 448)), "d_l")
+
+    issue(g, T, arrange(calls))
+
+
+def needs(calls):
+    before, seen, sent = [set() for _ in calls], {}, {}
+    for i, c in enumerate(calls):
+        for (name, lo, hi, w) in c["acc"]:
+            h = seen.setdefault(name, [])
+            before[i].update(j for (a, b, w2, j) in h
+                             if j != i and (bank(name) or (a < hi and lo < b and (w or w2))))
+            if bank(name):
+                h[:] = []
+            elif w:
+                h[:] = [x for x in h if not (lo <= x[0] and x[1] <= hi)]
+            h.append((lo, hi, w, i))
+        if "by" in c:
+            before[i].add(sent[c["by"]])
+        sent.setdefault(c["sem"], i)
+    return before
+
+
+def named(calls):
+    count, out = {}, []
+    for c in calls:
+        k = (c["step"], c["e"], c["name"])
+        count[k] = count.get(k, -1) + 1
+        one = c["e"] not in "vs" or c["step"] < 0 or not count[k]
+        out.append(c["name"] + ("" if one else "abcdefgh"[count[k]]))
+    return out
+
+
+def arrange(calls):
+    step, last = [{e: x[e].split() for e in x} for x in (STEP, LAST)]
+    queues = {}
+    for i, (c, name) in enumerate(zip(calls, named(calls))):
+        e, n = "p" if "by" in c else c["e"], c["step"]
+        if n < 0 or e == "y":
+            key = (n, 0, i)
+        else:
+            if n < ST - 1 and name + "+" in step[e]:
+                name, n = name + "+", n + 1
+            key = (n, (last if n == ST - 1 else step)[e].index(name), i)
+        queues.setdefault(c["e"], []).append((key, i))
+    queues = [[i for _, i in sorted(q)][::-1] for q in queues.values()]
+    before, done, out = needs(calls), set(), []
+    while len(out) < len(calls):
+        moved = len(out)
+        for q in queues:
+            while q and before[q[-1]] <= done:
+                done.add(q[-1])
+                out.append(calls[q.pop()])
+        assert len(out) > moved
+    return out
+
+
+def issue(g, T, calls):
     queues = {"v": g.vector, "t": g.tensor, "s": g.scalar, "p": g, "y": g.sync}
     semof = {"v": "cv", "t": "ct", "s": "cs", "p": "cp"}
     count = {s: 0 for s in SEMAPHORES}
@@ -49,20 +566,14 @@ def rank_program(g, core, T, topo):
     hist = {}
 
     def conflicts(e, name, lo, hi, write):
-        bank = name[0] == "p" and name[1:2].isupper()
         out = []
         for (a, b, e2, s2, v2, w2, asy) in hist.get(name, []):
-            if bank:
-                if e2 == e:
-                    if e == "t" or not (write or w2) or b <= lo or hi <= a:
-                        continue
+            if bank(name) and e2 != e:
                 out.append((s2, v2))
+            elif b <= lo or hi <= a or not (write or w2) or (bank(name) and e == "t"):
                 continue
-            if b <= lo or hi <= a or not (write or w2):
-                continue
-            if e2 == e and not asy and not w2:
-                continue
-            out.append((s2, v2))
+            elif e2 != e or asy or w2 or bank(name):
+                out.append((s2, v2))
         return out
 
     def waits(e, acc):
@@ -91,502 +602,22 @@ def rank_program(g, core, T, topo):
                 h[:] = [x for x in h if not (x[2] == e and not x[5] and not asy and lo <= x[0] and x[1] <= hi)]
             h.append((lo, hi, e, s, v, w, asy))
 
-    def access(rd, wr):
-        return [rg(o) + (False,) for o in rd] + [rg(o) + (True,) for o in wr]
-
-    def op(e, rd, wr, fn):
-        acc = access(rd, wr)
+    for c in calls:
+        e, acc, s = c["e"], c["acc"], c["sem"]
+        if "by" in c:
+            count[s] = c["n"]
+            note(e, acc, s, c["n"], True)
+            continue
         waits(e, acc)
-        s = semof[e]
-        count[s] += 1
-        fn(queues[e]).then_inc(T.sem[s], 1)
-        note(e, acc, s, count[s], False)
-
-    def dma(e, rd, wr, out, in_, s):
-        acc = access(rd, wr)
-        waits(e, acc)
-        count[s] += 16
-        queues[e].dma_start(out, in_).then_inc(T.sem[s], 16)
-        note(e, acc, s, count[s], True)
-
-    def ap(o):
-        if o[0] == "EQ":
-            c, a = divmod(o[1], 240)
-            return T.EQ[:, c, a:a + o[2] - o[1]] if len(o) == 3 else T.EQ[:, c:o[2] // 240, 0:16]
-        if o[0] == "EO":
-            return T.EO[:, o[3], o[1]:o[2]] if len(o) == 4 else T.EO[:, :, o[1]:o[2]]
-        rows = slice(0, 8) if o[-1] == "top" else slice(0, TOP[o[0]]) if o[0] in TOP else slice(None)
-        o = o[:-1] if o[-1] == "top" else o
-        if len(o) == 1:
-            return T[o[0]][rows]
-        if len(o) == 4:
-            return T[o[0]][rows, o[1]:o[2]:o[3]]
-        return T[o[0]][rows, o[1]:o[2]]
-
-    def rg(o):
-        if o[0] in ("sa", "sd"):
-            return ("%s%d" % (o[0], o[1] % 5), o[1], o[2])
-        if o[0] == "trm" and len(o) == 4:
-            return ("trm", o[1], o[1] + 1)
-        return (o[0], 0, SCRATCH[o[0]][1][1]) if len(o) == 1 else (o[0], o[1], o[2])
-
-    def vts(out, i, s1, o0, s2=None, o1=None):
-        rd = [i] + [s for s in (s1, s2) if isinstance(s, tuple)]
-        s1, s2 = [ap(s) if isinstance(s, tuple) else s for s in (s1, s2)]
-        if o1 is None:
-            op("v", rd, [out], lambda q: q.tensor_scalar(ap(out), ap(i), s1, None, o0))
-        else:
-            op("v", rd, [out], lambda q: q.tensor_scalar(ap(out), ap(i), s1, s2, o0, o1))
-
-    def vtt(out, a, b, o):
-        op("v", [a, b], [out], lambda q: q.tensor_tensor(ap(out), ap(a), ap(b), o))
-
-    def vcp(out, i):
-        op("v", [i], [out], lambda q: q.tensor_copy(ap(out), ap(i)))
-
-    def scan(out, a, b, o0, o1, init=0.0, also=()):
-        op("v", [a, b] + list(also), [out], lambda q: q.tensor_tensor_scan(ap(out), ap(a), ap(b), init, o0, o1))
-
-    def fill(out, c):
-        op("v", [], [out], lambda q: q.memset(ap(out), c))
-
-    def act(out, i, f, off=None, **kw):
-        cols = {k: v for k, v in kw.items() if isinstance(v, tuple)}
-        kw.update({k: ap(v) for k, v in cols.items()})
-        src = ap(i).indirect(ap(off)) if off else ap(i)
-        op("s", [i] + ([off] if off else []) + [v for k, v in cols.items() if k != "accum_out"],
-           [out] + [v for k, v in cols.items() if k == "accum_out"], lambda q: q.activation(ap(out), src, f, **kw))
-
-    def mm(out, l, r, start, stop):
-        op("t", [l, r], [out], lambda q: q.matmul(ap(out), ap(l), ap(r), start, stop))
-
-    def mat(n, r):
-        return (n, 128 * r, 128 * r + 128)
-
-    nxt = T.cores[(rank + 1) % NR]
-    prv = T.cores[(rank - 1) % NR]
-    rid, pid = topo.addr(nxt)[:2]
-    emask = topo.mask(core, nxt)
-    n_out = len(topo.engines(core, nxt))
-    n_in = len(topo.engines(prv, core))
-
-    def send(dst, src, s):
-        waits("p", access([src], []))
-        g.remote_dma(out_ap=ap(dst), in_ap=ap(src), remote_sem=T.sem[s], local_sem=T.sem["loc"], pid=pid,
-                     routing_id=rid, dma_engine_mask=emask)
-        count["loc"] += n_out
-
-    def lands(dst, s):
-        count[s] = n_in
-        note("r", access([], [dst]), s, n_in, True)
-
-    def slot(b, n, lo=0, hi=NB):
-        o = 256 * n + 32 if b in ("ZS", "ZO") else NB * n
-        return (b, o + lo, o + hi)
-
-    for n in range(ST):
-        lands(slot("YE", n), "ay%d" % n)
-        lands(slot("EL", n), "ae%d" % n)
-        for (lo, hi), s in zip(MSG, "zb"):
-            lands(slot("ZS", n + 1, lo, hi), "a%s%d" % (s, n))
-
-    dma("s", [], [("TLi", 0, 1)], T.TLi[0:8], T.tk0[:], "d_tk")
-    dma("s", [], [("TLi", 1, 2)], T.TLi[8:16], T.ln0[:], "d_ln")
-    dma("s", [], [slot("ZS", 0)], ap(slot("ZS", 0)), T.y0[:], "d_y")
-    for i, (lo, hi) in enumerate(zip(LOAD, LOAD[1:])):
-        dma("y", [], [("ilb", lo, hi)], T.ilb[:, lo:hi], T.il[:, lo:hi], "d_il%d" % i)
-    for i in range(2):
-        b = ("XT", 1792 * i, 1792 * i + 1792)
-        dma("y", [], [b], ap(b), T.xw[:, 1792 * i:1792 * i + 1792], "d_x%d" % i)
-
-    def asel(out, i, pat, cmp, base, cm):
-        op("p", [i], [out], lambda q: q.affine_select(ap(out), i if i is None else ap(i), pat, cmp, 0.0, base, cm))
-
-    def iota(out, pat, base, cm, **kw):
-        op("p", [], [out], lambda q: q.iota(ap(out), pat, base, cm, **kw))
-    fill(("ONE",), 1.0)
-    fill(mat("G8", 2), 1.0)
-    iota(("MODi",), [[0, 4], [1, 32]], -1792, 0)
-    asel(("ID",), ("ONE",), [[-1, 128]], A.is_equal, 0, 1)
-    for k in range(2):
-        asel(mat("G8", k), mat("G8", 2), [[1, 8], [0, 16]], A.is_equal, 8 * k, -1)
-    asel(("BO0",), ("ONE",), [[-16, 8], [0, 16]], A.is_ge, 0, 1)
-    asel(("BO",), ("BO0",), [[16, 8], [0, 16]], A.is_ge, 15, -1)
-    for k, base in enumerate((0, 16, -1, 15)):
-        asel(mat("P4", k), ("BO",), [[-16, 8], [-2, 16]], A.is_equal, base, 1)
-    send(slot("YE", 0), slot("ZS", 0), "ay0")
-    iota(("trf",), [[1, NB]], NP, 0, allow_small_or_imprecise_dtypes=True)
-    iota(("iw",), [[16, 14]], 0, 1)
-    iota(("ip",), [[0, 14]], 0, 1)
-    iota(("BLK",), [[2048, 14], [0, 16]], 0, 0, allow_small_or_imprecise_dtypes=True)
-    iota(("THR",), [[32, 14]], 9, 0, allow_small_or_imprecise_dtypes=True)
-    for k in range(2):
-        asel(mat("BC", k), ("ONE",), [[-16, 8], [0, 16]], A.is_equal, -7 - 8 * k, 1)
-    for m, k in (("SKD", 7), ("SKA", 0)):
-        fill((m, 0, 16), 0.0)
-        asel((m, 16, 144), ("BO",), [[-16, 8], [-8, 16]], A.is_equal, -k, 1)
-    fill(("RST",), 1.0)
-    fill(("tc",), -1.0)
-    fill(("qt",), 0.25)
-    fill(("zr",), 0.0)
-    fill(("RST", 0, NB, 16), 0.0)
-    fill(("tc", 0, 1, "top"), 2048.0)
-    for k in range(4):
-        vcp(("pW", 128 * k, 128 * k + 128), ("MODi",))
-    act(("MOD",), ("pW",), AF.Copy, bias=1792.0)
-    vtt(("h64",), ("ID", 0, 64), ("ID", 64, 128), A.add)
-    vts(("NID32",), ("ID",), -32.0, A.mult)
-    fill(("MASK", 0, 896), 256.0)
-    vtt(("h32",), ("h64", 0, 32), ("h64", 32, 64), A.add)
-    fill(("MASK", 896, 1792), 256.0)
-    vtt(("rm",), ("h32", 0, 16), ("h32", 16, 32), A.add)
-
-    def shift(i):
-        lo, hi = LOAD[i:i + 2]
-        vtt(("f16t", lo, hi), ("ilb", lo, hi), ("pW", 0, hi - lo), A.add)
-
-    def table(i):
-        lo, hi = LOAD[i:i + 2]
-        vts(("KF", lo, hi), ("f16t", lo, hi), 1.0 / 32, A.mult, 184.515625, A.add)
-        pb = (("pA", "pB", "pZ")[i % 3], 0, hi - lo)
-        mm(pb, ("ID",), ("f16t", lo, hi), True, False)
-        mm(pb, ("NID32",), ("KF", lo, hi), False, True)
-        act(("WT", lo, hi), pb, AF.Copy, bias=5920.0)
-
-    def diagonal():
-        for lo, hi in ((0, 16), (16, 32)):
-            act(("DG", lo, hi), ("rm",), AF.Copy)
-        act(mat("G8", 1), mat("G8", 1), AF.Copy, scale=4096.0)
-        act(("DG", 32, 64), ("DG", 0, 32), AF.Copy)
-        act(("NID",), ("ID",), AF.Copy, scale=-1.0)
-        act(("DG", 64, 128), ("DG", 0, 64), AF.Copy)
-        act(("BO8",), ("BO",), AF.Copy, scale=8192.0)
-        act(("DG", 128, 224), ("DG", 0, 96), AF.Copy)
-        act(("BIG",), ("BO",), AF.Copy, scale=2.0 ** 32)
-        act(("NEG",), ("DG",), AF.Copy, scale=2.0 ** 23, bias=-2.0 ** 23)
-
-    def spread():
-        mm(("pE", 0, NB), ("ID",), ("NEG",), True, False)
-        for k in range(2):
-            mm(("pE", 0, NB), mat("G8", k), ("TLh",), False, k == 1)
-    between = [
-        [diagonal, lambda: vts(("TLh",), ("TLi",), ("tc",), A.subtract)],
-        [lambda: act(("P32", 0, 256), ("P4", 0, 256), AF.Copy, scale=32.0)],
-        [spread],
-        [lambda: scan(("PK",), ("RST",), ("pE", 0, NB), A.mult, A.max)],
-        [lambda: vts(("q",), ("PK", 15, NB, 16), -2048.0, A.add),
-         lambda: act(("P32", 256, 512), ("P4", 256, 512), AF.Copy, scale=32.0)],
-        [lambda: vts(("c2",), ("q",), 31, A.bitwise_and),
-         lambda: vts(("t1",), ("q",), 7, A.arith_shift_right, 4064, A.bitwise_and)],
-        [lambda: vtt(("ao",), ("c2",), ("t1",), A.add)],
-        [lambda: vcp(("AO", 14, 28), ("ao",))],
-    ]
-    for i in range(8):
-        shift(i)
-        if i:
-            table(i - 1)
-        for f in between[i]:
-            f()
-    table(7)
-
-    def weights(k):
-        if k == 0:
-            scan(("th16",), ("qt",), ("zr",), A.mult, A.add, 2.0 ** 33)
-            fill(("MASK", 0, 1792, 8), 0.0)
-            vts(("ipq",), ("ip",), 112, A.bitwise_and)
-            vcp(slot("ZO", 0, -28, -14), ("c2",))
-            vtt(("rq",), ("rm",), ("th16",), A.mult)
-            vts(("hi0",), ("q",), 4064, A.bitwise_and)
-            fill(slot("ZO", 0, -14, 0), 129.0)
-            vtt(("iw",), ("iw",), ("ipq",), A.subtract)
-            op("v", [("rq",)], [("wq1",)], lambda q: q.tensor_reduce(T.wq1[:], T.rq[:], AxisListType.X, A.add))
-            fill(("A1",), 1.0)
-            fill(("B",), 0.0)
-            vts(("sa", 1, 70, 5), ("iw",), -16.0, A.mult)
-            vts(("wq2",), ("wq1",), -1.0, A.mult, -1.0, A.add)
-        elif k == 1:
-            for o, c in ((("sd", 0, 140, 5), 0.0), (("sd", 1, 70, 5), 0.0), (("sd", 2, 140, 5), 1.0),
-                         (("sd", 3, 140, 5), -1.0), (("sd", 4, 140, 5), 1.0), (("sa", 0, 70, 5), 0.0),
-                         (("sa", 3, 70, 5), M32 / 2), (("sa", 73, 140, 5), M32)):
-                fill(o, c)
-        else:
-            act(("WQ",), ("BO",), AF.Copy, scale=("wq1",))
-            act(("NTH",), ("DG",), AF.Copy, scale=("wq2",), bias=1.0)
-            act(("THR",), ("THR",), AF.Copy, scale=8192.0)
-            act(("ONF",), ("ONE",), AF.Copy)
-            for r in range(16):
-                act(("trm", r, NB, 16), ("trf", r, NB, 16), AF.Copy, scale=("rm", r, r + 1))
-
-    SUM, NEW = ("pE", "pL"), ("pD", "pA")
-
-    def opened(p):
-        mm((SUM[p],) + ARR[p], ("ID",), ("NEG",) + ARR[p], True, False)
-        mm((SUM[p],) + ARR[p], ("ONE",), ("BLK",) + ARR[p], False, False)
-
-    def reach(n, p):
-        lo, hi = ARR[p]
-        vtt(("SG", lo, hi), slot("ZS", n, lo, hi), ("pZ", lo, hi), A.is_ge)
-
-    def sums(n, p):
-        lo, hi = ARR[p]
-        mm((SUM[p], lo, hi), ("BO",), slot("ZS", n, lo, hi), False, False)
-        mm((SUM[p], lo, hi), ("BO8",), ("SG", lo, hi), False, True)
-
-    def renew(n, p):
-        lo, hi = ARR[p]
-        b = (NEW[p], lo, hi)
-        mm(b, ("ID",), ("DO", lo, hi), True, False)
-        mm(b, ("ID",), slot("ZS", n, lo, hi), False, True)
-        act(("KD", lo, hi), b, AF.Copy, scale=1.0 / 32, bias=191.515625)
-        act(("NW", lo, hi), b, AF.Copy, bias=-64.0)
-        act(("NK", lo, hi), ("KD", lo, hi), AF.Copy, scale=-32.0, bias=6208.0)
-
-    def rewrite(lo, hi):
-        off = ("OFF", lo // 16, hi // 16)
-        op("v", [("NW", lo, hi), ("NK", lo, hi), off], [("WT",)],
-           lambda q: q.tensor_tensor(T.WT[:].indirect(ap(off)), T.NW[:, lo:hi], T.NK[:, lo:hi], A.add))
-
-    def pick(p):
-        lo, hi = ARR[p]
-        scan(("PK", lo, hi), (SUM[p], lo, hi), ("B", lo, hi), A.max, A.add)
-
-    def losers(h):
-        lo, hi = HALF[h][1:]
-        scan(("SC", lo, hi), ("trm", lo, hi), ("LF", lo, hi), A.max, A.mult)
-
-    def late(n):
-        reach(n, 1)
-        renew(n, 1)
-        sums(n, 1)
-        losers(1)
-        vtt(("o2",), ("SC", 15, NB, 16), ("DW",), A.max)
-        pick(0)
-        pick(1)
-        vcp(("OFF", 0, 14), ("o2",))
-        pk = ("PK", 15, NB, 16)
-        vtt(("sa", 70, 140, 5), pk, ("THR",), A.is_ge)
-        vts(("sa", 72, 140, 5), pk, -15.5, A.add, M32, A.add)
-        act(("sa", 74, 140, 5), pk, AF.Copy)
-        if n < ST:
-            vts(("sa", 2, 70, 5), pk, -7.5, A.add, M32 / 2, A.add)
-            act(("sa", 4, 70, 5), pk, AF.Copy)
-            rewrite(*NEWS[0])
-        else:
-            rewrite(0, NB)
-        lo = 0 if n < ST else 70
-        scan(("LB", lo, 140), ("sd", lo, 140), ("sa", lo, 140), A.mult, A.add,
-             also=[(b, k + lo, 140) for b in ("sa", "sd") for k in range(1, 5)])
-        if n < ST:
-            rewrite(*NEWS[1])
-            vcp(("AO",), ("LB", 4, 140, 5))
-
-    def carry(n, k):
-        if k == 0:
-            vtt(slot("ZO", n, -28, -14), ("LB", 74, 140, 5), ("LB", 71, 140, 5), A.add)
-        elif k == 1:
-            mm(("pW", 64, 78), ("NID32",), slot("ZS", n, -14, 0), True, False)
-            mm(("pW", 64, 78), ("NID",), ("B", 15, NB, 16), False, False)
-            mm(("pW", 64, 78), ("ID",), slot("ZO", n, -28, -14), False, True)
-            if n < ST:
-                mm(("pW", 80, 94), ("ONF",), ("sa", 70, 140, 5), True, True)
-        else:
-            act(slot("ZO", n, -14, 0), ("pW", 64, 78), AF.Copy, scale=-1.0 / 32, bias=0.484375)
-            if n < ST:
-                act(("Aj",), ("pW", 80, 94), AF.Copy, accum_out=("Ar",))
-
-    def fetch(f):
-        lo, hi, b = FET[f]
-        w = (hi - lo) // 2
-        off = ("AO", 14 + lo // 16, 14 + hi // 16)
-        op("v", [("ilb",), off], [("LG", lo, hi)],
-           lambda q: q.tensor_scalar(T.LG[:, lo:hi], T.ilb[:].indirect(ap(off)), 1.0 / 32, 128.515625, A.mult, A.add))
-        act(("WA", lo, hi), ("WT", 0, NP), AF.Copy, off)
-        for src, m in (("LG", "P32"), ("WA", "P4")):
-            for k in range(4):
-                mm((b, w * (k // 2), w * (k // 2 + 1)), mat(m, k), (src, lo + k % 2, hi, 2),
-                   src == "LG" and k == 0, src == "WA" and k == 3)
-
-    def offsets(f):
-        lo, hi, b = FET[f]
-        vts(("EO", lo // 2, hi // 2), (b, 0, hi - lo), -4128.0, A.add)
-
-    ZB = ("pZ", "pY")
-
-    def even(i):
-        a, b = CH[i]
-        off = ("EO", a, b, 0)
-        if i:
-            act(("VE", 16 * a, 16 * b), ("XT",), AF.Copy, off)
-        else:
-            op("v", [("XT",), off], [("VE", 16 * a, 16 * b)],
-               lambda q: q.tensor_copy(T.VE[:, 16 * a:16 * b], T.XT[:].indirect(ap(off))))
-
-    def least(i):
-        a, b = CH[i]
-        off = ("EO", a, b, 1)
-        op("v", [("XT",), off, ("VE", 16 * a, 16 * b)], [("U", 16 * a, 16 * b)],
-           lambda q: q.tensor_tensor(T.U[:, 16 * a:16 * b], T.XT[:].indirect(ap(off)), T.VE[:, 16 * a:16 * b], A.min))
-
-    def greatest(i):
-        a, b = CH[i]
-        scan(("M", 16 * a, 16 * b), ("MASK", 16 * a, 16 * b), ("U", 16 * a, 16 * b), A.min, A.max)
-        mm((ZB[2 * b > EARLY], 2 * a, 2 * b), ("ID",), ("M", 16 * a + 7, 16 * b, 8), False, 2 * b in (EARLY, NB))
-
-    def out_z(n, p):
-        act(slot("ZO", n, *ARR[p]), (ZB[p],) + ARR[p], AF.Abs)
-        send(slot("ZS", n + 1, *MSG[p]), slot("ZO", n, *MSG[p]), "a%s%d" % ("zb"[p], n))
-
-    def step(n):
-        z = slot("ZS", n)
-        if n:
-            late(n)
-            send(slot("YE", n), z, "ay%d" % n)
-        fetch(0)
-        fetch(1)
-        if n:
-            op("v", [z, ("AO", 0, 14)], [("XT",)], lambda q: q.tensor_copy(T.XT[:].indirect(T.AO[:, 0:14]), ap(z)))
-        else:
-            weights(0)
-        offsets(0)
-        if n:
-            carry(n, 0)
-        even(0)
-        even(1)
-        offsets(1)
-        if n:
-            carry(n, 1)
-        for p in range(2):
-            mm((ZB[p],) + ARR[p], ("NID",), slot("ZS", n, *ARR[p]), True, False)
-        least(0)
-        vts(slot("EF", n), ("EO", 0, 112), -1792.0, A.add)
-        send(slot("EL", n), slot("EF", n), "ae%d" % n)
-        least(1)
-        greatest(0)
-        for i in range(2, len(CH)):
-            even(i)
-        if n == 0:
-            weights(2)
-        opened(0)
-        for h in HALF:
-            mm(h, ("ID",), ("NTH",) + h[1:], True, False)
-        if n:
-            carry(n, 2)
-            act(("KA",), ("Ar",), AF.Copy, scale=1.0 / 32, bias=191.515625)
-        for i in range(2, len(CH)):
-            least(i)
-            if 2 * CH[i - 1][1] != EARLY:
-                greatest(i - 1)
-            if 2 * CH[i][1] == EARLY:
-                greatest(i)
-                out_z(n, 0)
-                ahead(n)
-                if n:
-                    act(("Au",), ("KA",), AF.Copy, scale=-32.0, bias=6145.0)
-                act(("sa", 71, 210, 5), ("LL",), AF.Copy, scale=-32.0, bias=4128.0)
-        vts(("DR",), ("pD", 0, 224), 1792.0, A.add)
-        greatest(len(CH) - 1)
-        out_z(n, 1)
-        mm(("pZ", 0, NB), ("ID",), slot("YE", n), True, True)
-        opened(1)
-
-    def ahead(n):
-        el = NB * n
-        for k in range(2):
-            mm(("pD", k, 224, 2), mat("BC", k), ("EL", el + 112, el + 224), True, True)
-        for t in range(8):
-            mm(("pW", 32, 46), ("SKD", 16 - 2 * t, 144 - 2 * t), ("EL", el + 112 + t, el + 224, 8), t == 0, t == 7)
-        for t in range(8):
-            mm(("pL", 0, 28), ("SKA", 16 - 2 * t, 144 - 2 * t), ("EL", el + t, el + 224, 8), t == 0, t == 7)
-        act(("DW",), ("pW", 32, 46), AF.Copy, bias=1792.0)
-        act(("LL",), ("pL", 0, 28), AF.Copy, scale=1.0 / 32, bias=184.515625)
-
-    def ready(n):
-        vcp(("DWu", 0, 14), ("DW",))
-        if n:
-            act(("A1",), ("Au",), AF.Identity, bias=("Ar",))
-        act(("DO",), ("WT", 0, NP), AF.Copy, ("DWu", 0, 14))
-
-        for c in range(14):
-            e = ("EQ", 240 * c, 240 * c + 224 - 16 * c)
-            vts(e, ("DR", 16 * c, 224), ("DW", c, c + 1), A.is_equal, 0.5, A.mult)
-            for b, lo, hi in HALF:
-                lo = max(lo, 16 * c + 16)
-                if lo < hi:
-                    mm((b, lo, hi), ("BIG",), (e[0], e[1] + lo - 16 * c, e[1] + hi - 16 * c), False, False)
-            if c % 7 == 6:
-                h = c // 7
-                mm(HALF[h], ("WQ",), ("EQ", 7 * 240 * h, 7 * 240 * (h + 1), 1), False, True)
-                act(("LF",) + HALF[h][1:], HALF[h], AF.Sign)
-        act(("B", 15, NB, 16), slot("ZS", n + 1, -28, -14), AF.Identity, bias=("A1",))
-        if n == 0:
-            weights(1)
-        vtt(("sd", 71, 140, 5), ("sa", 141, 210, 5), ("sa", 71, 140, 5), A.subtract)
-        losers(0)
-        reach(n + 1, 0)
-        renew(n + 1, 0)
-        sums(n + 1, 0)
-
-    for n in range(ST):
-        step(n)
-        ready(n)
-
-    FIN = ("pY", "pB", "pZ", "pD", "pL", "pA", "pY")
-
-    def reduced(i, k):
-        if not 0 <= i < 7:
-            return
-        lo, hi = 512 * i, 512 * i + 512
-        b = (FIN[i],)
-        if k == 0:
-            mm(b, ("NID",), ("MOD",), True, False)
-        elif k == 1:
-            mm(b, ("ID",), ("WT", lo, hi), False, False)
-        elif k == 2:
-            vtt(("KF", lo, hi), ("WT", lo, hi), ("pE",), A.is_ge)
-        else:
-            mm(b, ("NID32",), ("KF", lo, hi), False, True)
-            if i < 6:
-                act(("YW", lo, hi), b, AF.Copy, bias=32.0)
-            else:
-                vts(("YW", lo, hi), b, 32.0, A.add)
-            dma("y", [("YW", lo, hi)], [], T.yw[:, lo:hi], T.YW[:, lo:hi], "d_o%d" % (1 + i))
-
-    def rows():
-        for r in range(16):
-            mm(("pW", r, 448, 16, "top"), ("ID", r, 128, 16), ("fo",), True, True)
-
-    def last():
-        act(("fr", 0, 224), ("pW", 0, 224, "top"), AF.Copy, bias=2048.0)
-        act(("fr", 224, 448), ("pW", 224, 448, "top"), AF.Copy, scale=1.0 / 32)
-        dma("s", [("fr", 0, 224)], [], T.yt[:], ap(("fr", 0, 224)), "d_t")
-        dma("s", [("fr", 224, 448)], [], T.yl[:], ap(("fr", 224, 448)), "d_l")
-    clock = [[lambda: vtt(("t1",), ("hi0",), slot("ZO", ST, -28, -14), A.add)],
-             [lambda: vts(("t2",), slot("ZO", ST, -14, 0), 32.0, A.mult, -4128.0, A.add)],
-             [lambda: vtt(("t3",), ("t1",), ("t2",), A.add)],
-             [lambda: vts(("q",), ("t3",), 4095, A.bitwise_and)],
-             [lambda: vts(("fo", 0, 14), ("q",), -2048.0, A.add), rows],
-             [last], []]
-
-    dma("y", [slot("ZS", ST)], [], T.yy[:], ap(slot("ZS", ST)), "d_o0")
-    late(ST)
-    mm(("pE",), ("ID",), ("MOD",), True, True)
-    for i in range(6):
-        reduced(i, 0)
-    reduced(0, 2)
-    carry(ST, 0)
-    vts(("fo", 14, 28), ("LB", 71, 140, 5), -1.0, A.mult)
-    reduced(0, 1)
-    for i in range(7):
-        reduced(i + 1, 2)
-        reduced(i, 3)
-        if i == 0:
-            carry(ST, 1)
-            carry(ST, 2)
-        if i == 3:
-            reduced(6, 0)
-        reduced(i + 1, 1)
-        for f in clock[i]:
-            f()
+        ins = c["fn"](queues[e])
+        if "out" in c:
+            count["loc"] += c["out"]
+            continue
+        k = 16 if s else 1
+        s = s or semof[e]
+        count[s] += k
+        ins.then_inc(T.sem[s], k)
+        note(e, acc, s, count[s], k > 1)
     for s in SEMAPHORES:
         if count[s] and known["p"].get(s, 0) < count[s]:
             g.wait_ge(T.sem[s], count[s])

from concourse.bass import DstId, RemoteDMATransfer
from concourse.mybir import AluOpType as A, AxisListType, ActivationFunctionType as AF

NP, NB, NR, ST = 3584, 224, 4, 8
LATE = 96
EDGE = (112, 102, 80, 64, 48, 20, 0)
CH = [(b, a) for a, b in zip(EDGE, EDGE[1:])]
ARR = ((LATE, NB), (0, LATE))
MSG = ((LATE, NB + 28), (0, LATE))
NL = LATE // 16
SLOT = ((2 * NL, 28), (0, 2 * NL))
WORD = ((14 + NL, 28), (0, NL))
HALF = (("pB",) + ARR[0], ("pW",) + ARR[1])
LOAD = [512 * i for i in range(7)] + [3392, NP]
ONV = ()
BYV = (6,)
M32, M16 = 2.0 ** 28, 2.0 ** 27

STEP = {
    "v": """sum1+ skip0+ target1+ rewrite0+ pick1+ place0+ target1b+ skip1+ place0b+ rewrite1+ place1+ first0 words0+
         place1b+ first1 carry words1+ lists0 even0 lists1 least0 send least3 most0 least2 least1 most2 most3 most1
         least4 least5 most4 most5 rows spares d alike3 alike3b alike4 alike4b alike5 alike5b alike6 alike6b alike0
         alike2 alike0b alike1 alike2b alike1b sum0 next lost0 target0 pick0 lost1 target0b""",
    "s": """lost1+ whole0+ off0+ floor0+ sums0+ sumw0+ half0+ renew1+ whole1+ off1+ half1+ sums1+ sumw1+ floor1+ lines0
         fetch0 skips lines1 fetch1 A even3 Ab even2 Ac even1 carry even4 even5 table tableb most3 tablec wrapped
         tabled most5 old both lost0 B renew0 next""",
    "t": """alike2+ lost1+ sum0+ sum0b+ open1+ renew1b+ sum1+ sum1b+ less skips fetch0 fetch0b fetch1 fetch1b carry
         table most0 most1 most2 most3 rows wrapped most4 y most5 open0 alone both alike3 alike4 alike5 alike6 lost0
         renew1 renew0 renew0b alike0 alike1""",
    "p": "send most3 most5",
}
LAST = {
    "v": """sum1+ skip0+ target1+ rewrite0+ pick1+ place0+ target1b+ skip1+ place0b+ rewrite1+ place1+ words0+ place1b+
         words1+ lists0 carry even0 lists1 least0 send least3 most0 least2 least1 most3 most2 most1 least4 least5 rows
         most4 most5 alike3b alike4 alike4b alike3 alike5 alike6 alike5b alike6b alike1b alike2b d alike0b alike0
         alike1 alike2 lost0 sum0 target0 lost1 target0b target1 rewrite0 target1b pick0 sum1 rewrite1 skip0 next
         turn0 pick1 turn1 skip1 turn2 place0 place1 turn3 final turn4 clockb turn5 clockc turn6 clockd clocke clock
         clockf turn6b""",
    "s": """lost1+ whole0+ off0+ sumw0+ floor0+ sums0+ renew1+ half0+ whole1+ off1+ sumw1+ sums1+ half1+ floor1+ lines0
         fetch0 skips lines1 fetch1 even3 even2 even1 even4 even5 A carry most3 Ab wrapped Ac most5 both lost0 lost1
         old mod B sums1 floor0 floor1 sums0 next turn0b turn1b turn2b final turn3b turn4b turn5b clock clockb clockc
         clockd""",
    "t": """alike2+ lost1+ sum0+ sum0b+ renew1b+ open1+ sum1+ open0 sum1b+ skips fetch0 fetch0b fetch1 fetch1b less most0
         most1 most2 alone most3 carry rows wrapped most4 y most5 both alike3 alike4 alike5 alike6 lost0 alike0 alike1
         alike2 lost1 less2 sum0 sum0b open1 less0 less3 less4 sum1 sum1b turn0 less1 turn0b turn1 turn2 turn1b turn3
         turn2b less5 turn4 final turn3b turn4b less6 turn5 turn6 turn5b turn6b clock""",
    "p": "send most3 most5",
}


def _sb(dtype, **widths):
    return {n: ("sbuf", [128, w], dtype) for n, w in widths.items()}


SCRATCH = {
    **_sb("int32", ilb=NP, TLi=NB, MODi=128, iw=14, ip=14, ipq=14, q=14, c2=14, ao=14, hi0=14, t1=14, t2=14, t3=14),
    **_sb("float16", f16t=NP, TLh=NB, fo=28, EF=8 * NB, EL=8 * NB),
    **_sb("uint16", DR=NB, DWu=16, OFF=16, AO=28),
    **_sb("float32", h64=64, h32=32, rm=16, DG=NB, PK=NB, tc=1, o2=14, DW=14, rq=16, qt=16, zr=16, wq1=1, wq2=1,
          th16=16, trf=NB, trm=NB, SC=NB, LB=140, sd=140, sa=140, THR=14, ONF=128, Ar=1, Au=1, A1=1, Aj=14, fr=2 * NB),
    **_sb("bfloat16", XT=NP, LT=NP, WT=NP + NB, YW=NP, KF=NP, ONE=128, BO0=128, BO=128, BO8=128, G8=384, MOD=512,
          BLK=NB,
          ID=128, NID=128, NID32=128, P4=512, BC=256, SKA=144, SKD=144, WQ=128, BIG=128, NTH=NB, LF=NB, LL=28,
          NEG=NB, RST=NB, ZS=9 * 256, ZO=9 * 256, YE=8 * 256, SG=NB, KA=1, DO=NB, KD=NB, NW=NB, NK=NB, B=NB,
          LW=2 * NB, VE=1792, MASK=1792, U=1792, M=1792),
    "EQ": ("sbuf", [128, 14, 240], "bfloat16"),
    "EO": ("sbuf", [128, 2, 112], "uint16"),
    **{n: ("psum", [128, 512], "float32") for n in ("pA", "pB", "pZ", "pY", "pD", "pW", "pE", "pL")},
}
SEMAPHORES = (["cv", "ct", "cs", "cp", "loc", "d_tk", "d_ln", "d_y", "d_x0", "d_x1", "d_t", "d_l"]
              + ["d_il%d" % i for i in range(8)] + ["d_o%d" % i for i in range(8)]
              + ["a%s%d" % (k, n) for k in "zbeyx" for n in range(ST)])
TOP = {"TLi": 16, "TLh": 16, "G8": 16, "tc": 16, "fr": 8}


def bank(name):
    return name[0] == "p" and name[1:2].isupper()


def rank_program(g, core, T, topo):
    rank = T.rank_of(core)
    if rank is None:
        return
    calls, now = [], [-1, ""]

    def tag(*name):
        now[1] = "".join(str(x) for x in name)

    def ap(o):
        if o[0] == "EQ":
            c, a = divmod(o[1], 240)
            return T.EQ[:, c, a:a + o[2] - o[1]] if len(o) == 3 else T.EQ[:, c:o[2] // 240, 0:16]
        if o[0] == "EO":
            return T.EO[:, o[3], o[1]:o[2]] if len(o) == 4 else T.EO[:, :, o[1]:o[2]]
        rows = slice(0, 8) if o[-1] == "top" else slice(0, TOP[o[0]]) if o[0] in TOP else slice(None)
        o = o[:-1] if o[-1] == "top" else o
        if len(o) == 1:
            return T[o[0]][rows]
        if len(o) == 4:
            return T[o[0]][rows, o[1]:o[2]:o[3]]
        return T[o[0]][rows, o[1]:o[2]]

    def rg(o):
        if o[0] in ("sa", "sd"):
            return ("%s%d" % (o[0], o[1] % 5), o[1], o[2])
        return (o[0], 0, SCRATCH[o[0]][1][1]) if len(o) == 1 else (o[0], o[1], o[2])

    def op(e, rd, wr, fn, sem=None, **more):
        acc = [rg(o) + (False,) for o in rd if o] + [rg(o) + (True,) for o in wr]
        calls.append(dict(e=e, acc=acc, fn=fn, sem=sem, step=now[0], name=now[1], **more))

    def dma(e, rd, wr, out, in_, s):
        op(e, rd, wr, lambda q: q.dma_start(out, in_), s)

    def by(o, off):
        return ap(o).indirect(ap(off)) if off else ap(o)

    def vts(out, i, s1, o0, s2=None, o1=None, off=None):
        rd = [i, off] + [s for s in (s1, s2) if isinstance(s, tuple)]
        s1, s2 = [ap(s) if isinstance(s, tuple) else s for s in (s1, s2)]
        more = () if o1 is None else (o1,)
        op("v", rd, [out], lambda q: q.tensor_scalar(ap(out), by(i, off), s1, s2, o0, *more))

    def vtt(out, a, b, o, off=None, into=None):
        op("v", [a, b, off, into], [out], lambda q: q.tensor_tensor(by(out, into), by(a, off), ap(b), o))

    def vcp(out, i, off=None, into=None):
        op("v", [i, off, into], [out], lambda q: q.tensor_copy(by(out, into), by(i, off)))

    def scan(out, a, b, o0, o1, also=(), init=0.0):
        op("v", [a, b] + list(also), [out], lambda q: q.tensor_tensor_scan(ap(out), ap(a), ap(b), init, o0, o1))

    def fill(out, c):
        op("v", [], [out], lambda q: q.memset(ap(out), c))

    def act(out, i, f, off=None, **kw):
        cols = {k: v for k, v in kw.items() if isinstance(v, tuple)}
        kw.update({k: ap(v) for k, v in cols.items()})
        op("s", [i, off] + [v for k, v in cols.items() if k != "accum_out"],
           [out] + [v for k, v in cols.items() if k == "accum_out"],
           lambda q: q.activation(ap(out), by(i, off), f, **kw))

    def lin(out, i, scale=1.0, bias=0.0):
        if now[1] in ONV:
            vts(out, i, scale, A.mult, bias, A.add)
        else:
            act(out, i, AF.Copy, scale=scale, bias=bias)

    def mm(out, l, r, start, stop):
        op("t", [l, r], [out], lambda q: q.matmul(ap(out), ap(l), ap(r), start, stop))

    def mat(n, r):
        return (n, 128 * r, 128 * r + 128)

    def ahead(a, k):
        return T.cores[(T.rank_of(a) + k) % NR]

    def engines(a, k):
        return [e for e in topo.engines(a, ahead(a, k)) if k == 1 or e not in topo.engines(a, ahead(a, 1))]

    def send(src, *ways):
        def transfer(k, dst, s):
            rid, pid = topo.addr(ahead(core, k))[:2]
            return RemoteDMATransfer(dst_ids=[DstId(rid=rid, pnc=pid)], remote_sem=T.sem[s], src=ap(src), dst=ap(dst),
                                     dma_engine_mask=sum(1 << e for e in engines(core, k)))
        op("p", [src], [], lambda q: q.remote_dma_fused([transfer(k + 1, *w) for k, w in enumerate(ways)],
                                                        local_sem=T.sem["loc"]),
           ways[0][1], out=sum(len(engines(core, k + 1)) for k in range(len(ways))))
        for k, (dst, s) in enumerate(ways):
            op("ro"[k], [], [dst], None, s, n=len(engines(ahead(core, -k - 1), k + 1)), by=ways[0][1])

    def slot(b, n, lo=0, hi=NB):
        o = {"EF": NB, "EL": NB}.get(b, 256) * n
        return (b, o + lo, o + hi)

    def five(b, lo, hi, k):
        return (b, 5 * lo + k, 5 * hi, 5)

    T32, CAR = (NB, NB + 14), (NB + 14, NB + 28)

    dma("s", [], [("TLi", 0, 1)], T.TLi[0:8], T.tk0[:], "d_tk")
    dma("s", [], [("TLi", 1, 2)], T.TLi[8:16], T.ln0[:], "d_ln")
    dma("s", [], [slot("ZS", 0)], ap(slot("ZS", 0)), T.y0[:], "d_y")
    for i, (lo, hi) in enumerate(zip(LOAD, LOAD[1:])):
        dma("y", [], [("ilb", lo, hi)], T.ilb[:, lo:hi], T.il[:, lo:hi], "d_il%d" % i)
    for i in range(2):
        b = ("XT", 1792 * i, 1792 * i + 1792)
        dma("y", [], [b], ap(b), T.xw[:, 1792 * i:1792 * i + 1792], "d_x%d" % i)

    def asel(out, i, pat, cmp, base, cm):
        op("p", [i], [out], lambda q: q.affine_select(ap(out), ap(i), pat, cmp, 0.0, base, cm))

    def iota(out, pat, base, cm):
        kw = {} if SCRATCH[out[0]][2] == "int32" else {"allow_small_or_imprecise_dtypes": True}
        op("p", [], [out], lambda q: q.iota(ap(out), pat, base, cm, **kw))
    for o, c in ((("ONE",), 1.0), (mat("G8", 2), 1.0), (("RST",), 1.0), (("tc",), -1.0), (("B",), 0.0),
                 (("RST", 0, NB, 16), 0.0), (("tc", 0, 1, "top"), 2048.0)):
        fill(o, c)
    iota(("MODi",), [[0, 4], [1, 32]], -1792, 0)
    asel(("ID",), ("ONE",), [[-1, 128]], A.is_equal, 0, 1)
    for k in range(2):
        asel(mat("G8", k), mat("G8", 2), [[1, 8], [0, 16]], A.is_equal, 8 * k, -1)
    asel(("BO0",), ("ONE",), [[-16, 8], [0, 16]], A.is_ge, 0, 1)
    asel(("BO",), ("BO0",), [[16, 8], [0, 16]], A.is_ge, 15, -1)
    for k, base in enumerate((0, 16, -1, 15)):
        asel(mat("P4", k), ("BO",), [[-16, 8], [-2, 16]], A.is_equal, base, 1)
    send(slot("ZS", 0), (slot("YE", 0), "ay0"))
    iota(("iw",), [[16, 14]], 0, 1)
    iota(("ip",), [[0, 14]], 0, 1)
    iota(("trf",), [[1, NB]], NP, 0)
    for k in range(2):
        asel(mat("BC", k), ("ONE",), [[-16, 8], [0, 16]], A.is_equal, -7 - 8 * k, 1)
    for m, k in (("SKD", 7), ("SKA", 0)):
        asel((m, 16, 144), ("BO",), [[-16, 8], [-8, 16]], A.is_equal, -k, 1)
    iota(("BLK",), [[2048, 14], [0, 16]], 0, 0)
    iota(("THR",), [[32, 14]], 9, 0)
    for k in range(4):
        vcp(("pW", 128 * k, 128 * k + 128), ("MODi",))
    act(("NID32",), ("ID",), AF.Copy, scale=-32.0)
    act(("MOD",), ("pW",), AF.Copy, bias=1792.0)
    act(("NID",), ("ID",), AF.Copy, scale=-1.0)
    vtt(("h64",), ("ID", 0, 64), ("ID", 64, 128), A.add)
    fill(("MASK", 0, 896), 256.0)
    vtt(("h32",), ("h64", 0, 32), ("h64", 32, 64), A.add)
    fill(("MASK", 896, 1792), 256.0)
    vtt(("rm",), ("h32", 0, 16), ("h32", 16, 32), A.add)
    fill(("MASK", 0, 1792, 8), 0.0)
    vts(("TLh",), ("TLi",), ("tc",), A.subtract)
    more = [(("ONF",), ("ONE",), 1.0), (mat("G8", 1), mat("G8", 1), 4096.0), None,
            (("BO8",), ("BO",), 8192.0), (("BIG",), ("BO",), 2.0 ** 32)]
    for (lo, hi), x in zip(((0, 16), (16, 32), (32, 64), (64, 128), (128, 224)), more):
        act(("DG", lo, hi), ("rm",) if hi <= 32 else ("DG", 0, hi - lo), AF.Copy)
        if x:
            act(x[0], x[1], AF.Copy, scale=x[2])
    act(("NEG",), ("DG",), AF.Copy, scale=2.0 ** 23, bias=-2.0 ** 23)
    mm(("pE", 0, NB), ("ID",), ("NEG",), True, False)
    for k in range(2):
        mm(("pE", 0, NB), mat("G8", k), ("TLh",), False, k == 1)

    def table(i, b):
        lo, hi = LOAD[i:i + 2]
        mm((b, 0, hi - lo), ("ID",), ("f16t", lo, hi), True, False)
        mm((b, 0, hi - lo), ("NID",), ("MOD", 0, hi - lo), False, True)
        act(("LT", lo, hi), (b, 0, hi - lo), AF.Copy, bias=5904.5)
    between = [
        [lambda: fill(("qt",), 0.25), lambda: fill(slot("ZO", 0, *CAR), 129.0), lambda: fill(("zr",), 0.0)],
        [lambda: fill(("SKD", 0, 16), 0.0), lambda: scan(("PK",), ("RST",), ("pE", 0, NB), A.mult, A.max)],
        [lambda: vts(("q",), ("PK", 15, NB, 16), -2048.0, A.add), lambda: vts(("c2",), ("q",), 31, A.bitwise_and),
         lambda: vts(("t1",), ("q",), 7, A.arith_shift_right, 4064, A.bitwise_and),
         lambda: vts(("hi0",), ("q",), 4064, A.bitwise_and)],
        [lambda: vtt(("ao",), ("c2",), ("t1",), A.add), lambda: vcp(("AO", NL, NL + 14), ("ao",)),
         lambda: vcp(slot("ZO", 0, *T32), ("c2",))],
        [lambda: vts(("ipq",), ("ip",), 112, A.bitwise_and), lambda: vtt(("iw",), ("iw",), ("ipq",), A.subtract)],
        [lambda: fill(("SKA", 0, 16), 0.0), lambda: act(("WQ",), ("BO",), AF.Copy, scale=("wq1",)),
         lambda: act(("NTH",), ("DG",), AF.Copy, scale=("wq2",), bias=1.0)],
        [lambda: vts(five("sa", 0, NL, 1), ("iw", 0, NL), -16.0, A.mult)],
        [lambda: vts(five("sa", 14 + NL, 28, 1), ("iw", NL, 14), -16.0, A.mult),
         lambda: act(("THR",), ("THR",), AF.Copy, scale=8192.0)],
    ]
    weights = [lambda: None,
               lambda: scan(("th16",), ("qt",), ("zr",), A.mult, A.add, init=2.0 ** 33),
               lambda: vtt(("rq",), ("rm",), ("th16",), A.mult),
               lambda: op("v", [("rq",)], [("wq1",)],
                          lambda q: q.tensor_reduce(T.wq1[:], T.rq[:], AxisListType.X, A.add)),
               lambda: vts(("wq2",), ("wq1",), -1.0, A.mult, -1.0, A.add)]
    fills = [(five("sa", 0, 28, 3), M16), (five("sa", 0, 28, 0), 0.0), (five("sd", 0, 28, 0), 0.0),
             (five("sd", 0, 28, 1), 0.0), (five("sd", 0, 28, 2), 1.0), (five("sd", 0, 28, 3), -1.0),
             (five("sd", 0, 28, 4), 1.0), (five("sa", NL, NL + 14, 3), M32), (("A1",), 65.5),
             (("WT", NP, NP + NB), 0.0)]
    for i, (lo, hi) in enumerate(zip(LOAD, LOAD[1:])):
        vtt(("f16t", lo, hi), ("ilb", lo, hi), ("pW", 0, hi - lo), A.add)
        between[i][0]()
        if weights:
            weights.pop(0)()
        for o, c in fills[i::8]:
            fill(o, c)
        vts(("KF", lo, hi), ("f16t", lo, hi), 1.0 / 32, A.mult, 184.515625, A.add)
        pb = (("pA", "pB", "pZ")[i % 3], 0, hi - lo)
        mm(pb, ("ID",), ("f16t", lo, hi), True, False)
        mm(pb, ("NID32",), ("KF", lo, hi), False, True)
        act(("WT", lo, hi), pb, AF.Copy, bias=5920.0)
        for f in between[i][1:]:
            f()
    now[0] = 0
    tag("spares")
    vtt(("trm",), ("trf",), ("DG",), A.mult)

    SUM, NEW, ZB, LIST = ("pE", "pL"), ("pD", "pY"), ("pZ", "pY"), ("pA", "pB")

    def summed(n, p):
        lo, hi = ARR[p]
        z, b = slot("ZS", n, lo, hi), (SUM[p], lo, hi)
        tag("open", p)
        mm(b, ("ID",), ("NEG", lo, hi), True, False)
        mm(b, ("ONE",), ("BLK", lo, hi), False, False)
        tag("sum", p)
        vtt(("SG", lo, hi), z, ("pZ", lo, hi), A.is_ge)
        mm(b, ("BO",), z, False, False)
        tag("sum", p, "b")
        mm(b, ("BO8",), ("SG", lo, hi), False, True)
        tag("pick", p)
        scan(("PK", lo, hi), b, ("B", lo, hi), A.max, A.add)

    def places(n, p):
        lo, hi = ARR[p]
        pk, a = ("PK", lo + 15, hi, 16), (NL + lo // 16, NL + hi // 16)
        tag("skip", p)
        vtt(five("sa", *a, 0), pk, ("THR", lo // 16, hi // 16), A.is_ge)
        tag("floor", p)
        lin(five("sa", *a, 2), pk, bias=M32 - 16)
        tag("sums", p)
        lin(five("sa", *a, 4), pk, bias=-0.5)
        if n < ST:
            tag("half", p)
            lin(five("sa", *WORD[p], 2), pk, bias=M16 - 8)
            tag("sumw", p)
            lin(five("sa", *WORD[p], 4), pk, bias=-0.5)
            a = SLOT[p]
        tag("place", p)
        scan(("LB", 5 * a[0], 5 * a[1]), ("sd", 5 * a[0], 5 * a[1]), ("sa", 5 * a[0], 5 * a[1]), A.mult, A.add,
             also=[five(x, *a, k) for x in ("sa", "sd") for k in range(1, 5)])
        if n < ST:
            vcp(("AO",) + a, five("LB", *a, 4))
            tag("words", p)
            vcp(("XT",), slot("ZS", n, lo, hi), into=("AO",) + WORD[p])

    def renew(n, p):
        lo, hi = ARR[p]
        b, off = (NEW[p], lo, hi), ("OFF", lo // 16, hi // 16)
        if n == ST:
            tag("rewrite", p)
            return vtt(("WT",), ("DO", lo, hi), slot("ZS", n, lo, hi), A.add, into=off)
        tag("renew", p)
        mm(b, ("ID",), ("DO", lo, hi), True, False)
        tag("renew", p, "b")
        mm(b, ("ID",), slot("ZS", n, lo, hi), False, True)
        tag("renew", p)
        lin(("KD", lo, hi), b, 1.0 / 32, 191.515625)
        tag("whole", p)
        lin(("NW", lo, hi), b, bias=-64.0)
        tag("off", p)
        lin(("NK", lo, hi), ("KD", lo, hi), -32.0, 6208.0)
        tag("rewrite", p)
        vtt(("WT",), ("NW", lo, hi), ("NK", lo, hi), A.add, into=off)

    def carry(n):
        tag("carry" if n < ST else "final")
        vtt(slot("ZO", n, *T32), five("LB", NL, NL + 14, 4), five("LB", NL, NL + 14, 1), A.add)
        b = ("pA" if n < ST else "pW", 464, 478)
        mm(b, ("NID32",), slot("ZS", n, *CAR), True, False)
        mm(b, ("NID",), ("B", 15, NB, 16), False, False)
        mm(b, ("ID",), slot("ZO", n, *T32), False, True)
        lin(slot("ZO", n, *CAR), b, -1.0 / 32, -1.53125)

    def skips():
        tag("skips")
        mm(("pL", 480, 494), ("ONF",), five("sa", NL, NL + 14, 0), True, True)
        act(("Aj",), ("pL", 480, 494), AF.Copy, accum_out=("Ar",))
        tag("A")
        lin(("KA",), ("Ar",), 1.0 / 32, 191.515625)
        lin(("Au",), ("KA",), -32.0, 6209.5)
        act(("A1",), ("Au",), AF.Identity, bias=("Ar",))

    def fetch(p):
        (lo, hi), b = ARR[p], LIST[p]
        off = ("AO", NL + lo // 16, NL + hi // 16)
        tag("lines", p)
        if now[0] > 1:
            act(("LW", lo, hi), ("LT",), AF.Copy, off)
        else:
            tag("first", p)
            vts(("LW", lo, hi), ("ilb",), 4112.5, A.add, off=off)
        tag("fetch", p)
        act(("LW", NB + lo, NB + hi), ("WT", 0, NP), AF.Copy, off)
        w = (hi - lo) // 2
        for src in range(2):
            tag("fetch", p, "b" * src)
            for k in range(4):
                mm((b, w * (k // 2), w * (k // 2 + 1)), mat("P4", k), ("LW", NB * src + lo + k % 2, NB * src + hi, 2),
                   src == 0 and k == 0, src == 1 and k == 3)
        tag("lists", p)
        vts(("EO", lo // 2, hi // 2), (b, 0, hi - lo), -4128.0, A.add)

    def lowest(n):
        el = NB * n
        tag("rows")
        for k in range(2):
            mm(("pD", k, 224, 2), mat("BC", k), ("EL", el + 112, el + 224), True, True)
        vts(("DR",), ("pD", 0, 224), 1792.0, A.add)
        tag("wrapped")
        for t in range(8):
            mm(("pL", 32, 46), ("SKD", 16 - 2 * t, 144 - 2 * t), ("EL", el + 112 + t, el + 224, 8), t == 0, t == 7)
        act(("DW",), ("pL", 32, 46), AF.Copy, bias=1792.0)
        tag("both")
        for t in range(8):
            mm(("pL", 0, 28), ("SKA", 16 - 2 * t, 144 - 2 * t), ("EL", el + t, el + 224, 8), t == 0, t == 7)
        act(("LL",), ("pL", 0, 28), AF.Copy, bias=5904.5)
        tag("next")
        lin(five("sa", NL, NL + 14, 1), ("LL", 0, 14), -1.0, 4128.0)
        vtt(five("sd", NL, NL + 14, 1), ("LL", 0, 14), ("LL", 14, 28), A.subtract)
        tag("d")
        vcp(("DWu", 0, 14), ("DW",))
        tag("old")
        act(("DO",), ("WT", 0, NP), AF.Copy, ("DWu", 0, 14), bias=0.0 if n + 1 < ST else -128.0)
        tag("alone")
        for h in HALF:
            mm(h, ("ID",), ("NTH",) + h[1:], True, False)
        for p, (b, lo, hi) in enumerate(HALF):
            for c in range(lo // 16, hi // 16):
                tag("alike", c // 2)
                e = ("EQ", 240 * c, 240 * c + hi - 16 * c)
                vts(e, ("DR", 16 * c, hi), ("DW", c, c + 1), A.is_equal, 0.5, A.mult)
                if 16 * c + 16 < hi:
                    mm((b, 16 * c + 16, hi), ("BIG",), (e[0], e[1] + 16, e[2]), False, False)
            tag("lost", p)
            mm(HALF[p], ("WQ",), ("EQ", 15 * lo, 15 * hi, 1), False, True)
            act(("LF", lo, hi), HALF[p], AF.Sign)
            scan(("SC", lo, hi), ("trm", lo, hi), ("LF", lo, hi), A.max, A.mult)
            tag("target", p)
            vtt(("o2", lo // 16, hi // 16), ("SC", lo + 15, hi, 16), ("DW", lo // 16, hi // 16), A.max)
            vcp(("OFF", lo // 16, hi // 16), ("o2", lo // 16, hi // 16))

    def results(n):
        for p in range(2):
            fetch(p)
        if n:
            carry(n)
            skips()
        if n < 2:
            tag("table")
            for k, b in enumerate(("pD", "pL", "pW", "pE")):
                table(4 * n + k, b)
        tag("less")
        for p in range(2):
            mm((ZB[p],) + ARR[p], ("NID",), slot("ZS", n, *ARR[p]), True, False)
        tag("send")
        vts(slot("EF", n), ("EO", 0, 112), -1792.0, A.add)
        send(slot("EF", n), (slot("EL", n), "ae%d" % n))
        for i, (a, b) in enumerate(CH):
            u, p = (16 * a, 16 * b), int(2 * a < LATE)
            tag("even", i)
            if i:
                act(("VE",) + u, ("XT",), AF.Copy, ("EO", a, b, 0))
            else:
                vcp(("VE",) + u, ("XT",), off=("EO", a, b, 0))
            tag("least", i)
            vtt(("U",) + u, ("XT",), ("VE",) + u, A.min, off=("EO", a, b, 1))
            tag("most", i)
            scan(("M",) + u, ("MASK",) + u, ("U",) + u, A.min, A.max)
            mm((ZB[p], 2 * a, 2 * b), ("ID",), ("M", 16 * a + 7, 16 * b, 8), False, 2 * a == ARR[p][0])
            if 2 * a == ARR[p][0]:
                lo, hi = MSG[p]
                act(slot("ZO", n, *ARR[p]), (ZB[p],) + ARR[p], AF.Abs)
                ways = [(slot(x, n + 1, lo, hi), "a%s%d" % (s[p], m)) for x, s, m in (("ZS", "zb", n), ("YE", "yx", n + 1))]
                send(slot("ZO", n, lo, hi), *ways[:1 + (n + 1 < ST)])

    def arrival(n):
        tag("y")
        mm(("pZ", 0, NB), ("ID",), slot("YE", n - 1), True, True)
        lowest(n - 1)
        tag("B")
        act(("B", 15, NB, 16), slot("ZS", n, *T32), AF.Identity, bias=("A1",))
        for p in range(2):
            summed(n, p)
            renew(n, p)
            places(n, p)

    for n in range(ST):
        now[0] = n
        results(n)
        arrival(n + 1)

    dma("y", [slot("ZS", ST)], [], T.yy[:], ap(slot("ZS", ST)), "d_o0")
    carry(ST)
    tag("mod")
    act(("pA",), ("MOD",), AF.Copy, bias=-6128.5)
    for i, b in enumerate(("pY", "pZ", "pD", "pB", "pE", "pL", "pY")):
        lo, hi, b = 512 * i, 512 * i + 512, (b,)
        tag("less", i)
        mm(b, ("NID",), ("MOD",), True, False)
        tag("turn", i)
        mm(b, ("ID",), ("WT", lo, hi), False, False)
        vtt(("KF", lo, hi), ("WT", lo, hi), ("pA",), A.subtract)
        tag("turn", i, "b")
        mm(b, ("NID",), ("KF", lo, hi), False, True)
        if i in BYV:
            vts(("YW", lo, hi), b, 6144.0, A.add)
        else:
            act(("YW", lo, hi), b, AF.Copy, bias=6144.0)
        dma("y", [("YW", lo, hi)], [], T.yw[:, lo:hi], T.YW[:, lo:hi], "d_o%d" % (1 + i))
    tag("clock")
    vts(("fo", 14, 28), five("LB", NL, NL + 14, 1), -1.0, A.mult)
    vtt(("t1",), ("hi0",), slot("ZO", ST, *T32), A.add)
    vts(("t2",), slot("ZO", ST, *CAR), 32.0, A.mult, -4128.0, A.add)
    vtt(("t3",), ("t1",), ("t2",), A.add)
    vts(("q",), ("t3",), 4095, A.bitwise_and)
    vts(("fo", 0, 14), ("q",), -2048.0, A.add)
    for r in range(16):
        mm(("pW", r, 448, 16, "top"), ("ID", r, 128, 16), ("fo",), True, True)
    act(("fr", 0, 224), ("pW", 0, 224, "top"), AF.Copy, bias=2048.0)
    act(("fr", 224, 448), ("pW", 224, 448, "top"), AF.Copy, scale=1.0 / 32)
    dma("s", [("fr", 0, 224)], [], T.yt[:], ap(("fr", 0, 224)), "d_t")
    dma("s", [("fr", 224, 448)], [], T.yl[:], ap(("fr", 224, 448)), "d_l")

    issue(g, T, arrange(calls))


def needs(calls):
    before, seen, sent = [set() for _ in calls], {}, {}
    for i, c in enumerate(calls):
        for (name, lo, hi, w) in c["acc"]:
            h = seen.setdefault(name, [])
            before[i].update(j for (a, b, w2, j) in h
                             if j != i and (bank(name) or (a < hi and lo < b and (w or w2))))
            if bank(name):
                h[:] = []
            elif w:
                h[:] = [x for x in h if not (lo <= x[0] and x[1] <= hi)]
            h.append((lo, hi, w, i))
        if "by" in c:
            before[i].add(sent[c["by"]])
        sent.setdefault(c["sem"], i)
    return before


def named(calls):
    count, out = {}, []
    for c in calls:
        k = (c["step"], c["e"], c["name"])
        count[k] = count.get(k, -1) + 1
        one = c["e"] not in "vs" or c["step"] < 0 or not count[k]
        out.append(c["name"] + ("" if one else "abcdefgh"[count[k]]))
    return out


def arrange(calls):
    step, last = [{e: x[e].split() for e in x} for x in (STEP, LAST)]
    queues = {}
    for i, (c, name) in enumerate(zip(calls, named(calls))):
        e, n = "p" if "by" in c else c["e"], c["step"]
        if n < 0 or e == "y":
            key = (n, 0, i)
        else:
            if n < ST - 1 and name + "+" in step[e]:
                name, n = name + "+", n + 1
            key = (n, (last if n == ST - 1 else step)[e].index(name), i)
        queues.setdefault(c["e"], []).append((key, i))
    queues = [[i for _, i in sorted(q)][::-1] for q in queues.values()]
    before, done, out = needs(calls), set(), []
    while len(out) < len(calls):
        moved = len(out)
        for q in queues:
            while q and before[q[-1]] <= done:
                done.add(q[-1])
                out.append(calls[q.pop()])
        assert len(out) > moved
    return out


def issue(g, T, calls):
    queues = {"v": g.vector, "t": g.tensor, "s": g.scalar, "p": g, "y": g.sync}
    semof = {"v": "cv", "t": "ct", "s": "cs", "p": "cp"}
    count = {s: 0 for s in SEMAPHORES}
    known = {e: {} for e in queues}
    snaps = {}
    hist = {}

    def conflicts(e, name, lo, hi, write):
        out = []
        for (a, b, e2, s2, v2, w2, asy) in hist.get(name, []):
            if bank(name) and e2 != e:
                out.append((s2, v2))
            elif b <= lo or hi <= a or not (write or w2) or (bank(name) and e == "t"):
                continue
            elif e2 != e or asy or w2 or bank(name):
                out.append((s2, v2))
        return out

    def waits(e, acc):
        need = {}
        for (name, lo, hi, w) in acc:
            for s, v in conflicts(e, name, lo, hi, w):
                need[s] = max(need.get(s, 0), v)
        own = semof.get(e)
        for s in sorted(need, key=lambda s: (s == own, s)):
            v = need[s]
            if known[e].get(s, 0) >= v:
                continue
            queues[e].wait_ge(T.sem[s], v)
            for s2, v2 in snaps[(s, v)].items():
                known[e][s2] = max(known[e].get(s2, 0), v2)

    def note(e, acc, s, v, asy):
        sn = dict(known[e]) if e in known else {}
        sn[s] = v
        snaps[(s, v)] = sn
        for (name, lo, hi, w) in acc:
            h = hist.setdefault(name, [])
            if w:
                h[:] = [x for x in h if not (lo <= x[0] and x[1] <= hi)]
            else:
                h[:] = [x for x in h if not (x[2] == e and not x[5] and not asy and lo <= x[0] and x[1] <= hi)]
            h.append((lo, hi, e, s, v, w, asy))

    for c in calls:
        e, acc, s = c["e"], c["acc"], c["sem"]
        if "by" in c:
            count[s] = c["n"]
            note(e, acc, s, c["n"], True)
            continue
        waits(e, acc)
        ins = c["fn"](queues[e])
        if "out" in c:
            count["loc"] += c["out"]
            continue
        k = 16 if s else 1
        s = s or semof[e]
        count[s] += k
        ins.then_inc(T.sem[s], k)
        note(e, acc, s, count[s], k > 1)
    for s in SEMAPHORES:
        if count[s] and known["p"].get(s, 0) < count[s]:
            g.wait_ge(T.sem[s], count[s])
